import numpy as np, ml_dtypes
CORES = [48,51,52,55]
N = 4
BF = ml_dtypes.bfloat16
def gentries(a):
    return np.ascontiguousarray(a.reshape(8, 16, -1).transpose(0, 2, 1)).reshape(8, -1)
def gtable(e):
    e = np.asarray(e); return np.ascontiguousarray(e.reshape(8, -1, 16).transpose(0, 2, 1)).reshape(128, -1).astype(np.int32)
V, T, J, CAP, RO, M, LN = 1024, 1024, 4, 64, 3, 4, 2
E = N * CAP * J; A = V + RO * E; F = 2 * J + 2
def codes(rng, back):
    u = rng.random((N, 8, 16, T))
    c = np.where(u < 0.15, 0, np.where(u < 0.5, rng.integers(1, J + 1, u.shape), J + back))
    c[:, :, F:] = 0; c[:, :, F] = rng.integers(1, J + 1, (N, 8, T))
    return c
def parts(rng):
    x = rng.integers(0, 16, (N, 8, 16, V)); kd = np.where(rng.random((N, 8, 2, V)) < 0.25, A, rng.integers(0, V, (N, 8, 2, V)))
    wt = rng.integers(0, 256, (N, 8, 16)); wt[..., 0] |= 1
    th = rng.integers(40, 81, (N, 8))
    for q in range(N):
        o = rng.permutation(8); th[q, o[0]] = 42; th[q, o[1]] = 80
    rx = rng.integers(0, 16, (N, 8, 16, T)); nx = rng.integers(0, 16, (N, 8, 16, J, T)); tk = codes(rng, rng.integers(1, V + 1, (N, 8, 16, T)))
    return x, kd, wt, th, rx, nx, tk
def small(a, n):
    return np.ascontiguousarray(a.reshape(N, 128, n)).astype(np.float32).astype(BF)
def pack(x, kd, wt, th, rx, nx, tk):
    return {"x0": small(x, V), "k0": np.stack([gtable(a) for a in kd[:, :, 0]]), "k1": np.stack([gtable(a) for a in kd[:, :, 1]]),
            "wt": wt.reshape(N, 128, 1).astype(np.int32), "th": np.repeat(th, 16, axis=1).reshape(N, 128, 1).astype(np.int32),
            "rx": small(rx, T), "nx": small(nx, J * T), "tk": np.ascontiguousarray(tk.reshape(N, 128, T)).astype(np.int32)}
def setup_inputs(rng):
    return pack(*parts(rng))
def setup_inputs_alike(rng):
    x, kd, wt, th, rx, nx, tk = parts(rng); v = np.arange(V)
    wt[:, ::2] = 0; th[:, ::2] = 70; th[:, ::4] = 241; th[:, 5] = 241
    kd[:, 1] = v; kd[:, 2, 0] = 0; kd[:, 2, 1] = V - 1; kd[:, 3] = np.where(v < V - 1, v + 1, A)
    x[:, 5] = np.tile(x[:, 5, :, :4], (1, 1, V // 4))
    tk[:, 4, :F] = 0; tk[:, 5, :F] = 1; tk[:, 6, :F] = rng.choice(np.array([J + 1, J + V]), (N, F, T)); tk[:, 7, :F] = rng.integers(1, J + 1, (N, F, T))
    tk[:, 0, F] = 1; tk[:, 1, F] = J
    return pack(x, kd, wt, th, rx, nx, tk)
def setup_inputs_edge(rng):
    x, kd, wt, th, rx, nx, tk = parts(rng)
    rho = rng.integers(2, 6, (8, 16)); th = rng.integers(8, 21, (N, 8))
    rx = np.broadcast_to(rho[None, :, :, None], (N, 8, 16, T)).copy(); rx[:, :, 0] += (rng.random((N, 8, T)) < 0.7).astype(np.int64)
    want = th[:, :, None] - 1 + rng.choice(np.array([-1, 0, 0, 1]), (N, 8, E))
    e = np.argsort(rng.random((N, 8, E, 30)), axis=-1) < want[..., None]
    e = np.add.reduce(e.reshape(N, 8, E, 15, 2).astype(np.int64), axis=-1)
    y = np.broadcast_to(rho[None, :, None, :], (N, 8, E, 16)).copy(); y[..., 1:] += e * rng.choice(np.array([-1, 1]), e.shape)
    x[..., V - E:] = 2 * y.transpose(0, 1, 3, 2) + rng.integers(0, 2, (N, 8, 16, E)); kd[..., V - E:] = A
    nx = rho[None, :, :, None, None] + rng.integers(-1, 2, (N, 8, 16, J, T))
    far = [int(g) for g in rng.permutation(8)[:3]]
    for g in far: kd[:, g, :, V - E:] = np.arange(V - E, V)
    for i in (0, 1):
        g = far[i]; lv = rng.integers(10, 15, N)
        if i == 0: lv[:] = 14
        x[:, g, :, V - E:] = lv[:, None, None] + rng.integers(-1, 2, (N, 16, E)); rx[:, g] = rng.integers(0, 4, (N, 16, T))
        th[:, g] = 16 * lv - 24 + rng.choice(np.array([-5, -3, -1, 1, 3, 5]), N)
    g = far[2]; few = rng.random((N, 1, E)) < 0.5
    x[:, g, :, V - E:] = np.where(few & (rng.random((N, 16, E)) < 0.2), 14, 15); x[:, g, :, V - E] = 15; rx[:, g] = 0
    th[:, g] = np.where(rng.permutation(N) % 2 == 0, 241, 240)
    wt[:, far[0]] = rng.integers(240, 256, (N, 16)); wt[:, far[2]] = rng.integers(240, 256, (N, 16))
    return pack(x, kd, wt, th, rx, nx, tk)
def setup_inputs_quiet(rng):
    x, kd, wt, th, rx, nx, tk = parts(rng)
    q = rng.permutation(N); th[q[1]] = 241; th[:, rng.integers(0, 8)] = 0; th[q[0]] = 0
    return pack(x, kd, wt, th, rx, nx, tk)
def setup_inputs_room(rng):
    x, kd, wt, th, rx, nx, tk = parts(rng)
    wt[:] = 0; wt[..., 0] = 1; wt[..., 1] = 8; wt[..., 2] = 64
    rx[:, :, 3:] = 0; th[:] = 50; kd[..., V - E:] = A
    for q in range(N):
        for g in range(8):
            n = rng.choice(np.array([0, 1, CAP - 1, CAP, CAP + 1, 2 * CAP]), N)
            if q == 0: n[1] = (CAP, CAP + 1, 0, CAP - 1, 1, 2 * CAP, CAP, CAP + 1)[g]
            own = np.concatenate([np.repeat(np.arange(N), n), np.full(E - int(np.sum(n)), -1)])
            own = rng.permutation(own)
            y = rng.integers(0, 8, (16, E)); y[3:] = np.where(own >= 0, 0, rng.integers(4, 8, (13, E)))
            y[0] = np.where(own >= 0, own + N * rng.integers(0, 8 // N, E), y[0])
            x[q, g, :, V - E:] = 2 * y + rng.integers(0, 2, (16, E))
    return pack(x, kd, wt, th, rx, nx, tk)
def setup_inputs_spread(rng):
    x, kd, wt, th, rx, nx, tk = parts(rng)
    x = np.floor(np.exp2(4 * rng.random((N, 8, 1, V))) * rng.random(x.shape)).astype(np.int64)
    rx = np.floor(np.exp2(4 * rng.random((N, 8, 1, T))) * rng.random(rx.shape)).astype(np.int64)
    nx = np.floor(np.exp2(4 * rng.random((N, 8, 1, J, T))) * rng.random(nx.shape)).astype(np.int64)
    wt = np.floor(np.exp2(8 * rng.random(wt.shape)) * rng.random(wt.shape)).astype(np.int64); wt[..., 0] |= 1
    th = np.where(rng.random((N, 8)) < 0.25, rng.integers(0, 242, (N, 8)), rng.integers(20, 80, (N, 8)))
    kd = np.where(rng.random(kd.shape) < 0.2, A, np.floor(V * rng.random(kd.shape) ** 3).astype(np.int64))
    tk = codes(rng, 1 + np.floor(V * rng.random((N, 8, 16, T)) ** 3).astype(np.int64))
    return pack(x, kd, wt, th, rx, nx, tk)
def check_inputs(d):
    bad = []
    for k in ("x0", "rx", "nx"):
        a = d[k].astype(np.float32)
        if not np.all((a >= 0) & (a <= 15) & (a == np.floor(a))): bad.append("range of " + k)
    for k in ("k0", "k1"):
        a = d[k]
        if not np.all(((a >= 0) & (a < V)) | (a == A)): bad.append("range of " + k)
    if np.min(d["wt"]) < 0 or np.max(d["wt"]) > 255: bad.append("range of wt")
    if np.min(d["th"]) < 0 or np.max(d["th"]) > 241: bad.append("range of th")
    a = d["th"].reshape(-1, 8, 16)
    if not np.all(a == a[:, :, :1]): bad.append("th alike in a group")
    a = d["tk"].reshape(-1, 8, 16, T)
    if np.min(a[:, :, :F]) < 0 or np.max(a[:, :, :F]) > J + V: bad.append("kid codes of tk")
    if np.min(a[:, :, F]) < 1 or np.max(a[:, :, F]) > J: bad.append("feet of tk")
    if np.any(a[:, :, F + 1:] != 0): bad.append("unused rows of tk")
    return bad
def pick(a, ix):
    return np.take_along_axis(a, ix[:, None, :], 2)
def sweep(x, kd, S):
    a, b = kd[:, 0, :S], kd[:, 1, :S]
    m = np.maximum(pick(x, a), pick(x, b))
    for u in (a, b):
        for i in range(2):
            m = np.maximum(m, pick(x, pick(kd[:, i:i + 1], u)[:, 0]) - 2)
    x[:, :, :S] = (x[:, :, :S] + m) >> 1
def whole_of(a):
    return a.astype(np.float32).astype(np.int64)
def reference(x0, k0, k1, wt, th, rx, nx, tk):
    X = np.zeros((N, 8, 16, A + 1), np.int64); X[..., :V] = whole_of(x0).reshape(N, 8, 16, V)
    K = np.full((N, 8, 2, A + 1), A, np.int64)
    for q in range(N):
        K[q, :, 0, :V] = gentries(k0[q]); K[q, :, 1, :V] = gentries(k1[q])
    ws = wt.astype(np.int64).reshape(N, 8, 16, 1); lim = th.astype(np.int64).reshape(N, 8, 16)[:, :, :1]
    rt = whole_of(rx).reshape(N, 8, 16, T); nd = whole_of(nx).reshape(N, 8, 16, J, T); rec = tk.astype(np.int64).reshape(N, 8, 16, T)
    roots = np.ascontiguousarray(rt.transpose(1, 2, 3, 0)).reshape(8, 16, T * N)
    live = np.ones((N, 8, E), bool)
    for t in range(RO):
        S = V + E * t; fresh = np.zeros((N, 8, E), bool)
        for q in range(N):
            sweep(X[q], K[q], S)
            x = X[q][:, :, S - E:S].copy(); h = np.add.reduce(ws[q] * x, axis=1)
            took = np.full((8, E), -1, np.int64)
            for m in range(M):
                c = (h + 97 * m + 31 * t) & (T * N - 1)
                dist = np.add.reduce(np.abs(x - pick(roots, c)), axis=1)
                took = np.where((took < 0) & live[q] & (dist < lim[q]), c, took)
            for g in range(8):
                xg, kg = X[q, g], K[q, g]
                for o in range(N):
                    i = np.flatnonzero((took[g] >= 0) & ((took[g] & (N - 1)) == o))[:CAP]
                    if len(i) == 0: continue
                    s = took[g, i] >> LN; v = S - E + i; k = CAP * o + np.arange(len(i)); b = S + J * k
                    oldx = xg[:, v].copy(); oldk = kg[:, v].copy(); cd = rec[o, g][:, s]
                    back = v - (cd - J); back = np.where(back < 0, back + S, back)
                    new = np.where(cd == 0, A, np.where(cd <= J, b + cd - 1, back))
                    for j in range(1, J + 1):
                        foot = cd[F] == j
                        xg[:, b + j - 1] = np.where(foot, oldx, nd[o, g, :, j - 1][:, s])
                        kg[:, b + j - 1] = np.where(foot, oldk, new[2 * j:2 * j + 2])
                        fresh[q, g, J * k + j - 1] = True
                    kg[:, v] = new[0:2]
                    xg[:, v] = (oldx + rt[o, g][:, s]) >> 1
        live = fresh
    for q in range(N): sweep(X[q], K[q], A)
    return {"y": np.ascontiguousarray(X[..., :A]).reshape(N, 128, A).astype(np.float32).astype(BF)}

@@ -1,0 +1,705 @@
+from concourse.bass import DstId, RemoteDMATransfer
+from concourse.mybir import AluOpType as ALU, ActivationFunctionType as ACT
+
+N = 4
+V = 1024
+RCW = 4096 + 368
+XN0 = RCW + 16
+NXB = XN0 + V
+CEN = 2064.0
+BIG = 16384.0
+FAR = 131072.0
+MAGIC = 12582912.0
+RELU_CHUNKS = (1, 2, 2)
+LAST_V = (1, 3, 5, 7)
+OLDK_ON = ("s", "v", "v")
+EARLY = 2
+PIECES = ((0, 256), (256, 512), (768, 256))
+RELAY = (("tkf", [0], "t"), ("bt", [NXB, NXB + 4096], "n"), ("bt", [NXB + 8192, NXB + 12288], "m"))
+
+MATS = {"I": 128, "I2": 128, "I65": 128, "IB": 128, "I63": 128, "NI": 128, "NB": 128, "BLK": 128, "UP": 128, "UN": 128,
+        "LW": 128, "LB": 128, "LF": 128, "ZW": 144, "ZN": 144}
+ZMATS = {"Z": 144, "D11": 128, "ZK0": 144, "ZK1": 144, "PF": 144, "PO": 144, "PV": 144, "PK0": 144, "PK1": 144,
+         "D12": 128, "LO": 128}
+MOFF = {}
+for _d in (MATS, ZMATS):
+    _o = 0
+    for _k in _d:
+        MOFF[_k] = _o
+        _o += _d[_k]
+ZW_ = sum(ZMATS.values())
+
+SCRATCH = {"bt": ("sbuf", [128, NXB + 16384], "bfloat16"), "cm": ("sbuf", [128, sum(MATS.values())], "bfloat16"),
+           "cz": ("sbuf", [128, ZW_], "bfloat16")}
+for _t, _l in (("bfloat16", (("rl", 4096), ("xin", V), ("ar", 4112), ("qq", 4112), ("ta", 4096), ("tb", 4096), ("dd", 4096),
+                             ("da", 4096), ("yo", 4096), ("sel", V), ("ones", V), ("uu", 2064), ("zt", 128), ("wb", 8),
+                             ("thl", 64), ("ask", 256), ("keep", V), ("cs", 256), ("ic", 512), ("il", 256), ("rs", 256),
+                             ("sg", V), ("sn", V), ("c2", 256))),
+               ("float32", (("tkf", 4096), ("tkv", 1040), ("rec", 512), ("dw", 1296), ("ktm", 256), ("col", 32), ("val", 256),
+                            ("sc", 512), ("ra", 512), ("vc", 128), ("de", 1536), ("fl", 512))),
+               ("float16", (("vi", V), ("dv", V), ("k16", 128), ("r16", 256), ("kb", 256), ("d16", 256), ("ra16", 320))),
+               ("int32", (("tki", V), ("kin", 128), ("wti", 8), ("thi", 8), ("pi", 8), ("c1", 128), ("bi", 320))),
+               ("uint16", (("kl0", 256), ("kl1", 256), ("offl", 256), ("ls", 288)))):
+    for _k, _n in _l:
+        SCRATCH[_k] = ("sbuf", [128, _n], _t)
+for _b in range(8):
+    SCRATCH["ps%d" % _b] = ("psum", [128, 512], "float32")
+
+SEMAPHORES = (["cv", "cs", "cp", "cg", "ar_r", "ar_t", "ar_n", "ar_m", "sn_r", "sn_t", "sn_n", "sn_m"]
+              + ["dm%d" % i for i in range(24)])
+
+
+def rank_program(g, core, T, topo):
+    rank = T.rank_of(core)
+    ranks = list(T.cores)
+    spare = [c for c in topo.cores_of(ranks[0]) if c not in ranks]
+    helper = {}
+    for c in ranks:
+        helper[c] = [h for h in spare if topo.die(h) != topo.die(c) and h not in helper.values()][0]
+
+    def common(src, dsts):
+        return [e for e in topo.engines(src, dsts[0]) if all(e in topo.engines(src, d) for d in dsts)]
+
+    def send(src, dsts, name, starts, tag):
+        eng = common(src, dsts)
+        per = len(eng) // len(starts)
+        ids = [DstId(rid=topo.addr(c)[0], pnc=topo.addr(c)[1]) for c in dsts]
+        trs = []
+        for i, s0 in enumerate(starts):
+            a = T[name][:, s0:s0 + V]
+            trs.append(RemoteDMATransfer(dst_ids=ids, dma_engine_mask=sum(1 << e for e in eng[i * per:(i + 1) * per]),
+                                         remote_sem=T.sem["ar_" + tag], src=a, dsts=[a] * len(ids)))
+        g.remote_dma_fused(trs, local_sem=T.sem["sn_" + tag])
+        return per * len(starts)
+
+    def count(src, dsts, k):
+        return len(common(src, dsts)) // k * k
+
+    def near_of(c):
+        return [d for d in ranks if d != c and topo.die(d) == topo.die(c)]
+
+    def far_of(c):
+        return [d for d in ranks if topo.die(d) != topo.die(c)]
+
+    if rank is None:
+        for c in ranks:
+            if helper[c] == core:
+                o = T.rank_of(c)
+                done = {}
+                for (name, starts, tag) in RELAY:
+                    g.wait_ge(T.sem["ar_" + tag], count(c, near_of(c) + [core], len(starts)))
+                    done[tag] = send(core, far_of(c), name, [s0 + V * o for s0 in starts], tag)
+                for tag in done:
+                    g.wait_ge(T.sem["sn_" + tag], done[tag])
+        return
+    Q = {"v": g.vector, "s": g.scalar, "p": g.tensor, "g": g, "y": g.sync}
+    cnt = {"v": 0, "s": 0, "p": 0, "g": 0}
+    seen = {e: {} for e in Q}
+    hist = {}
+    ndm = [0]
+    final = {}
+    group = []
+
+    def R(name, lo, hi, st=1):
+        ap = T[name][:, lo:hi] if st == 1 else T[name][:, lo:hi:st]
+        return (ap, [(name, lo, hi)])
+
+    def W(name, lo, n):
+        return R(name, lo, lo + n)
+
+    def G(name, lo, hi, oname, olo, n):
+        return (T[name][:, lo:hi].indirect(T[oname][:, olo:olo + n]), [(name, lo, hi), (oname, olo, olo + n)])
+
+    def M(k, lo=0, n=128, st=1):
+        return R("cm" if k in MATS else "cz", MOFF[k] + lo, MOFF[k] + lo + n, st)
+
+    def C(i):
+        return R("col", i, i + 1)
+
+    def wait(e, sem, val):
+        if seen[e].get(sem, 0) < val:
+            Q[e].wait_ge(T.sem[sem], val)
+            seen[e][sem] = val
+
+    def before(e, rd, wr):
+        need = {}
+        for w, regs in ((False, rd), (True, wr)):
+            for (n, lo, hi) in regs:
+                whole = n.startswith("ps")
+                for (l2, h2, w2, e2, sem, val) in hist.get(n, []):
+                    if (whole and e2 != e) or (l2 < hi and lo < h2 and (w or w2)):
+                        need[sem] = max(need.get(sem, 0), val)
+        for sem in need:
+            wait(e, sem, need[sem])
+
+    def note(e, rd, wr, sem, val):
+        for w, regs in ((False, rd), (True, wr)):
+            for (n, lo, hi) in regs:
+                h = hist.setdefault(n, [])
+                if w:
+                    h[:] = [x for x in h if not (lo <= x[0] and x[1] <= hi)]
+                h.append((lo, hi, w, e, sem, val))
+        final[sem] = max(final.get(sem, 0), val)
+
+    def split(out, ins):
+        rd = []
+        for a in ins:
+            if isinstance(a, tuple):
+                rd += a[1]
+        return rd + out[1][1:], out[1][:1]
+
+    def A(a):
+        return a[0] if isinstance(a, tuple) else a
+
+    def run(e, out, ins, fn):
+        rd, wr = split(out, ins)
+        before(e, rd, wr)
+        cnt[e] += 1
+        fn().then_inc(T.sem["c" + e], 1)
+        note(e, rd, wr, "c" + e, cnt[e])
+
+    def ts(out, a, s1, op0, s2=None, op1=None):
+        if op1 is None:
+            run("v", out, [a, s1], lambda: g.vector.tensor_scalar(A(out), A(a), A(s1), None, op0))
+        else:
+            run("v", out, [a, s1, s2], lambda: g.vector.tensor_scalar(A(out), A(a), A(s1), A(s2), op0, op1))
+
+    def tt(out, a, b, op):
+        run("v", out, [a, b], lambda: g.vector.tensor_tensor(A(out), A(a), A(b), op))
+
+    def cp(out, a):
+        run("v", out, [a], lambda: g.vector.tensor_copy(A(out), A(a)))
+
+    def ms(out, c):
+        run("v", out, [], lambda: g.vector.memset(A(out), c))
+
+    def scan(out, a, b, init, op0, op1):
+        run("v", out, [a, b], lambda: g.vector.tensor_tensor_scan(A(out), A(a), A(b), init, op0, op1))
+
+    def act(out, a, func=ACT.Identity, bias=0.0, scale=1.0):
+        run("s", out, [a, bias, scale], lambda: g.scalar.activation(A(out), A(a), func, bias=A(bias), scale=A(scale)))
+
+    def asel(out, a, pat, op, fill, base, cm=1):
+        run("g", out, [a], lambda: g.affine_select(A(out), A(a), pat, op, fill, base, cm))
+
+    def put(a, pat, val, base):
+        asel(a, a, pat, ALU.not_equal, val, base)
+
+    def iota(out, pat, base):
+        run("g", out, [], lambda: g.iota(A(out), pat, base, 0, allow_small_or_imprecise_dtypes=True))
+
+    def mm(out, lt, rhs, start, stop):
+        rd, wr = split(out, [lt, rhs])
+        before("p", rd, wr)
+        i = g.tensor.matmul(A(out), A(lt), A(rhs), start, stop)
+        group.append((rd, wr))
+        if stop:
+            cnt["p"] += 1
+            i.then_inc(T.sem.cp, 1)
+            for (r_, w_) in group:
+                note("p", r_, w_, "cp", cnt["p"])
+            del group[:]
+
+    def mms(out, pairs):
+        for i, (lt, rhs) in enumerate(pairs):
+            mm(out, lt, rhs, i == 0, i == len(pairs) - 1)
+
+    def dma(e, out, in_):
+        rd = in_[1] if isinstance(in_, tuple) else []
+        wr = out[1] if isinstance(out, tuple) else []
+        before(e, rd, wr)
+        sem = "dm%d" % ndm[0]
+        ndm[0] += 1
+        Q[e].dma_start(A(out), A(in_)).then_inc(T.sem[sem], 16)
+        note("dma", rd, wr, sem, 16)
+
+    def share(name, starts, tag):
+        own = [s0 + V * rank for s0 in starts]
+        before("g", [(name, s0, s0 + V) for s0 in own], [])
+        if tag == "r":
+            final["sn_r"] = send(core, [c for c in ranks if c != core], name, own, tag)
+            got = sum(count(c, [d for d in ranks if d != c], 1) for c in ranks if c != core)
+        else:
+            final["sn_" + tag] = send(core, near_of(core) + [helper[core]], name, own, tag)
+            got = (sum(count(c, near_of(c) + [helper[c]], len(starts)) for c in near_of(core))
+                   + sum(count(helper[c], far_of(c), len(starts)) for c in far_of(core)))
+        note("rem", [], [(name, s0 + V * o, s0 + V * o + V) for s0 in starts for o in range(N) if o != rank], "ar_" + tag, got)
+
+    rot = [0]
+
+    def bank(n=512):
+        rot[0] = (rot[0] + 1) % 3
+        return W("ps%d" % rot[0], 0, n)
+
+    def weave(o, e):
+        out, src = R("bt", o, 4096, 4), W("rl", V * o, V)
+        if e == "g":
+            asel(out, src, [[0, V]], ALU.is_equal, 0.0, 0, 0)
+        elif e == "s":
+            act(out, src)
+        else:
+            cp(out, src)
+
+    dma("y", W("kin", 0, 64), T.k0[:])
+    dma("s", W("rl", V * rank, V), T.rx[:])
+    dma("y", W("kin", 64, 64), T.k1[:])
+    dma("y", W("xin", 0, V), T.x0[:])
+    dma("y", W("wti", 0, 1), T.wt[:])
+    dma("y", W("thi", 0, 1), T.th[:])
+    dma("s", W("tki", 0, V), T.tk[:])
+
+    ROW, CENC, JC, XOC, WF, THF, HC, ROWH, KFB, TMP = 0, 1, 2, 3, 4, 5, 6, 7, 8, 12
+    run("g", W("pi", 0, 1), [], lambda: g.iota(T.pi[:, 0:1], [[0, 1]], 0, 1))
+    ms(W("zt", 0, 128), 0.0)
+    ms(W("ones", 0, V), 1.0)
+    asel(M("I"), W("zt", 0, 128), [[-1, 128]], ALU.not_equal, 1.0, 0)
+    ms(W("cz", 0, 272), 0.0)
+    put(M("D11", 11, 117, 16), [[-16, 8]], 1.0, -11)
+    ts(W("pi", 1, 1), W("pi", 0, 1), 15, ALU.bitwise_and)
+    ts(W("pi", 2, 1), W("pi", 0, 1), 3, ALU.bitwise_and)
+    scan(W("vi", 0, V), W("ones", 0, V), W("ones", 0, V), float(V * rank - 2049), ALU.mult, ALU.add)
+    act(R("cz", 272, 272 + V), W("ones", 0, V), scale=0.0)
+    act(R("cz", 272 + V, ZW_), W("ones", 0, ZW_ - 272 - V), scale=0.0)
+    act(M("I2"), M("I"), scale=65.0 / 64.0)
+    act(M("NI"), M("I"), scale=-1.0)
+    ms(W("ar", 0, 16), 128.0)
+    ms(W("qq", 0, 16), 130.0)
+    cp(C(ROW), W("pi", 1, 1))
+    ts(C(JC), W("pi", 2, 1), 1.0, ALU.add)
+    ts(C(XOC), W("pi", 2, 1), 4096.0, ALU.mult)
+    asel(W("zt", 0, 8), W("ones", 0, 8), [[-16, 8]], ALU.is_ge, 0.0, 0)
+    asel(M("Z", 15, 113, 16), W("zt", 0, 8), [[16, 8]], ALU.is_ge, 0.0, 15, -1)
+    asel(W("zt", 0, 128), W("ones", 0, 128), [[-16, 8], [0, 16]], ALU.is_ge, 0.0, 0)
+    asel(M("BLK"), W("zt", 0, 128), [[16, 8], [0, 16]], ALU.is_ge, 0.0, 15, -1)
+    share("rl", [0], "r")
+    act(M("ZN", 0, 144), M("Z", 0, 144), scale=-FAR)
+    act(M("IB"), M("I"), scale=FAR)
+    act(M("I65"), M("I"), scale=-65.0)
+    act(M("NB"), M("I"), scale=-BIG)
+    act(M("I63"), M("I"), scale=63.0 / 128.0)
+    weave(rank, "g")
+    ts(W("ktm", 0, 128), W("kin", 0, 128), 4096.0, ALU.is_ge, -8192.0, ALU.mult)
+    ts(C(CENC), C(ROW), 12.0, ALU.is_ge, -CEN, ALU.mult)
+    tt(W("ktm", 128, 128), W("ktm", 0, 128), W("kin", 0, 128), ALU.add)
+    ts(W("ar", 16, V), W("xin", 0, V), 128.0, ALU.add)
+    ts(W("kl0", 0, 64), W("ktm", 128, 64), 16.0, ALU.add)
+    ts(W("kl1", 0, 64), W("ktm", 192, 64), 16.0, ALU.add)
+    wait("y", "sn_r", final["sn_r"])
+    for j in range(4):
+        dma("y", W("bt", NXB + 4096 * j + V * rank, V), T.nx[:, V * j:V * j + V])
+
+    def table_tk(hf):
+        b = W("ps%d" % (3 + hf), 0, 512)
+        mms(b, [(M("D11"), W("vi", 512 * hf, 512))])
+        tt(W("tkf", V * rank + 512 * hf, 512), W("tki", 512 * hf, 512), b, ALU.add)
+
+    def small_consts():
+        cp(C(WF), W("wti", 0, 1))
+        cp(C(THF), W("thi", 0, 1))
+        ts(C(TMP), C(ROW), 15.0, ALU.is_equal)
+        cp(W("wb", 0, 1), C(WF))
+        ts(M("ZW", 0, 144), M("Z", 0, 144), C(WF), ALU.mult)
+
+    def more_consts():
+        for t in range(3):
+            ts(C(TMP + 2 + t), C(ROW), 12.0, ALU.is_equal, float(V * t + 20 - V * rank + 2048) - CEN, ALU.mult)
+        tt(C(TMP + 1), C(TMP), C(CENC), ALU.subtract)
+        ts(W("k16", 0, 128), W("ktm", 128, 128), -16.0, ALU.max, 16.0 - CEN, ALU.add)
+        ts(C(ROWH), C(ROW), 0.5, ALU.add)
+        ts(W("col", KFB, 3), W("col", TMP + 2, 3), C(TMP + 1), ALU.add)
+
+    def mid_consts_g():
+        put(R("uu", 16 + 13, 2064, 16), [[-1, 16], [-16, 8]], 1.0, 0)
+        put(M("D12", 12, 116, 16), [[-16, 8]], 1.0, -12)
+        asel(M("UP"), M("BLK"), [[-1, 128]], ALU.is_gt, 0.0, 0)
+        iota(W("ic", 0, 512), [[0, 2], [-16, 4], [0, 64]], 0)
+
+    def late_consts_g():
+        asel(R("keep", 0, V, 64), R("keep", 0, V, 64), [[0, 16]], ALU.is_ge, 0.0, -1, 0)
+        iota(W("il", 0, 256), [[0, 4], [1, 64]], -65)
+        rows = [[-16, 8], [0, 16]]
+        asel(M("LB"), M("I"), rows, ALU.not_equal, CEN, -15)
+        asel(M("LW"), M("NI"), rows, ALU.not_equal, 1.0, -12)
+        put(M("LO"), [[-16, 8], [0, 8], [-1, 2]], 1.0, -13)
+        iota(M("LF"), [[0, 8], [-1, 8], [0, 2]], 0)
+        put(M("LW"), rows, CEN, -15)
+        put(M("LO"), rows, CEN, -15)
+        asel(M("LF"), M("LF"), rows, ALU.is_equal, 0.0, -15)
+        for j in range(4):
+            put(M("PF", 12 + j, 420 - j, 16), [[-1, 3], [-16, 9]], 1.0, -10)
+            put(M("PK0", 12 + j, 276 - j, 16), [[-1, 2], [-16, 9]], 1.0, -2 * j - 2)
+        put(M("LF"), rows, 1.0, -10)
+        for r0 in (0, 13):
+            put(M("ZK0", 15, 273, 16), [[-1, 2], [-16, 9]], 1.0, -r0)
+        for cc in (13, 14):
+            for k in ("LO", "LF"):
+                a = M(k, cc, 128 - cc, 16)
+                asel(a, a, [[0, 8]], ALU.is_ge, 0.0, -1, 0)
+
+    def ga(src, lo, n, win):
+        act(W("ta", lo, n), G(src, 0, 16 + win, "kl0", lo // 16, n // 16))
+
+    def gb(src, lo, n, win):
+        tt(W("tb", lo, n), G(src, 0, 16 + win, "kl1", lo // 16, n // 16), W("ta", lo, n), ALU.max)
+
+    def p1b(c, win, cut=False):
+        b = W("ps%d" % (c % 2), 0, 512)
+        mms(b, [(M("I2"), W("ar", 16 + 512 * c, 512))])
+        for (lo, n) in (((0, 256), (256, 256)) if cut else ((0, 512),)):
+            gb("ar", 512 * c + lo, n, win)
+        return lambda: tt(W("qq", 16 + 512 * c, 512), W("tb", 512 * c, 512), b, ALU.max)
+
+    def p1r(c):
+        b = W("ps%d" % (2 + c % 2), 0, 512)
+        mms(b, [(M("NI"), W("ar", 16 + 512 * c, 512)), (M("I"), W("tb", 512 * c, 512))])
+        act(W("ta", 512 * c, 512), b, ACT.Relu, bias=-2.0)
+
+    def p1s(c):
+        b = W("ps%d" % (4 + 2 * (c % 2)), 0, 512)
+        mms(b, [(M("I"), W("ar", 16 + 512 * c, 512)), (M("I"), W("ta", 512 * c, 512))])
+        act(W("qq", 16 + 512 * c, 512), b, bias=2.0)
+
+    def p2c(lo, n, e):
+        b, x = bank(n), W("ar", 16 + lo, n)
+        mms(b, [(M("I"), x), (M("I"), W("tb", lo, n))])
+        if e == "s":
+            act(x, b, bias=-1.25, scale=0.5)
+        else:
+            ts(x, b, 0.5, ALU.mult, -1.25, ALU.add)
+
+    def kf_half(t, hf):
+        b = W("ps%d" % (5 + hf), 0, 512)
+        mm(b, M("D12"), W("vi", 512 * hf, 512), True, False)
+        for kid in range(2):
+            for r in range(16):
+                mm(R(b[1][0][0], r, 512, 16), W("uu", 16 + 128 * r - kid, 128), W("k16", 64 * kid + 32 * hf, 32),
+                   False, kid == 1 and r == 15)
+        return lambda: act(W("dw", 256 + 512 * hf, 512), b, bias=C(KFB + t))
+
+    def wrap16(out, k, src, lo, n=V, first=None):
+        prs = [] if first is None else [first]
+        mms(out, prs + [(M(k, 15 - r), R(src, lo + r, lo + n, 16)) for r in range(16)])
+
+    def wrap4(out, k, src):
+        mms(out, [(M(k, 12 - 4 * kk), R(src, kk, 256, 4)) for kk in range(4)])
+
+    ga("ar", 0, 256, V)
+    ga("ar", 256, 256, V)
+    ga("ar", 512, 512, V)
+    small_consts()
+    act(W("uu", 0, V), W("ones", 0, V), scale=0.0)
+    act(W("uu", V, V), W("ones", 0, V), scale=0.0)
+    act(W("uu", 2048, 16), W("ones", 0, 16), scale=0.0)
+    f0 = p1b(0, V, True)
+    f1 = p1b(1, V)
+    mms(W("ps6", 0, 1), [(M("BLK"), W("wb", 0, 1))])
+    f0()
+    f1()
+    table_tk(0)
+    others = [o for o in range(N) if o != rank]
+
+    for t in range(3):
+        S = V * (t + 1)
+        B0 = S - V
+        nb = 16 + B0
+        c0, c1 = 2 * t, 2 * t + 1
+        old = list(range(2 * t))
+
+        def o2a(i):
+            if i < len(old):
+                ga("qq", 512 * i, 512, S)
+
+        def o2b(i):
+            if i < len(old):
+                gb("qq", 512 * i, 512, S)
+
+        def o2c(i):
+            if i < len(old):
+                p2c(512 * i, 512, "s")
+
+        for (lo, n) in PIECES:
+            ga("qq", B0 + lo, n, S)
+        if t == 0:
+            table_tk(1)
+            share(*RELAY[0])
+            weave(others[0], "g")
+            mid_consts_g()
+            share(*RELAY[1])
+            share(*RELAY[2])
+        else:
+            ts(W("kb", 0, 256), R("vi", 0, V, 4), float(2048 - V * rank + S + 15) - CEN, ALU.add)
+        gb("qq", B0, 256, S)
+        if t == 0:
+            ts(C(HC), W("ps6", 0, 1), -128.0, ALU.mult)
+        gb("qq", B0 + 256, 512, S)
+        p2c(B0, 256, "s")
+        gb("qq", B0 + 768, 256, S)
+        p2c(B0 + 256, 512, "s")
+        p2c(B0 + 768, 256, "v")
+        wrap16(W("ps6", 0, 64), "ZW", "ar", nb)
+        if t == 0:
+            weave(others[1], "s")
+            act(W("keep", 0, V), W("ones", 0, V))
+            late_consts_g()
+            more_consts()
+            ts(W("thl", 0, 64), W("ones", 0, 64), C(THF), ALU.mult)
+            weave(others[2], "v")
+        else:
+            ts(W("bt", XN0, V), W("ar", nb, V), -128.0, ALU.add)
+        o2a(0)
+        ts(W("c1", 0, 64), W("ps6", 0, 64), C(HC), ALU.add)
+        if t == 0:
+            cp(W("bt", 4096, 368), W("bt", 0, 368))
+        ts(W("c1", 64, 64), W("c1", 0, 64), 4095, ALU.bitwise_and)
+        for m in (0, 1, 2, 3):
+            ts(W("offl", 64 * m, 64), W("c1", 64, 64), float(97 * m + 31 * t), ALU.add)
+
+        def dist_v(m, lo, n):
+            tt(W("dd", V * m + lo, n), G("bt", 0, RCW, "offl", 64 * m + lo // 16, n // 16), W("ar", nb + lo, n), ALU.subtract)
+
+        def dist_abs(m, lo, n):
+            act(W("da", V * m + lo, n), W("dd", V * m + lo, n), ACT.Abs, bias=128.0)
+
+        def near(m, b):
+            wrap16(W(b, 0, 64), "ZN", "da", V * m, V, (M("IB"), W("thl", 0, 64)))
+
+        def score(m, b):
+            tt(W("sc", 64 * m, 64), W("val", 64 * m, 64), W(b, 0, 64), ALU.min)
+
+        act(W("dd", 0, V), G("bt", 0, RCW, "offl", 0, 64))
+        kf = [kf_half(t, 0)]
+        dist_v(1, 0, V)
+        bs = [bank(), bank()]
+        for hf in range(2):
+            mms(bs[hf], [(M("NI"), W("ar", nb + 512 * hf, 512)), (M("I"), W("dd", 512 * hf, 512))])
+        dist_abs(1, 0, V)
+        near(1, "ps3")
+        dist_v(2, 0, V)
+        for hf in range(2):
+            act(W("da", 512 * hf, 512), bs[hf], ACT.Abs, bias=128.0)
+        near(0, "ps4")
+        dist_v(3, 0, 512)
+        dist_abs(2, 0, V)
+        dist_v(3, 512, 512)
+        for k in range(4):
+            ts(W("val", 64 * k, 64), W("c1", 64, 64), 2.0, ALU.mult, float(2 * (8192 * (4 - k) + 97 * k + 31 * t) + 1), ALU.add)
+        score(1, "ps3")
+        near(2, "ps3")
+        dist_abs(3, 0, 512)
+        dist_abs(3, 512, 512)
+        score(0, "ps4")
+        near(3, "ps4")
+        kf[0]()
+        o2a(1)
+        if t == 0:
+            act(M("UN"), M("UP"), scale=-1.0)
+            ts(W("kb", 0, 256), R("vi", 0, V, 4), float(2048 - V * rank + S + 15) - CEN, ALU.add)
+        tt(W("sc", 256, 64), W("sc", 0, 64), W("sc", 64, 64), ALU.max)
+        if t == 0:
+            ts(W("bt", XN0, V), W("ar", nb, V), -128.0, ALU.add)
+        o2b(0)
+        ts(W("sc", 320, 64), W("sc", 256, 64), 0.0, ALU.max)
+        score(2, "ps3")
+        if t == 0:
+            ts(W("vc", 0, 64), R("vi", 0, V, 16), C(ROW), ALU.add, float(256 + 2048 - V * rank), ALU.add)
+        score(3, "ps4")
+        tt(W("sc", 384, 64), W("sc", 320, 64), W("sc", 128, 64), ALU.max)
+        o2c(0)
+        o2a(2)
+        tt(W("bi", 0, 64), W("sc", 384, 64), W("sc", 192, 64), ALU.max)
+        if t == 0:
+            ts(W("vc", 64, 64), R("vi", 0, V, 16), C(ROW), ALU.add, float(XN0 + 2048 - V * rank), ALU.add)
+        ts(W("bi", 128, 64), W("bi", 0, 64), 7, ALU.bitwise_and)
+        ts(W("bi", 64, 64), W("bi", 0, 64), 1, ALU.logical_shift_right, 4095, ALU.bitwise_and)
+        for o in range(4):
+            ts(W("ask", 64 * o, 64), W("bi", 128, 64), float(2 * o + 1), ALU.is_equal)
+        ts(W("bi", 192, 64), W("bi", 64, 64), 4097.0, ALU.mult)
+        scan(W("cs", 0, 256), W("keep", 0, 256), W("ask", 0, 256), 0.0, ALU.mult, ALU.add)
+        ts(W("bi", 256, 64), W("bi", 192, 64), 2, ALU.logical_shift_right, 4095, ALU.bitwise_and)
+        ts(W("ra16", 256, 64), W("bi", 128, 64), 32.0, ALU.mult, 32.0, ALU.add)
+        cp(W("ls", 0, 64), W("bi", 256, 64))
+        if t == 0:
+            ms(W("bt", RCW, 16), 0.0)
+            ms(W("tkv", V, 16), 0.0)
+            ms(W("dw", 1280, 16), 0.0)
+        mms(W("ps5", 0, 256), [(M("I65"), W("ones", 0, 256)), (M("UN"), W("ask", 0, 256)), (M("BLK"), W("cs", 0, 256))])
+        act(W("tkv", 0, 512), G("tkf", 0, 4096, "ls", 0, 32))
+        tt(W("ra16", 0, 256), W("ask", 0, 256), W("ps5", 0, 256), ALU.mult)
+        for hf in range(2):
+            b = "ps%d" % (3 + hf)
+            mm(W(b, 0, 512), M("I"), W("ic", 0, 512), True, False)
+            for i in range(8):
+                mm(W(b, 64 * i, 64), M("BLK"), W("cs", 64 * (2 * hf + i // 4), 64), False, i == 7)
+            if hf == 0:
+                mms(W("ps7", 0, 64), [(M("I"), W("ra16", 64 * o, 64)) for o in range(4)])
+                mms(W("ps7", 64, 64), [(M("I"), W("ra16", 64 * o, 64)) for o in range(5)])
+        kf.append(kf_half(t, 1))
+        for hf in range(2):
+            act(W("sg", 512 * hf, 512), W("ps%d" % (3 + hf), 0, 512), ACT.Sign, bias=C(ROWH), scale=-1.0)
+        act(W("rs", 0, 256), W("ps5", 0, 256))
+        o2b(1)
+        act(W("tkv", 512, 512), G("tkf", 0, 4096, "ls", 32, 32))
+        kf[1]()
+        ts(W("ra", 0, 64), W("ps7", 0, 64), 0.0, ALU.is_ge, BIG, ALU.mult)
+        tt(W("ra", 64, 64), W("ra", 0, 64), W("ps7", 64, 64), ALU.max)
+        tt(W("ra", 128, 64), W("ra", 0, 64), W("bi", 64, 64), ALU.max)
+        scan(W("sn", 0, V), W("keep", 0, V), W("sg", 0, V), 0.0, ALU.mult, ALU.add)
+        tt(W("ra", 192, 128), W("ra", 64, 128), W("vc", 0, 128), ALU.min)
+        ts(W("ls", 256, 16), R("sn", 62, V, 64), 0.5, ALU.mult, 31.5, ALU.add)
+        cp(W("ls", 64, 128), W("ra", 192, 128))
+        for o in range(4):
+            tt(W("c2", 64 * o, 64), G("rs", 64 * o, 64 * o + 64, "ls", 256 + 4 * o, 4), W("il", 64 * o, 64), ALU.is_le)
+        wrap16(W("ps6", 0, 16), "Z", "c2", 0, 256)
+        ts(W("ra", 320, 16), R("sn", 62, V, 64), 8.0, ALU.mult, 504.0, ALU.add)
+        act(W("sel", 0, 512), G("bt", 0, NXB, "ls", 128, 32))
+        if OLDK_ON[t] == "v":
+            act(W("sel", 512, 512), G("bt", 0, NXB, "ls", 160, 32))
+        o2c(1)
+        o2b(2)
+        o2a(3)
+        tt(W("ra", 336, 16), W("ra", 320, 16), W("ps6", 0, 16), ALU.add)
+        cp(W("ls", 272, 16), W("ra", 336, 16))
+        (act if OLDK_ON[t] == "s" else cp)(W("rec", 256, 256), G("dw", 256, 1296, "ls", 272, 16))
+        if OLDK_ON[t] == "s":
+            act(W("sel", 512, 512), G("bt", 0, NXB, "ls", 160, 32))
+        tt(W("rec", 0, 256), G("tkv", 0, 1040, "ls", 272, 16), W("rec", 256, 256), ALU.add)
+        ts(W("r16", 0, 256), W("rec", 0, 256), C(CENC), ALU.add)
+        act(W("c2", 0, 256), W("rec", 0, 256), ACT.Relu, bias=1.0, scale=-1.0)
+        act(W("de", 0, 256), W("rec", 0, 256), bias=4.5 * BIG, scale=-BIG)
+        wrap4(W("ps3", 0, 64), "PF", "r16")
+        wrap4(W("ps3", 64, 64), "PO", "r16")
+        wrap4(W("ps3", 128, 64), "PV", "r16")
+        mms(W("ps5", 0, 256), [(M("LW"), W("r16", 0, 256))])
+        mms(W("ps6", 0, 256), [(M("LF"), W("r16", 0, 256))])
+        mms(W("ps5", 256, 256), [(M("I"), W("kb", 0, 256)), (M("LB"), W("r16", 0, 256)), (M("NB"), W("c2", 0, 256))])
+        mms(W("ps4", 0, 256), [(M("LO"), W("r16", 0, 256))])
+        ub = [bank(), bank()]
+        for hf in range(2):
+            mms(ub[hf], [(M("I"), W("bt", XN0 + 512 * hf, 512)), (M("I"), W("sel", 512 * hf, 512))])
+        act(W("de", 256, 256), W("ps6", 0, 256), ACT.Abs, scale=BIG)
+        act(W("ps7", 256, 256), W("de", 256, 256))
+        for hf in range(2):
+            act(W("ar", nb + 512 * hf, 512), ub[hf], bias=127.75, scale=0.5)
+        o2b(3)
+        sh = CEN - 4.0 - B0
+        ts(W("fl", 0, 64), W("ps3", 0, 64), C(JC), ALU.subtract)
+        ts(W("fl", 64, 64), W("ps3", 64, 64), C(XOC), ALU.add, 1040.0 + 2048.0 - sh, ALU.add)
+        tt(W("fl", 128, 64), W("fl", 0, 64), W("ps3", 0, 64), ALU.mult)
+        if t == 0:
+            ts(W("de", 1024, 256), W("ps5", 0, 256), 16.0, ALU.is_lt, 1024.0, ALU.mult)
+        else:
+            tt(W("de", 512, 256), W("de", 0, 256), W("ps5", 0, 256), ALU.max)
+        ts(W("fl", 192, 64), W("fl", 128, 64), 0.0, ALU.is_equal, -65536.0, ALU.mult)
+        if t == 0:
+            tt(W("de", 1280, 256), W("de", 1024, 256), W("ps5", 0, 256), ALU.add)
+        else:
+            tt(W("de", 768, 256), W("de", 512, 256), W("ps5", 256, 256), ALU.min)
+        tt(W("fl", 256, 64), W("fl", 192, 64), W("fl", 64, 64), ALU.add)
+        if t == 0:
+            tt(W("de", 512, 256), W("de", 1280, 256), W("de", 0, 256), ALU.max)
+        else:
+            tt(W("de", 1280, 256), W("de", 768, 256), W("ps7", 256, 256), ALU.min)
+        tt(W("fl", 320, 64), W("fl", 256, 64), W("ps3", 128, 64), ALU.max)
+        tt(W("ps6", 256, 256), W("ps4", 0, 256), W("de", 256, 256), ALU.subtract)
+        ts(W("ls", 192, 64), W("fl", 320, 64), sh, ALU.add)
+        o2c(2)
+        o2c(3)
+        for c in old[:EARLY]:
+            ga("ar", 512 * c, 512, S)
+        for hf in range(2):
+            act(W("ar", 16 + S + 512 * hf, 512), G("bt", RCW, NXB + 16384, "ls", 192 + 32 * hf, 32), bias=128.0)
+        if t == 0:
+            tt(W("de", 768, 256), W("de", 512, 256), W("ps5", 256, 256), ALU.min)
+            ts(W("thl", 0, 64), W("ps3", 0, 64), 0.0, ALU.is_gt, C(THF), ALU.mult)
+            tt(W("de", 1280, 256), W("de", 768, 256), W("ps7", 256, 256), ALU.min)
+        if t == 1:
+            ts(W("thl", 0, 64), W("ps3", 0, 64), 0.0, ALU.is_gt, C(THF), ALU.mult)
+        tt(W("dw", 0, 256), W("de", 1280, 256), W("ps6", 256, 256), ALU.max)
+        ts(W("d16", 0, 256), W("dw", 0, 256), 0.0, ALU.max, -CEN, ALU.add)
+        wrap4(W("ps4", 0, 64), "PK0", "d16")
+        wrap4(W("ps4", 64, 64), "PK1", "d16")
+        for c in old[EARLY:]:
+            ga("ar", 512 * c, 512, S)
+        ts(W("dv", 0, 512), G("dw", 0, 1280, "ls", 64, 32), 0.0, ALU.max, -CEN, ALU.add)
+        ts(W("kl0", 64 * t + 64, 64), W("ps4", 0, 64), CEN, ALU.add)
+        ts(W("kl1", 64 * t + 64, 64), W("ps4", 64, 64), CEN, ALU.add)
+        ts(W("dv", 512, 512), G("dw", 0, 1280, "ls", 96, 32), 0.0, ALU.max, -CEN, ALU.add)
+        if t < 2:
+            cp(W("k16", 0, 128), W("ps4", 0, 128))
+        wrap16(W("ps3", 0, 64), "ZK0", "dv", 0)
+        wrap16(W("ps6", 0, 64), "ZK1", "dv", 0)
+        E = S + V
+        ga("ar", S, 512, E)
+        ga("ar", S + 512, 512, E)
+        seq = [(c, S) for c in old] + [(c1 + 1, E), (c1 + 2, E), (c0, E), (c1, E)]
+        nr = RELU_CHUNKS[t]
+        gb("ar", 512 * seq[0][0], 512, seq[0][1])
+        ts(W("kl0", 64 * t, 64), W("ps3", 0, 64), 2 * CEN, ALU.add)
+        ts(W("kl1", 64 * t, 64), W("ps6", 0, 64), 2 * CEN, ALU.add)
+        ga("ar", B0, 512, E)
+        ga("ar", B0 + 512, 512, E)
+        for (c, w) in seq[1:nr]:
+            gb("ar", 512 * c, 512, w)
+        side = []
+        for (c, w) in seq[:nr]:
+            side.append((p1r, c))
+        for (c, w) in seq[:nr]:
+            side.insert(min(len(side), side.index((p1r, c)) + 2), (p1s, c))
+        pend = None
+        rest = seq[nr:]
+        for i, (c, w) in enumerate(rest):
+            f = p1b(c, w)
+            if pend is not None:
+                pend()
+            pend = f
+            k = -(-len(side) // max(1, len(rest) - 1 - i))
+            for (fn, cc) in side[:k]:
+                fn(cc)
+            side = side[k:]
+        pend()
+
+    def last(c):
+        lo = 512 * c
+        b, x, m = bank(), W("ar", 16 + lo, 512), W("tb", lo, 512)
+        if c in LAST_V:
+            mms(b, [(M("I63"), x), (M("I63"), m)])
+            ts(W("yo", lo, 512), b, MAGIC - 127.0, ALU.add, -MAGIC, ALU.add)
+        else:
+            mms(b, [(M("I"), x), (M("I"), m)])
+            act(W("dd", lo, 512), b, bias=-1.25, scale=0.5)
+
+    def result(c):
+        lo = 512 * c
+        if c not in LAST_V:
+            ts(W("yo", lo, 512), W("dd", lo, 512), -128.0, ALU.add)
+        if c >= 6:
+            dma("y", T.y[:, lo:lo + 512], W("yo", lo, 512))
+        elif c % 2:
+            dma("y", T.y[:, lo - 512:lo + 512], W("yo", lo - 512, V))
+
+    ga("qq", 0, 256, 4096)
+    ga("qq", 256, 256, 4096)
+    ga("qq", 512, 512, 4096)
+    for c in range(8):
+        if c == 0:
+            gb("qq", 0, 256, 4096)
+            gb("qq", 256, 256, 4096)
+        elif c == 7:
+            gb("qq", 3584, 384, 4096)
+            gb("qq", 3968, 128, 4096)
+        else:
+            gb("qq", 512 * c, 512, 4096)
+        if c + 2 < 8:
+            ga("qq", 512 * (c + 2), 512, 4096)
+        if c >= 1:
+            last(c - 1)
+        if c >= 2:
+            result(c - 2)
+    result(6)
+    for (lo, n) in ((3584, 384), (3968, 128)):
+        b = bank(n)
+        mms(b, [(M("I63"), W("ar", 16 + lo, n)), (M("I63"), W("tb", lo, n))])
+        ts(W("yo", lo, n), b, MAGIC - 127.0, ALU.add, -MAGIC, ALU.add)
+        dma("y" if n > 128 else "s", T.y[:, lo:lo + n], W("yo", lo, n))
+    for sem in final:
+        wait("g" if sem == "cg" else "y", sem, final[sem])

@@ -3,50 +3,157 @@ from concourse.mybir import AluOpType as ALU, ActivationFunctionType as ACT
 
 N = 4
 V = 1024
-RCW = 4096 + 368
-XN0 = RCW + 16
+RCW = 4096 + 304
+RL0 = RCW
+ZR0 = RL0 + 4096
+XN0 = ZR0 + 16
 NXB = XN0 + V
 CEN = 2064.0
 BIG = 16384.0
 FAR = 131072.0
 MAGIC = 12582912.0
-RELU_CHUNKS = (1, 2, 2)
-LAST_V = (1, 3, 5, 7)
-OLDK_ON = ("s", "v", "v")
-EARLY = 2
-PIECES = ((0, 256), (256, 512), (768, 256))
-RELAY = (("tkf", [0], "t"), ("bt", [NXB, NXB + 4096], "n"), ("bt", [NXB + 8192, NXB + 12288], "m"))
+RELAY = (("tkt", [0], "t"), ("bt", [NXB, NXB + 4096], "n"), ("bt", [NXB + 8192, NXB + 12288], "m"))
 
-MATS = {"I": 128, "I2": 128, "I65": 128, "IB": 128, "I63": 128, "NI": 128, "NB": 128, "BLK": 128, "UP": 128, "UN": 128,
-        "LW": 128, "LB": 128, "LF": 128, "ZW": 144, "ZN": 144}
-ZMATS = {"Z": 144, "D11": 128, "ZK0": 144, "ZK1": 144, "PF": 144, "PO": 144, "PV": 144, "PK0": 144, "PK1": 144,
-         "D12": 128, "LO": 128}
-MOFF = {}
-for _d in (MATS, ZMATS):
-    _o = 0
-    for _k in _d:
-        MOFF[_k] = _o
-        _o += _d[_k]
-ZW_ = sum(ZMATS.values())
+DIST = (("s", "vs", "vs", "vs"),) * 3
+EARLY = False
+HALVE = ("s", "s", "s")
+RELU = ((), (0,), (0, 2), (0, 2, 4, 6))
+LAST_V = (3, 7)
+FILL = ("ss", "ss", "ss")
+NEW_V = (0, 1, 2, 3)
+PIECES = ((0, 256), (256, 384), (640, 256), (896, 128))
+OLD = 512
+TAIL = ((0, 512), (512, 512), (1024, 512), (1536, 512))
+FIRST = ((0, 128), (128, 384), (512, 384), (896, 128))
+WEAVE = ("v", "g", "s", "v")
 
-SCRATCH = {"bt": ("sbuf", [128, NXB + 16384], "bfloat16"), "cm": ("sbuf", [128, sum(MATS.values())], "bfloat16"),
-           "cz": ("sbuf", [128, ZW_], "bfloat16")}
-for _t, _l in (("bfloat16", (("rl", 4096), ("xin", V), ("ar", 4112), ("qq", 4112), ("ta", 4096), ("tb", 4096), ("dd", 4096),
-                             ("da", 4096), ("yo", 4096), ("sel", V), ("ones", V), ("uu", 2064), ("zt", 128), ("wb", 8),
-                             ("thl", 64), ("ask", 256), ("keep", V), ("cs", 256), ("ic", 512), ("il", 256), ("rs", 256),
-                             ("sg", V), ("sn", V), ("c2", 256))),
-               ("float32", (("tkf", 4096), ("tkv", 1040), ("rec", 512), ("dw", 1296), ("ktm", 256), ("col", 32), ("val", 256),
-                            ("sc", 512), ("ra", 512), ("vc", 128), ("de", 1536), ("fl", 512))),
-               ("float16", (("vi", V), ("dv", V), ("k16", 128), ("r16", 256), ("kb", 256), ("d16", 256), ("ra16", 320))),
-               ("int32", (("tki", V), ("kin", 128), ("wti", 8), ("thi", 8), ("pi", 8), ("c1", 128), ("bi", 320))),
-               ("uint16", (("kl0", 256), ("kl1", 256), ("offl", 256), ("ls", 288)))):
+CYC, GATHER, HOP, PECYC = 0.9, 1.56, 90.0, 0.45
+TURNS = 4
+GIVE = {"v": 1.0, "s": 1.0, "p": 0.3, "g": 0.3, "y": 0.0}
+GRACE = {"v": 300.0, "s": 300.0, "p": 50.0, "g": 50.0, "y": 0.0}
+LOAD = 2000.0
+ARRIVE = {"r": (1500.0, 900.0), "t": (10000.0, 0.0), "n": (14000.0, 0.0), "m": (16000.0, 0.0)}
+
+DIAG = {"I": 1.0, "I2": 65.0 / 64.0, "I63": 63.0 / 128.0, "NI": -1.0, "C2": 2.0, "IB": FAR, "BI": BIG, "NBI": -BIG,
+        "N2B": -2 * BIG, "IK": 1024.0, "N4": -4.0, "I4": 0.25 if EARLY else 0.0625}
+MATS = list(DIAG) + ["N3B", "DL", "DH", "BLK", "BB", "UN", "RF", "B12", "RW", "RH", "LO0", "LO1", "TA", "TB"]
+WIDE = ["Z", "ZW", "ZN", "ZM", "ZP", "ZK0", "ZK1", "PK0", "PK1", "PFI", "PG"]
+MOFF = {k: 128 * i for i, k in enumerate(MATS)}
+MOFF.update({k: 144 * i for i, k in enumerate(WIDE)})
+
+SCRATCH = {"bt": ("sbuf", [128, NXB + 16384], "bfloat16"), "cm": ("sbuf", [128, 128 * len(MATS)], "bfloat16"),
+           "cz": ("sbuf", [128, 144 * len(WIDE)], "bfloat16")}
+for _t, _l in (("bfloat16", (("x_0", 1040), ("x_1", 2064), ("x_2", 3088), ("x_3", 4112), ("q_0", 1040), ("q_1", 2064),
+                             ("q_2", 3088), ("q_3", 4112), ("ta", 4096), ("tb", 4096), ("tc", 4096), ("td", 4096), ("dd", 4096),
+                             ("da", 4096), ("yo", 4096), ("sel", V), ("ones", 512), ("zt", 384), ("t8", 128), ("thl", 64),
+                             ("ask", 256), ("keep", 256), ("cs", 256), ("cg", 256), ("c16", 64), ("oc", 16), ("hi", V), ("rs", V),
+                             ("il", 64), ("ra", 256), ("sg", V), ("sn", V), ("mask", 256), ("ob", 64), ("inv", 64), ("mk", V),
+                             ("rm", 384))),
+               ("float32", (("col", 32), ("val", 256), ("sc", 192), ("pay", 128), ("wk", 512), ("de", 768),
+                            ("c0", 64), ("tkt", 4096))),
+               ("float16", (("q16", V), ("k16", 128), ("r16", 256), ("kb", V), ("d16", 256), ("pr", 768), ("k4", 512), ("vl", 128),
+                            ("tcc", 64), ("rq", 128), ("rb", 64), ("rd", 128))),
+               ("int32", (("tki", V), ("kin", 128), ("wti", 8), ("thi", 8), ("pi", 8), ("c1", 128), ("bi", 192))),
+               ("uint16", (("kz", 128), ("kl0", 256), ("kl1", 256), ("offl", 256), ("ls", 224)))):
     for _k, _n in _l:
         SCRATCH[_k] = ("sbuf", [128, _n], _t)
+if not EARLY:
+    SCRATCH["tkt"] = ("sbuf", [128, 4096], "int32")
+    SCRATCH["d32"] = ("sbuf", [128, 272], "float32")
 for _b in range(8):
     SCRATCH["ps%d" % _b] = ("psum", [128, 512], "float32")
 
-SEMAPHORES = (["cv", "cs", "cp", "cg", "ar_r", "ar_t", "ar_n", "ar_m", "sn_r", "sn_t", "sn_n", "sn_m"]
-              + ["dm%d" % i for i in range(24)])
+SEMAPHORES = (["cv", "cs", "cp", "cg", "ar_t", "ar_n", "ar_m", "sn_r", "sn_t", "sn_n", "sn_m"] + ["ar_r%d" % i for i in range(N)]
+              + ["dm%d" % i for i in range(32)])
+
+
+def run(ops, pred, release, rank, choose=False):
+    n = len(ops)
+    succ = [[] for _ in ops]
+    for b in range(n):
+        for a in pred[b]:
+            succ[a].append(b)
+    order = sorted(range(n), key=lambda i: (-rank[i], i))
+    start, free = [None] * n, {e: 0.0 for e in (None, "v", "s", "p", "g", "y")}
+    wait = [len(p) for p in pred]
+    ready = {i: release[i] for i in range(n) if not wait[i]}
+    while ready:
+        t, _, b, e = min((max(ready[i], free[e]), -rank[i], i, e) for i in ready
+                         for e in (ops[i]["alt"] if choose and ops[i]["alt"] else [ops[i]["e"]]))
+        if ops[b]["alt"]:
+            ops[b].update(e=e, cost=ops[b]["alt"][e][0], fn=ops[b]["alt"][e][1])
+        if e is not None:
+            soon, hold = {}, []
+            for i in order:
+                if rank[i] <= rank[b]:
+                    break
+                if start[i] is None:
+                    soon[i] = max([soon.get(a, start[a]) + ops[a]["cost"] + pred[i][a] for a in pred[i]] + [t, free[ops[i]["e"]]])
+                    if ops[i]["e"] == e and t + ops[b]["cost"] - soon[i] > GIVE[e] * (soon[i] - t) + GRACE[e]:
+                        hold.append(soon[i])
+            if hold and min(hold) > t:
+                ready[b] = min(hold) + 1.0
+                continue
+            free[e] = t + ops[b]["cost"]
+        start[b] = t
+        del ready[b]
+        for c in succ[b]:
+            wait[c] -= 1
+            if not wait[c]:
+                ready[c] = max([start[a] + ops[a]["cost"] + pred[c][a] for a in pred[c]] + [release[c]])
+    return start
+
+
+def place(ops, extra):
+    n = len(ops)
+    pred = [{a: ops[a]["lat"] + HOP if o["dep"][a] else 1.0 for a in o["dep"]} for o in ops]
+    for (a, b) in extra:
+        pred[b][a] = ops[a]["lat"] + HOP
+    back = [{} for _ in ops]
+    for b in range(n):
+        for a in pred[b]:
+            back[a][b] = pred[b][a]
+    free = [dict(o, e=None, alt=None) for o in ops]
+    tail = [o["lat"] for o in ops]
+    late, best = run(free, back, tail, [0.0] * n), None
+    for _ in range(TURNS):
+        start = run(ops, pred, [0.0] * n, [late[i] + ops[i]["cost"] for i in range(n)], True)
+        span = max(start[i] + ops[i]["cost"] + tail[i] for i in range(n))
+        if best is None or span < best[0]:
+            best = (span, start, [o["e"] for o in ops])
+        late = run(ops, back, tail, [start[i] + ops[i]["cost"] for i in range(n)])
+    for o, e in zip(ops, best[2]):
+        if o["alt"]:
+            o.update(e=e, cost=o["alt"][e][0], fn=o["alt"][e][1])
+    return best[1], [list(x) for x in back]
+
+
+def banks(ops, tiles):
+    start, succ = place(ops, [])
+    end = [start[i] + o["cost"] + o["lat"] for i, o in enumerate(ops)]
+    held, where, extra = [[] for _ in range(8)], {}, []
+
+    def reaches(a, goal):
+        seen, todo = {a}, [a]
+        while todo:
+            for b in succ[todo.pop()]:
+                if b in goal:
+                    return True
+                if b not in seen:
+                    seen.add(b)
+                    todo.append(b)
+        return False
+
+    for name in sorted(tiles, key=lambda k: start[tiles[k][0]]):
+        first = tiles[name][0]
+        for b in sorted(range(8), key=lambda b: max([end[i] for i in held[b]] + [0.0])):
+            if all(end[i] <= start[first] for i in held[b]) or not reaches(first, set(held[b])):
+                break
+        for i in held[b]:
+            extra.append((i, first))
+            succ[i].append(first)
+        held[b], where[name] = tiles[name], "ps%d" % b
+    return where, extra
 
 
 def rank_program(g, core, T, topo):
@@ -60,7 +167,7 @@ def rank_program(g, core, T, topo):
     def common(src, dsts):
         return [e for e in topo.engines(src, dsts[0]) if all(e in topo.engines(src, d) for d in dsts)]
 
-    def send(src, dsts, name, starts, tag):
+    def send(src, dsts, name, starts, tag, sem):
         eng = common(src, dsts)
         per = len(eng) // len(starts)
         ids = [DstId(rid=topo.addr(c)[0], pnc=topo.addr(c)[1]) for c in dsts]
@@ -68,9 +175,8 @@ def rank_program(g, core, T, topo):
         for i, s0 in enumerate(starts):
             a = T[name][:, s0:s0 + V]
             trs.append(RemoteDMATransfer(dst_ids=ids, dma_engine_mask=sum(1 << e for e in eng[i * per:(i + 1) * per]),
-                                         remote_sem=T.sem["ar_" + tag], src=a, dsts=[a] * len(ids)))
+                                         remote_sem=T.sem[sem], src=a, dsts=[a] * len(ids)))
         g.remote_dma_fused(trs, local_sem=T.sem["sn_" + tag])
-        return per * len(starts)
 
     def count(src, dsts, k):
         return len(common(src, dsts)) // k * k
@@ -85,154 +191,156 @@ def rank_program(g, core, T, topo):
         for c in ranks:
             if helper[c] == core:
                 o = T.rank_of(c)
-                done = {}
                 for (name, starts, tag) in RELAY:
                     g.wait_ge(T.sem["ar_" + tag], count(c, near_of(c) + [core], len(starts)))
-                    done[tag] = send(core, far_of(c), name, [s0 + V * o for s0 in starts], tag)
-                for tag in done:
-                    g.wait_ge(T.sem["sn_" + tag], done[tag])
+                    send(core, far_of(c), name, [s0 + V * o for s0 in starts], tag, "ar_" + tag)
+                for (name, starts, tag) in RELAY:
+                    g.wait_ge(T.sem["sn_" + tag], count(core, far_of(c), len(starts)))
         return
+
     Q = {"v": g.vector, "s": g.scalar, "p": g.tensor, "g": g, "y": g.sync}
-    cnt = {"v": 0, "s": 0, "p": 0, "g": 0}
-    seen = {e: {} for e in Q}
-    hist = {}
-    ndm = [0]
-    final = {}
-    group = []
+    ops, hist, tiles, where = [], {}, {}, {}
 
     def R(name, lo, hi, st=1):
-        ap = T[name][:, lo:hi] if st == 1 else T[name][:, lo:hi:st]
-        return (ap, [(name, lo, hi)])
+        return (name, lo, hi, st, None)
 
     def W(name, lo, n):
         return R(name, lo, lo + n)
 
     def G(name, lo, hi, oname, olo, n):
-        return (T[name][:, lo:hi].indirect(T[oname][:, olo:olo + n]), [(name, lo, hi), (oname, olo, olo + n)])
+        return (name, lo, hi, 1, W(oname, olo, n))
 
     def M(k, lo=0, n=128, st=1):
         return R("cm" if k in MATS else "cz", MOFF[k] + lo, MOFF[k] + lo + n, st)
 
     def C(i):
-        return R("col", i, i + 1)
+        return W("col", i, 1)
 
-    def wait(e, sem, val):
-        if seen[e].get(sem, 0) < val:
-            Q[e].wait_ge(T.sem[sem], val)
-            seen[e][sem] = val
-
-    def before(e, rd, wr):
-        need = {}
-        for w, regs in ((False, rd), (True, wr)):
-            for (n, lo, hi) in regs:
-                whole = n.startswith("ps")
-                for (l2, h2, w2, e2, sem, val) in hist.get(n, []):
-                    if (whole and e2 != e) or (l2 < hi and lo < h2 and (w or w2)):
-                        need[sem] = max(need.get(sem, 0), val)
-        for sem in need:
-            wait(e, sem, need[sem])
-
-    def note(e, rd, wr, sem, val):
-        for w, regs in ((False, rd), (True, wr)):
-            for (n, lo, hi) in regs:
-                h = hist.setdefault(n, [])
-                if w:
-                    h[:] = [x for x in h if not (lo <= x[0] and x[1] <= hi)]
-                h.append((lo, hi, w, e, sem, val))
-        final[sem] = max(final.get(sem, 0), val)
-
-    def split(out, ins):
-        rd = []
-        for a in ins:
-            if isinstance(a, tuple):
-                rd += a[1]
-        return rd + out[1][1:], out[1][:1]
+    def tile(n=512):
+        name = "#%d" % len(tiles)
+        tiles[name] = []
+        return W(name, 0, n)
 
     def A(a):
-        return a[0] if isinstance(a, tuple) else a
+        if not isinstance(a, tuple):
+            return a
+        ap = T[where.get(a[0], a[0])][:, a[1]:a[2]:a[3]] if a[3] > 1 else T[where.get(a[0], a[0])][:, a[1]:a[2]]
+        return ap if a[4] is None else ap.indirect(A(a[4]))
 
-    def run(e, out, ins, fn):
-        rd, wr = split(out, ins)
-        before(e, rd, wr)
-        cnt[e] += 1
-        fn().then_inc(T.sem["c" + e], 1)
-        note(e, rd, wr, "c" + e, cnt[e])
+    def size(a):
+        return len(range(a[1], a[2], a[3])) if a[4] is None else 16 * size(a[4])
+
+    def short(*xs):
+        return all(a[0] in SCRATCH and SCRATCH[a[0]][2] in ("bfloat16", "float16", "uint16") for a in xs)
+
+    def meets(a, b):
+        if a[2] <= b[1] or b[2] <= a[1]:
+            return False
+        return a[3] != b[3] or (a[1] - b[1]) % a[3] == 0
+
+    def add(e, outs, ins, cost, fn, lat=0.0, after=(), sem=None, behind=(), alt=None):
+        me, dep = len(ops), {a: a in after for a in list(after) + list(behind)}
+        ins = [a for a in ins if isinstance(a, tuple)]
+        ins = ins + [a[4] for a in ins if a[4] is not None]
+        for w, regs in ((False, ins), (True, outs)):
+            for a in regs:
+                for (b, w2, i) in hist.get(a[0], []):
+                    if a[0] in tiles:
+                        if w or w2 or e != ops[i]["e"]:
+                            dep[i] = dep.get(i, False) or e != "p" or ops[i]["e"] != "p"
+                    elif (w or w2) and meets(a, b):
+                        dep[i] = True
+        for w, regs in ((False, ins), (True, outs)):
+            for a in regs:
+                h = hist.setdefault(a[0], [])
+                if w and a[3] == 1 and a[0] not in tiles:
+                    h[:] = [x for x in h if not (a[1] <= x[0][1] and x[0][2] <= a[2])]
+                h.append((a, w, me))
+                if a[0] in tiles and me not in tiles[a[0]]:
+                    tiles[a[0]].append(me)
+        ops.append({"e": e, "dep": dep, "cost": cost, "lat": lat, "fn": fn, "sem": sem, "alt": alt})
+        return me
+
+    def vcost(out, a, per):
+        return 50.0 + GATHER * CYC * size(a) if a[4] is not None else max(64.0, per * size(a)) * CYC
 
     def ts(out, a, s1, op0, s2=None, op1=None):
-        if op1 is None:
-            run("v", out, [a, s1], lambda: g.vector.tensor_scalar(A(out), A(a), A(s1), None, op0))
-        else:
-            run("v", out, [a, s1, s2], lambda: g.vector.tensor_scalar(A(out), A(a), A(s1), A(s2), op0, op1))
+        more = (op0,) if op1 is None else (op0, op1)
+        return add("v", [out], [a, s1, s2], vcost(out, a, 0.5 if short(out, a) else 1.0),
+                   lambda: g.vector.tensor_scalar(A(out), A(a), A(s1), A(s2), *more))
 
     def tt(out, a, b, op):
-        run("v", out, [a, b], lambda: g.vector.tensor_tensor(A(out), A(a), A(b), op))
+        return add("v", [out], [a, b], vcost(out, a, 1.0 if a[0] in tiles or b[0] in tiles else 2.0),
+                   lambda: g.vector.tensor_tensor(A(out), A(a), A(b), op))
 
     def cp(out, a):
-        run("v", out, [a], lambda: g.vector.tensor_copy(A(out), A(a)))
+        return add("v", [out], [a], vcost(out, a, 0.5 if short(out, a) else 1.0), lambda: g.vector.tensor_copy(A(out), A(a)))
 
     def ms(out, c):
-        run("v", out, [], lambda: g.vector.memset(A(out), c))
+        return add("v", [out], [], vcost(out, out, 0.5 if short(out) else 1.0), lambda: g.vector.memset(A(out), c))
 
     def scan(out, a, b, init, op0, op1):
-        run("v", out, [a, b], lambda: g.vector.tensor_tensor_scan(A(out), A(a), A(b), init, op0, op1))
+        return add("v", [out], [a, b], vcost(out, a, 0.5), lambda: g.vector.tensor_tensor_scan(A(out), A(a), A(b), init, op0, op1))
 
     def act(out, a, func=ACT.Identity, bias=0.0, scale=1.0):
-        run("s", out, [a, bias, scale], lambda: g.scalar.activation(A(out), A(a), func, bias=A(bias), scale=A(scale)))
+        return add("s", [out], [a, bias, scale], vcost(out, a, 1.0),
+                   lambda: g.scalar.activation(A(out), A(a), func, bias=A(bias), scale=A(scale)))
+
+    def lin(out, a, scale=1.0, bias=0.0):
+        alt = {"v": (vcost(out, a, 0.5 if short(out, a) else 1.0),
+                     lambda: g.vector.tensor_scalar(A(out), A(a), A(scale), A(bias), ALU.mult, ALU.add)),
+               "s": (vcost(out, a, 1.0), lambda: g.scalar.activation(A(out), A(a), ACT.Identity, bias=A(bias), scale=A(scale)))}
+        return add("v", [out], [a, scale, bias], alt["v"][0], alt["v"][1], alt=alt)
 
     def asel(out, a, pat, op, fill, base, cm=1):
-        run("g", out, [a], lambda: g.affine_select(A(out), A(a), pat, op, fill, base, cm))
+        return add("g", [out], [a], 170.0 + 2 * CYC * size(a), lambda: g.affine_select(A(out), A(a), pat, op, fill, base, cm))
 
     def put(a, pat, val, base):
         asel(a, a, pat, ALU.not_equal, val, base)
 
-    def iota(out, pat, base):
-        run("g", out, [], lambda: g.iota(A(out), pat, base, 0, allow_small_or_imprecise_dtypes=True))
+    def iota(out, pat, base, cm=0):
+        if SCRATCH[out[0]][2] == "int32":
+            return add("g", [out], [], 130.0 + 2 * CYC * size(out), lambda: g.iota(A(out), pat, base, cm))
+        return add("g", [out], [], 130.0 + 2 * CYC * size(out),
+                   lambda: g.iota(A(out), pat, base, cm, allow_small_or_imprecise_dtypes=True))
 
-    def mm(out, lt, rhs, start, stop):
-        rd, wr = split(out, [lt, rhs])
-        before("p", rd, wr)
-        i = g.tensor.matmul(A(out), A(lt), A(rhs), start, stop)
-        group.append((rd, wr))
-        if stop:
-            cnt["p"] += 1
-            i.then_inc(T.sem.cp, 1)
-            for (r_, w_) in group:
-                note("p", r_, w_, "cp", cnt["p"])
-            del group[:]
+    def mms(out, pairs, first=True, final=True, after=()):
+        def fn():
+            for i, (lt, rhs) in enumerate(pairs):
+                last = g.tensor.matmul(A(out), A(lt), A(rhs), first and i == 0, final and i == len(pairs) - 1)
+            return last
+        return add("p", [out], [x for p in pairs for x in p], sum(10.0 + PECYC * max(64, size(r)) for (_, r) in pairs), fn, 60.0, after)
 
-    def mms(out, pairs):
-        for i, (lt, rhs) in enumerate(pairs):
-            mm(out, lt, rhs, i == 0, i == len(pairs) - 1)
+    ndm = [0]
 
-    def dma(e, out, in_):
-        rd = in_[1] if isinstance(in_, tuple) else []
-        wr = out[1] if isinstance(out, tuple) else []
-        before(e, rd, wr)
-        sem = "dm%d" % ndm[0]
+    def dma(e, out, in_, nbytes, after=(), behind=()):
         ndm[0] += 1
-        Q[e].dma_start(A(out), A(in_)).then_inc(T.sem[sem], 16)
-        note("dma", rd, wr, sem, 16)
+        return add(e, [out] if isinstance(out, tuple) else [], [in_], 60.0 + (nbytes / 300.0 if e == "y" else 0.0),
+                   lambda: Q[e].dma_start(A(out), A(in_)), LOAD, after, ("dm%d" % (ndm[0] - 1), 16), behind)
+
+    sent = {}
 
     def share(name, starts, tag):
         own = [s0 + V * rank for s0 in starts]
-        before("g", [(name, s0, s0 + V) for s0 in own], [])
+        src = [W(name, s0, V) for s0 in own]
         if tag == "r":
-            final["sn_r"] = send(core, [c for c in ranks if c != core], name, own, tag)
-            got = sum(count(c, [d for d in ranks if d != c], 1) for c in ranks if c != core)
+            to = [ranks[(rank + k) % N] for k in range(1, N)]
+            me = add("g", [], src, 3000.0, lambda: send(core, to, name, own, tag, "ar_r%d" % rank), sem=())
+            for k in range(1, N):
+                o = (rank - k) % N
+                add(None, [W(name, starts[0] + V * o, V)], [], 0.0, None, ARRIVE[tag][0] + k * ARRIVE[tag][1], [me],
+                    ("ar_r%d" % o, count(ranks[o], [c for c in ranks if c != ranks[o]], 1)))
         else:
-            final["sn_" + tag] = send(core, near_of(core) + [helper[core]], name, own, tag)
+            to = near_of(core) + [helper[core]]
+            me = add("g", [], src, 400.0, lambda: send(core, to, name, own, tag, "ar_" + tag), sem=())
             got = (sum(count(c, near_of(c) + [helper[c]], len(starts)) for c in near_of(core))
                    + sum(count(helper[c], far_of(c), len(starts)) for c in far_of(core)))
-        note("rem", [], [(name, s0 + V * o, s0 + V * o + V) for s0 in starts for o in range(N) if o != rank], "ar_" + tag, got)
-
-    rot = [0]
-
-    def bank(n=512):
-        rot[0] = (rot[0] + 1) % 3
-        return W("ps%d" % rot[0], 0, n)
+            add(None, [W(name, s0 + V * o, V) for s0 in starts for o in range(N) if o != rank], [], 0.0, None, ARRIVE[tag][0], [me],
+                ("ar_" + tag, got))
+        sent[tag] = add(None, [], [], 0.0, None, ARRIVE["r"][0] + 2000.0, [me], ("sn_" + tag, count(core, to, len(starts))))
 
     def weave(o, e):
-        out, src = R("bt", o, 4096, 4), W("rl", V * o, V)
+        out, src = R("bt", o, 4096, 4), W("bt", RL0 + V * o, V)
         if e == "g":
             asel(out, src, [[0, V]], ALU.is_equal, 0.0, 0, 0)
         elif e == "s":
@@ -240,466 +348,401 @@ def rank_program(g, core, T, topo):
         else:
             cp(out, src)
 
-    dma("y", W("kin", 0, 64), T.k0[:])
-    dma("s", W("rl", V * rank, V), T.rx[:])
-    dma("y", W("kin", 64, 64), T.k1[:])
-    dma("y", W("xin", 0, V), T.x0[:])
-    dma("y", W("wti", 0, 1), T.wt[:])
-    dma("y", W("thi", 0, 1), T.th[:])
-    dma("s", W("tki", 0, V), T.tk[:])
+    def wrap16(k, src, lo, n=V):
+        return [(M(k, 15 - r), R(src, lo + r, lo + n, 16)) for r in range(16)]
 
-    ROW, CENC, JC, XOC, WF, THF, HC, ROWH, KFB, TMP = 0, 1, 2, 3, 4, 5, 6, 7, 8, 12
-    run("g", W("pi", 0, 1), [], lambda: g.iota(T.pi[:, 0:1], [[0, 1]], 0, 1))
-    ms(W("zt", 0, 128), 0.0)
-    ms(W("ones", 0, V), 1.0)
-    asel(M("I"), W("zt", 0, 128), [[-1, 128]], ALU.not_equal, 1.0, 0)
-    ms(W("cz", 0, 272), 0.0)
-    put(M("D11", 11, 117, 16), [[-16, 8]], 1.0, -11)
-    ts(W("pi", 1, 1), W("pi", 0, 1), 15, ALU.bitwise_and)
-    ts(W("pi", 2, 1), W("pi", 0, 1), 3, ALU.bitwise_and)
-    scan(W("vi", 0, V), W("ones", 0, V), W("ones", 0, V), float(V * rank - 2049), ALU.mult, ALU.add)
-    act(R("cz", 272, 272 + V), W("ones", 0, V), scale=0.0)
-    act(R("cz", 272 + V, ZW_), W("ones", 0, ZW_ - 272 - V), scale=0.0)
-    act(M("I2"), M("I"), scale=65.0 / 64.0)
-    act(M("NI"), M("I"), scale=-1.0)
-    ms(W("ar", 0, 16), 128.0)
-    ms(W("qq", 0, 16), 130.0)
-    cp(C(ROW), W("pi", 1, 1))
-    ts(C(JC), W("pi", 2, 1), 1.0, ALU.add)
-    ts(C(XOC), W("pi", 2, 1), 4096.0, ALU.mult)
-    asel(W("zt", 0, 8), W("ones", 0, 8), [[-16, 8]], ALU.is_ge, 0.0, 0)
-    asel(M("Z", 15, 113, 16), W("zt", 0, 8), [[16, 8]], ALU.is_ge, 0.0, 15, -1)
-    asel(W("zt", 0, 128), W("ones", 0, 128), [[-16, 8], [0, 16]], ALU.is_ge, 0.0, 0)
-    asel(M("BLK"), W("zt", 0, 128), [[16, 8], [0, 16]], ALU.is_ge, 0.0, 15, -1)
-    share("rl", [0], "r")
-    act(M("ZN", 0, 144), M("Z", 0, 144), scale=-FAR)
-    act(M("IB"), M("I"), scale=FAR)
-    act(M("I65"), M("I"), scale=-65.0)
-    act(M("NB"), M("I"), scale=-BIG)
-    act(M("I63"), M("I"), scale=63.0 / 128.0)
-    weave(rank, "g")
-    ts(W("ktm", 0, 128), W("kin", 0, 128), 4096.0, ALU.is_ge, -8192.0, ALU.mult)
-    ts(C(CENC), C(ROW), 12.0, ALU.is_ge, -CEN, ALU.mult)
-    tt(W("ktm", 128, 128), W("ktm", 0, 128), W("kin", 0, 128), ALU.add)
-    ts(W("ar", 16, V), W("xin", 0, V), 128.0, ALU.add)
-    ts(W("kl0", 0, 64), W("ktm", 128, 64), 16.0, ALU.add)
-    ts(W("kl1", 0, 64), W("ktm", 192, 64), 16.0, ALU.add)
-    wait("y", "sn_r", final["sn_r"])
+    def wrap4(k, src, lo=0):
+        return [(M(k, 12 - 4 * kk), R(src, lo + kk, lo + 256, 4)) for kk in range(4)]
+
+    loads = []
+    for (name, n, src) in (("kin", 64, T.k0), ("x_0", V, T.x0), ("tki", V, T.tk), ("wti", 1, T.wt), ("thi", 1, T.th)):
+        out = W("tkt", V * rank, V) if name == "tki" and not EARLY else W(name, 0, n)
+        loads.append(dma("y", out, src[:], 256 * n, behind=loads[-1:]))
+    dma("s", W("bt", RL0 + V * rank, V), T.rx[:], 1 << 18, behind=[dma("s", W("kin", 64, 64), T.k1[:], 1 << 15)])
+    share("bt", [RL0], "r")
     for j in range(4):
-        dma("y", W("bt", NXB + 4096 * j + V * rank, V), T.nx[:, V * j:V * j + V])
+        dma("y", W("bt", NXB + 4096 * j + V * rank, V), T.nx[:, V * j:V * j + V], 1 << 18, [sent["r"]])
+    for k in range(N):
+        weave((rank - k) % N, WEAVE[k])
+    lin(W("bt", 4096, RCW - 4096), W("bt", 0, RCW - 4096))
 
-    def table_tk(hf):
-        b = W("ps%d" % (3 + hf), 0, 512)
-        mms(b, [(M("D11"), W("vi", 512 * hf, 512))])
-        tt(W("tkf", V * rank + 512 * hf, 512), W("tki", 512 * hf, 512), b, ALU.add)
+    ROW, JC, ZC, LOW, WF, THF, FC, HIGH, IC, TMP, INC, TBC, KBC = 0, 1, 2, 3, 4, 5, 6, 7, 8, 12, 16, 17, 20
+    rows = [[-16, 8], [0, 16]]
+    ms(W("zt", 0, 128), 0.0)
+    ms(W("ones", 0, 512), 1.0)
+    ms(W("x_0", V, 16), 0.0)
+    ms(W("q_0", V, 16), 2.0)
+    iota(W("pi", 0, 1), [[0, 1]], 0, 1)
+    asel(M("I"), W("zt", 0, 128), [[-1, 128]], ALU.not_equal, 1.0, 0)
+    asel(W("t8", 0, 128), W("ones", 0, 128), rows, ALU.is_ge, 0.0, 0)
+    asel(M("BLK"), W("t8", 0, 128), [[16, 8], [0, 16]], ALU.is_ge, 0.0, 15, -1)
+    for k in list(DIAG)[1:]:
+        lin(M(k), M("I"), DIAG[k])
+    for s in (1, 2, 3):
+        lin(W("x_%d" % s, 0, 16), W("zt", 0, 16), 0.0, 128.0)
+        lin(W("q_%d" % s, 0, 16), W("zt", 0, 16), 0.0, 130.0)
+    lin(W("bt", ZR0, 16), W("zt", 0, 16))
+    for (k, n) in (("Z", 144), ("ZK0", 432), ("PK1", 432), ("TB", 128)):
+        lin(M(k, 0, n), W("ones", 0, n), 0.0)
+    lin(M("TA"), M("I"))
 
-    def small_consts():
-        cp(C(WF), W("wti", 0, 1))
-        cp(C(THF), W("thi", 0, 1))
-        ts(C(TMP), C(ROW), 15.0, ALU.is_equal)
-        cp(W("wb", 0, 1), C(WF))
-        ts(M("ZW", 0, 144), M("Z", 0, 144), C(WF), ALU.mult)
+    def move(k, col, row, val, src="I"):
+        lin(M(k, col, 113, 16), M(src, row, 113, 16), val)
 
-    def more_consts():
-        for t in range(3):
-            ts(C(TMP + 2 + t), C(ROW), 12.0, ALU.is_equal, float(V * t + 20 - V * rank + 2048) - CEN, ALU.mult)
-        tt(C(TMP + 1), C(TMP), C(CENC), ALU.subtract)
-        ts(W("k16", 0, 128), W("ktm", 128, 128), -16.0, ALU.max, 16.0 - CEN, ALU.add)
-        ts(C(ROWH), C(ROW), 0.5, ALU.add)
-        ts(W("col", KFB, 3), W("col", TMP + 2, 3), C(TMP + 1), ALU.add)
+    move("Z", 15, 0, 1.0, "BLK")
+    lin(M("ZN", 0, 144), M("Z", 0, 144), -FAR)
+    if any("v" in d for d in DIST):
+        lin(M("ZM", 0, 144), M("Z", 0, 144), -2 * FAR)
+        lin(M("ZP", 0, 144), M("Z", 0, 144), FAR)
+    lin(M("BB"), M("BLK"), 2 * BIG)
+    asel(W("t8", 0, 128), M("BLK"), [[-1, 128]], ALU.is_gt, 0.0, 0)
+    lin(W("zt", 128, 128), W("t8", 0, 128), -1.0)
+    asel(M("UN"), W("zt", 128, 128), [[-1, 128]], ALU.not_equal, -BIG, 0)
+    asel(M("RF"), W("zt", 0, 128), rows, ALU.not_equal, 1.0, -10)
+    asel(M("B12"), M("BLK"), [[0, 8], [1, 16]], ALU.is_ge, 0.0, -12, 0)
+    asel(W("zt", 256, 128), M("BLK"), [[0, 8], [-1, 16]], ALU.is_ge, 0.0, 11, 0)
+    for b in range(2):
+        asel(M("LO%d" % b), W("zt", 256, 128), [[0, 64], [1, 2]], ALU.is_equal, 0.0, -b, 0)
+    if EARLY:
+        put(M("ZK0", 15, 273, 16), [[-2, 2], [-16, 9]], 64.0, -12)
+        put(M("ZK0", 15, 273, 16), [[-2, 2], [-16, 9]], 1.0, -13)
+    else:
+        put(M("ZK0", 15, 273, 16), [[-1, 2], [-16, 9]], 1.0, 0)
+    for j in range(4):
+        for b in range(2):
+            move("PK%d" % b, 12 + j, 2 * j + 2 + b, 1.0)
+        move("PFI", 12 + j, 12 + j, 1.0)
+        move("PG", 12 + j, 12 + j, -4096.0 * (j + 1))
+    for b in range(2) if EARLY else ():
+        put(M("TA", 13 + 2 * b, 113, 16), [[-16, 8]], 1.0, -b)
+        move("TB", 12 + 2 * b, b, 1.0)
+        move("TB", 13 + 2 * b, b, -64.0)
+    asel(W("keep", 0, 256), W("ones", 0, 256), [[0, 4], [1, 64]], ALU.is_gt, 0.0, 0, 0)
+    iota(W("il", 0, 64), [[-1, 64]], 64)
+    iota(W("oc", 0, 16), [[1024, 4], [0, 4]], 0)
+    scan(W("k4", 0, 256), W("ones", 0, 256), W("ones", 0, 256), -1.0, ALU.mult, ALU.add)
+    ts(W("c16", 0, 64), W("k4", 0, 64), 16.0, ALU.mult)
+    ts(W("pi", 1, 1), W("pi", 0, 1), 15, ALU.bitwise_and)
+    ts(W("pi", 2, 1), W("pi", 1, 1), 1, ALU.logical_shift_right)
+    ts(W("pi", 3, 1), W("pi", 0, 1), 3, ALU.bitwise_and)
+    ts(W("pi", 4, 1), W("pi", 0, 1), 1, ALU.bitwise_and)
+    cp(C(ROW), W("pi", 1, 1))
+    ts(C(LOW), C(ROW), 12.0, ALU.is_lt)
+    ts(C(HIGH), C(ROW), 12.0, ALU.is_ge)
+    lin(C(ZC), C(HIGH), -4096.0)
+    lin(C(INC), C(HIGH), 4096.0, 4.5)
+    ts(C(TMP), W("pi", 2, 1), C(LOW), ALU.mult)
+    ts(C(TMP + 1), C(ROW), -11.0, ALU.add, 0.0, ALU.max)
+    tt(C(JC), C(TMP), C(TMP + 1), ALU.add)
+    ts(C(FC), W("pi", 3, 1), 4096.0, ALU.mult, NXB - ZR0 + 2048.0, ALU.add)
+    for ic in range(4):
+        lin(C(IC + ic), C(ROW), 1.0, 16.0 * ic + 0.5)
+    ts(C(TBC), W("pi", 4, 1), C(HIGH), ALU.mult, 12288.0, ALU.mult)
+    lin(C(TMP + 2), C(HIGH), 1024.0, -3 * BIG)
+    for (k, base, c) in (("N3B", "I", TMP + 2), ("DL", "I", LOW), ("DH", "I", HIGH), ("RW", "BLK", ROW), ("RH", "B12", ROW)):
+        lin(M(k), M(base), C(c))
+    lin(C(TMP + 3), C(LOW), 4.0)
+    for o in range(4):
+        lin(C(KBC + 4 + o), C(HIGH), 1024.0 * o - 2048.0)
+        ts(W("kb", 768 + 64 * o, 64), W("k4", 64 * o, 64), C(TMP + 3), ALU.mult, C(KBC + 4 + o), ALU.add)
+    for t in range(3):
+        lin(C(KBC + t), C(LOW), V * (t + 1) + 15.0 - CEN)
+        ts(W("kb", 256 * t, 256), W("kb", 768, 256), C(KBC + t), ALU.add)
+    for b in range(2):
+        ts(W("vl", 64 * b, 64), W("c16", 0, 64), C(ROW), ALU.add)
+    ts(W("wk", 0, 64), W("c16", 0, 64), C(ROW), ALU.add, XN0 - RL0 - 2048.0, ALU.add)
+    for lo in (0, 512) if EARLY else ():
+        cp(W("q16", lo, 512), W("tki", lo, 512))
+        ts(W("hi", lo, 512), W("q16", lo, 512), 1.0 / 64.0, ALU.mult, 192.0, ALU.add)
+        p = tile()
+        mms(p, [(M("TA"), W("q16", lo, 512)), (M("TB"), W("hi", lo, 512))])
+        act(W("tkt", V * rank + lo, 512), p, bias=C(TBC))
+    for r in RELAY:
+        share(*r)
+    cp(C(WF), W("wti", 0, 1))
+    cp(C(THF), W("thi", 0, 1))
+    lin(M("ZW", 0, 144), M("Z", 0, 144), C(WF))
+    lin(W("thl", 0, 64), W("ones", 0, 64), C(THF))
+    ts(W("kz", 0, 128), W("kin", 0, 128), float(V), ALU.min)
+    ts(W("wk", 64, 128), W("kin", 0, 128), -8.0, ALU.mult, 32768.0 - CEN, ALU.add)
+    ts(W("wk", 192, 128), W("kin", 0, 128), 16.0 - CEN, ALU.add)
+    tt(W("pay", 0, 128), W("wk", 64, 128), W("wk", 192, 128), ALU.min)
+    if EARLY:
+        cp(W("k16", 0, 128), W("pay", 0, 128))
+    else:
+        lin(W("d32", 256, 16), W("zt", 0, 16))
 
-    def mid_consts_g():
-        put(R("uu", 16 + 13, 2064, 16), [[-1, 16], [-16, 8]], 1.0, 0)
-        put(M("D12", 12, 116, 16), [[-16, 8]], 1.0, -12)
-        asel(M("UP"), M("BLK"), [[-1, 128]], ALU.is_gt, 0.0, 0)
-        iota(W("ic", 0, 512), [[0, 2], [-16, 4], [0, 64]], 0)
+    def own(buf, s, lo, n):
+        return W("%s_%d" % (buf, s), lo + (16 if s else 0), n)
 
-    def late_consts_g():
-        asel(R("keep", 0, V, 64), R("keep", 0, V, 64), [[0, 16]], ALU.is_ge, 0.0, -1, 0)
-        iota(W("il", 0, 256), [[0, 4], [1, 64]], -65)
-        rows = [[-16, 8], [0, 16]]
-        asel(M("LB"), M("I"), rows, ALU.not_equal, CEN, -15)
-        asel(M("LW"), M("NI"), rows, ALU.not_equal, 1.0, -12)
-        put(M("LO"), [[-16, 8], [0, 8], [-1, 2]], 1.0, -13)
-        iota(M("LF"), [[0, 8], [-1, 8], [0, 2]], 0)
-        put(M("LW"), rows, CEN, -15)
-        put(M("LO"), rows, CEN, -15)
-        asel(M("LF"), M("LF"), rows, ALU.is_equal, 0.0, -15)
-        for j in range(4):
-            put(M("PF", 12 + j, 420 - j, 16), [[-1, 3], [-16, 9]], 1.0, -10)
-            put(M("PK0", 12 + j, 276 - j, 16), [[-1, 2], [-16, 9]], 1.0, -2 * j - 2)
-        put(M("LF"), rows, 1.0, -10)
-        for r0 in (0, 13):
-            put(M("ZK0", 15, 273, 16), [[-1, 2], [-16, 9]], 1.0, -r0)
-        for cc in (13, 14):
-            for k in ("LO", "LF"):
-                a = M(k, cc, 128 - cc, 16)
-                asel(a, a, [[0, 8]], ALU.is_ge, 0.0, -1, 0)
+    def kid(buf, s, b, lo, n):
+        end = 16 + V * min(lo // V + 2, s + 1)
+        return G("%s_%d" % (buf, s), 0, end, *(("kl%d" % b, lo // 16) if s else ("kz", 64 * b + lo // 16)), n // 16)
 
-    def ga(src, lo, n, win):
-        act(W("ta", lo, n), G(src, 0, 16 + win, "kl0", lo // 16, n // 16))
-
-    def gb(src, lo, n, win):
-        tt(W("tb", lo, n), G(src, 0, 16 + win, "kl1", lo // 16, n // 16), W("ta", lo, n), ALU.max)
-
-    def p1b(c, win, cut=False):
-        b = W("ps%d" % (c % 2), 0, 512)
-        mms(b, [(M("I2"), W("ar", 16 + 512 * c, 512))])
-        for (lo, n) in (((0, 256), (256, 256)) if cut else ((0, 512),)):
-            gb("ar", 512 * c + lo, n, win)
-        return lambda: tt(W("qq", 16 + 512 * c, 512), W("tb", 512 * c, 512), b, ALU.max)
-
-    def p1r(c):
-        b = W("ps%d" % (2 + c % 2), 0, 512)
-        mms(b, [(M("NI"), W("ar", 16 + 512 * c, 512)), (M("I"), W("tb", 512 * c, 512))])
-        act(W("ta", 512 * c, 512), b, ACT.Relu, bias=-2.0)
-
-    def p1s(c):
-        b = W("ps%d" % (4 + 2 * (c % 2)), 0, 512)
-        mms(b, [(M("I"), W("ar", 16 + 512 * c, 512)), (M("I"), W("ta", 512 * c, 512))])
-        act(W("qq", 16 + 512 * c, 512), b, bias=2.0)
-
-    def p2c(lo, n, e):
-        b, x = bank(n), W("ar", 16 + lo, n)
-        mms(b, [(M("I"), x), (M("I"), W("tb", lo, n))])
-        if e == "s":
-            act(x, b, bias=-1.25, scale=0.5)
+    def pass1(s, lo, n=512):
+        first = act(W("ta", lo, n), kid("x", s, 0, lo, n))
+        tt(W("tb", lo, n), kid("x", s, 1, lo, n), W("ta", lo, n), ALU.max)
+        x, p = own("x", s, lo, n), tile(n)
+        if lo // 256 in RELU[s]:
+            mms(p, [(M("NI"), x), (M("I"), W("tb", lo, n))])
+            act(W("ta", lo, n), p, ACT.Relu, bias=-2.0)
+            p = tile(n)
+            mms(p, [(M("I"), x), (M("I"), W("ta", lo, n))])
+            act(own("q", s, lo, n), p, bias=2.0)
         else:
-            ts(x, b, 0.5, ALU.mult, -1.25, ALU.add)
+            mms(p, [(M("I2"), x)] if s else [(M("I"), x), (M("C2"), W("ones", 0, n))], after=[first])
+            tt(own("q", s, lo, n), W("tb", lo, n), p, ALU.max)
 
-    def kf_half(t, hf):
-        b = W("ps%d" % (5 + hf), 0, 512)
-        mm(b, M("D12"), W("vi", 512 * hf, 512), True, False)
-        for kid in range(2):
-            for r in range(16):
-                mm(R(b[1][0][0], r, 512, 16), W("uu", 16 + 128 * r - kid, 128), W("k16", 64 * kid + 32 * hf, 32),
-                   False, kid == 1 and r == 15)
-        return lambda: act(W("dw", 256 + 512 * hf, 512), b, bias=C(KFB + t))
+    def pass2(s, lo, n, out, how):
+        act(W("tc", lo, n), kid("q", s, 0, lo, n))
+        tt(W("td", lo, n), kid("q", s, 1, lo, n), W("tc", lo, n), ALU.max)
+        p, k = tile(n), "I63" if how == "v" else "I"
+        mms(p, [(M(k), own("x", s, lo, n)), (M(k), W("td", lo, n))])
+        if how == "v":
+            ts(out, p, MAGIC - (127.0 if s else 1.0), ALU.add, -MAGIC, ALU.add)
+        elif how == "s":
+            act(out, p, bias=-1.25, scale=0.5)
+        else:
+            act(W("tc", lo, n), p, bias=-1.25 if s else 126.75, scale=0.5)
+            ts(out, W("tc", lo, n), -128.0, ALU.add)
 
-    def wrap16(out, k, src, lo, n=V, first=None):
-        prs = [] if first is None else [first]
-        mms(out, prs + [(M(k, 15 - r), R(src, lo + r, lo + n, 16)) for r in range(16)])
-
-    def wrap4(out, k, src):
-        mms(out, [(M(k, 12 - 4 * kk), R(src, kk, 256, 4)) for kk in range(4)])
-
-    ga("ar", 0, 256, V)
-    ga("ar", 256, 256, V)
-    ga("ar", 512, 512, V)
-    small_consts()
-    act(W("uu", 0, V), W("ones", 0, V), scale=0.0)
-    act(W("uu", V, V), W("ones", 0, V), scale=0.0)
-    act(W("uu", 2048, 16), W("ones", 0, 16), scale=0.0)
-    f0 = p1b(0, V, True)
-    f1 = p1b(1, V)
-    mms(W("ps6", 0, 1), [(M("BLK"), W("wb", 0, 1))])
-    f0()
-    f1()
-    table_tk(0)
-    others = [o for o in range(N) if o != rank]
+    for (lo, n) in FIRST:
+        pass1(0, lo, n)
 
     for t in range(3):
         S = V * (t + 1)
         B0 = S - V
-        nb = 16 + B0
-        c0, c1 = 2 * t, 2 * t + 1
-        old = list(range(2 * t))
-
-        def o2a(i):
-            if i < len(old):
-                ga("qq", 512 * i, 512, S)
-
-        def o2b(i):
-            if i < len(old):
-                gb("qq", 512 * i, 512, S)
-
-        def o2c(i):
-            if i < len(old):
-                p2c(512 * i, 512, "s")
-
-        for (lo, n) in PIECES:
-            ga("qq", B0 + lo, n, S)
-        if t == 0:
-            table_tk(1)
-            share(*RELAY[0])
-            weave(others[0], "g")
-            mid_consts_g()
-            share(*RELAY[1])
-            share(*RELAY[2])
-        else:
-            ts(W("kb", 0, 256), R("vi", 0, V, 4), float(2048 - V * rank + S + 15) - CEN, ALU.add)
-        gb("qq", B0, 256, S)
-        if t == 0:
-            ts(C(HC), W("ps6", 0, 1), -128.0, ALU.mult)
-        gb("qq", B0 + 256, 512, S)
-        p2c(B0, 256, "s")
-        gb("qq", B0 + 768, 256, S)
-        p2c(B0 + 256, 512, "s")
-        p2c(B0 + 768, 256, "v")
-        wrap16(W("ps6", 0, 64), "ZW", "ar", nb)
-        if t == 0:
-            weave(others[1], "s")
-            act(W("keep", 0, V), W("ones", 0, V))
-            late_consts_g()
-            more_consts()
-            ts(W("thl", 0, 64), W("ones", 0, 64), C(THF), ALU.mult)
-            weave(others[2], "v")
-        else:
-            ts(W("bt", XN0, V), W("ar", nb, V), -128.0, ALU.add)
-        o2a(0)
-        ts(W("c1", 0, 64), W("ps6", 0, 64), C(HC), ALU.add)
-        if t == 0:
-            cp(W("bt", 4096, 368), W("bt", 0, 368))
+        nxt = "x_%d" % (t + 1)
+        for i, (lo, n) in enumerate(PIECES):
+            pass2(t, B0 + lo, n, W("bt", XN0 + lo, n), "v" if i in NEW_V else "sv")
+        for lo in range(0, B0, OLD):
+            pass2(t, lo, OLD, own("x", t + 1, lo, OLD), "s")
+        p = tile(64)
+        mms(p, wrap16("ZW", "bt", XN0))
+        ts(W("c1", 0, 64), p, 31.0 * t, ALU.add)
         ts(W("c1", 64, 64), W("c1", 0, 64), 4095, ALU.bitwise_and)
-        for m in (0, 1, 2, 3):
-            ts(W("offl", 64 * m, 64), W("c1", 64, 64), float(97 * m + 31 * t), ALU.add)
-
-        def dist_v(m, lo, n):
-            tt(W("dd", V * m + lo, n), G("bt", 0, RCW, "offl", 64 * m + lo // 16, n // 16), W("ar", nb + lo, n), ALU.subtract)
-
-        def dist_abs(m, lo, n):
-            act(W("da", V * m + lo, n), W("dd", V * m + lo, n), ACT.Abs, bias=128.0)
-
-        def near(m, b):
-            wrap16(W(b, 0, 64), "ZN", "da", V * m, V, (M("IB"), W("thl", 0, 64)))
-
-        def score(m, b):
-            tt(W("sc", 64 * m, 64), W("val", 64 * m, 64), W(b, 0, 64), ALU.min)
-
-        act(W("dd", 0, V), G("bt", 0, RCW, "offl", 0, 64))
-        kf = [kf_half(t, 0)]
-        dist_v(1, 0, V)
-        bs = [bank(), bank()]
-        for hf in range(2):
-            mms(bs[hf], [(M("NI"), W("ar", nb + 512 * hf, 512)), (M("I"), W("dd", 512 * hf, 512))])
-        dist_abs(1, 0, V)
-        near(1, "ps3")
-        dist_v(2, 0, V)
-        for hf in range(2):
-            act(W("da", 512 * hf, 512), bs[hf], ACT.Abs, bias=128.0)
-        near(0, "ps4")
-        dist_v(3, 0, 512)
-        dist_abs(2, 0, V)
-        dist_v(3, 512, 512)
-        for k in range(4):
-            ts(W("val", 64 * k, 64), W("c1", 64, 64), 2.0, ALU.mult, float(2 * (8192 * (4 - k) + 97 * k + 31 * t) + 1), ALU.add)
-        score(1, "ps3")
-        near(2, "ps3")
-        dist_abs(3, 0, 512)
-        dist_abs(3, 512, 512)
-        score(0, "ps4")
-        near(3, "ps4")
-        kf[0]()
-        o2a(1)
-        if t == 0:
-            act(M("UN"), M("UP"), scale=-1.0)
-            ts(W("kb", 0, 256), R("vi", 0, V, 4), float(2048 - V * rank + S + 15) - CEN, ALU.add)
-        tt(W("sc", 256, 64), W("sc", 0, 64), W("sc", 64, 64), ALU.max)
-        if t == 0:
-            ts(W("bt", XN0, V), W("ar", nb, V), -128.0, ALU.add)
-        o2b(0)
-        ts(W("sc", 320, 64), W("sc", 256, 64), 0.0, ALU.max)
-        score(2, "ps3")
-        if t == 0:
-            ts(W("vc", 0, 64), R("vi", 0, V, 16), C(ROW), ALU.add, float(256 + 2048 - V * rank), ALU.add)
-        score(3, "ps4")
-        tt(W("sc", 384, 64), W("sc", 320, 64), W("sc", 128, 64), ALU.max)
-        o2c(0)
-        o2a(2)
-        tt(W("bi", 0, 64), W("sc", 384, 64), W("sc", 192, 64), ALU.max)
-        if t == 0:
-            ts(W("vc", 64, 64), R("vi", 0, V, 16), C(ROW), ALU.add, float(XN0 + 2048 - V * rank), ALU.add)
-        ts(W("bi", 128, 64), W("bi", 0, 64), 7, ALU.bitwise_and)
-        ts(W("bi", 64, 64), W("bi", 0, 64), 1, ALU.logical_shift_right, 4095, ALU.bitwise_and)
+        for m in range(4):
+            ts(W("offl", 64 * m, 64), W("c1", 64, 64), 97.0 * m, ALU.add)
+        cp(W("c0", 0, 64), W("c1", 64, 64))
+        for m in range(4):
+            act(W("val", 64 * m, 64), W("c0", 0, 64), bias=float(2 * (8192 * (4 - m) + 97 * m) + 1), scale=2.0)
+        for m in range(4):
+            how = DIST[t][m]
+            for lo in (0, 512):
+                root, x = G("bt", 0, RCW, "offl", 64 * m + lo // 16, 32), W("bt", XN0 + lo, 512)
+                d, a = W("dd", V * m + lo, 512), W("da", V * m + lo, 512)
+                if how == "s":
+                    act(d, root)
+                    p = tile()
+                    mms(p, [(M("NI"), x), (M("I"), d)])
+                    act(a, p, ACT.Abs)
+                else:
+                    tt(d, root, x, ALU.subtract)
+                    if how == "vs":
+                        act(a, d, ACT.Abs)
+                    else:
+                        ts(a, d, 0.0, ALU.max)
+            p = tile(64)
+            pairs = wrap16("ZP", "dd", V * m) + wrap16("ZM", "da", V * m) if how == "v" else wrap16("ZN", "da", V * m)
+            mms(p, [(M("IB"), W("thl", 0, 64))] + pairs)
+            tt(W(p[0], 64, 64) if m else W("sc", 0, 64), W("val", 64 * m, 64), p, ALU.min)
+            if m:
+                tt(W("sc", 64 * m, 64) if m < 3 else W("bi", 0, 64), W("sc", 64 * m - 64, 64), W(p[0], 64, 64), ALU.max)
+        ts(W("bi", 64, 64), W("bi", 0, 64), 7, ALU.bitwise_and)
         for o in range(4):
-            ts(W("ask", 64 * o, 64), W("bi", 128, 64), float(2 * o + 1), ALU.is_equal)
-        ts(W("bi", 192, 64), W("bi", 64, 64), 4097.0, ALU.mult)
+            ts(W("ask", 64 * o, 64), W("bi", 64, 64), float(2 * o + 1), ALU.is_equal)
         scan(W("cs", 0, 256), W("keep", 0, 256), W("ask", 0, 256), 0.0, ALU.mult, ALU.add)
-        ts(W("bi", 256, 64), W("bi", 192, 64), 2, ALU.logical_shift_right, 4095, ALU.bitwise_and)
-        ts(W("ra16", 256, 64), W("bi", 128, 64), 32.0, ALU.mult, 32.0, ALU.add)
-        cp(W("ls", 0, 64), W("bi", 256, 64))
-        if t == 0:
-            ms(W("bt", RCW, 16), 0.0)
-            ms(W("tkv", V, 16), 0.0)
-            ms(W("dw", 1280, 16), 0.0)
-        mms(W("ps5", 0, 256), [(M("I65"), W("ones", 0, 256)), (M("UN"), W("ask", 0, 256)), (M("BLK"), W("cs", 0, 256))])
-        act(W("tkv", 0, 512), G("tkf", 0, 4096, "ls", 0, 32))
-        tt(W("ra16", 0, 256), W("ask", 0, 256), W("ps5", 0, 256), ALU.mult)
-        for hf in range(2):
-            b = "ps%d" % (3 + hf)
-            mm(W(b, 0, 512), M("I"), W("ic", 0, 512), True, False)
-            for i in range(8):
-                mm(W(b, 64 * i, 64), M("BLK"), W("cs", 64 * (2 * hf + i // 4), 64), False, i == 7)
-            if hf == 0:
-                mms(W("ps7", 0, 64), [(M("I"), W("ra16", 64 * o, 64)) for o in range(4)])
-                mms(W("ps7", 64, 64), [(M("I"), W("ra16", 64 * o, 64)) for o in range(5)])
-        kf.append(kf_half(t, 1))
-        for hf in range(2):
-            act(W("sg", 512 * hf, 512), W("ps%d" % (3 + hf), 0, 512), ACT.Sign, bias=C(ROWH), scale=-1.0)
-        act(W("rs", 0, 256), W("ps5", 0, 256))
-        o2b(1)
-        act(W("tkv", 512, 512), G("tkf", 0, 4096, "ls", 32, 32))
-        kf[1]()
-        ts(W("ra", 0, 64), W("ps7", 0, 64), 0.0, ALU.is_ge, BIG, ALU.mult)
-        tt(W("ra", 64, 64), W("ra", 0, 64), W("ps7", 64, 64), ALU.max)
-        tt(W("ra", 128, 64), W("ra", 0, 64), W("bi", 64, 64), ALU.max)
-        scan(W("sn", 0, V), W("keep", 0, V), W("sg", 0, V), 0.0, ALU.mult, ALU.add)
-        tt(W("ra", 192, 128), W("ra", 64, 128), W("vc", 0, 128), ALU.min)
-        ts(W("ls", 256, 16), R("sn", 62, V, 64), 0.5, ALU.mult, 31.5, ALU.add)
-        cp(W("ls", 64, 128), W("ra", 192, 128))
+        ts(W("bi", 128, 64), W("bi", 0, 64), 3, ALU.logical_shift_right, 1023, ALU.bitwise_and)
+        ts(W("ob", 0, 64), W("bi", 64, 64), 512.0, ALU.mult, -2560.0, ALU.add)
+        tt(W("tcc", 0, 64), W("bi", 128, 64), W("ob", 0, 64), ALU.add)
+        if EARLY:
+            ts(W("ls", 32, 64), W("tcc", 0, 64), 2048.0, ALU.add)
+        p = tile(256)
+        mms(p, [(M("BLK"), W("cs", 0, 256))])
+        for ic in range(4):
+            act(W("sg", 256 * ic, 256), p, ACT.Sign, bias=C(IC + ic), scale=-1.0)
+            scan(W("sn", 256 * ic, 256), W("keep", 0, 256), W("sg", 256 * ic, 256), 0.0, ALU.mult, ALU.add)
+        p = tile(256)
+        mms(p, [(M("UN"), W("ask", 0, 256)), (M("BLK"), W("cs", 0, 256))])
+        act(W("ra", 0, 256), p, ACT.Relu, bias=65.0 - BIG, scale=-1.0)
         for o in range(4):
-            tt(W("c2", 64 * o, 64), G("rs", 64 * o, 64 * o + 64, "ls", 256 + 4 * o, 4), W("il", 64 * o, 64), ALU.is_le)
-        wrap16(W("ps6", 0, 16), "Z", "c2", 0, 256)
-        ts(W("ra", 320, 16), R("sn", 62, V, 64), 8.0, ALU.mult, 504.0, ALU.add)
-        act(W("sel", 0, 512), G("bt", 0, NXB, "ls", 128, 32))
-        if OLDK_ON[t] == "v":
-            act(W("sel", 512, 512), G("bt", 0, NXB, "ls", 160, 32))
-        o2c(1)
-        o2b(2)
-        o2a(3)
-        tt(W("ra", 336, 16), W("ra", 320, 16), W("ps6", 0, 16), ALU.add)
-        cp(W("ls", 272, 16), W("ra", 336, 16))
-        (act if OLDK_ON[t] == "s" else cp)(W("rec", 256, 256), G("dw", 256, 1296, "ls", 272, 16))
-        if OLDK_ON[t] == "s":
-            act(W("sel", 512, 512), G("bt", 0, NXB, "ls", 160, 32))
-        tt(W("rec", 0, 256), G("tkv", 0, 1040, "ls", 272, 16), W("rec", 256, 256), ALU.add)
-        ts(W("r16", 0, 256), W("rec", 0, 256), C(CENC), ALU.add)
-        act(W("c2", 0, 256), W("rec", 0, 256), ACT.Relu, bias=1.0, scale=-1.0)
-        act(W("de", 0, 256), W("rec", 0, 256), bias=4.5 * BIG, scale=-BIG)
-        wrap4(W("ps3", 0, 64), "PF", "r16")
-        wrap4(W("ps3", 64, 64), "PO", "r16")
-        wrap4(W("ps3", 128, 64), "PV", "r16")
-        mms(W("ps5", 0, 256), [(M("LW"), W("r16", 0, 256))])
-        mms(W("ps6", 0, 256), [(M("LF"), W("r16", 0, 256))])
-        mms(W("ps5", 256, 256), [(M("I"), W("kb", 0, 256)), (M("LB"), W("r16", 0, 256)), (M("NB"), W("c2", 0, 256))])
-        mms(W("ps4", 0, 256), [(M("LO"), W("r16", 0, 256))])
-        ub = [bank(), bank()]
-        for hf in range(2):
-            mms(ub[hf], [(M("I"), W("bt", XN0 + 512 * hf, 512)), (M("I"), W("sel", 512 * hf, 512))])
-        act(W("de", 256, 256), W("ps6", 0, 256), ACT.Abs, scale=BIG)
-        act(W("ps7", 256, 256), W("de", 256, 256))
-        for hf in range(2):
-            act(W("ar", nb + 512 * hf, 512), ub[hf], bias=127.75, scale=0.5)
-        o2b(3)
-        sh = CEN - 4.0 - B0
-        ts(W("fl", 0, 64), W("ps3", 0, 64), C(JC), ALU.subtract)
-        ts(W("fl", 64, 64), W("ps3", 64, 64), C(XOC), ALU.add, 1040.0 + 2048.0 - sh, ALU.add)
-        tt(W("fl", 128, 64), W("fl", 0, 64), W("ps3", 0, 64), ALU.mult)
-        if t == 0:
-            ts(W("de", 1024, 256), W("ps5", 0, 256), 16.0, ALU.is_lt, 1024.0, ALU.mult)
+            ts(W("ls", 4 * o, 4), R("sn", 64 * o + 62, V, 256), 0.5, ALU.mult, 31.5, ALU.add)
+        for o in range(4):
+            hit = tt(W("mask", 64 * o, 64), G("ra", 64 * o, 64 * o + 64, "ls", 4 * o, 4), W("il", 0, 64), ALU.is_equal)
+        mask, cg = W("mask", 0, 256), W("cg", 0, 256)
+        tree, old0, old1 = [W("pr", 256 * i, 256) for i in range(3)]
+        tt(tree, G("bi", 128, 192, "ls", 0, 16), mask, ALU.mult)
+        act(cg, G("c16", 0, 64, "ls", 0, 16))
+        tt(old0, G("pay", 0, 64, "ls", 0, 16), mask, ALU.mult)
+        tt(old1, G("pay", 64, 128, "ls", 0, 16), mask, ALU.mult)
+        p = tile(16)
+        mms(p, [(M("I"), W("oc", 0, 16))] + wrap16("Z", "pr", 0, 256))
+        cp(W("ls", 16, 16), p)
+        q = W("r16", 0, 256)
+        cp(q, G("tkt", 0, 4096, "ls", 16, 16))
+        inv = W("inv", 0, 64)
+        p = tile(64)
+        mms(p, [(M("I"), W("ra", 64 * o, 64)) for o in range(4)])
+        act(inv, p, ACT.Relu, bias=1.0, scale=-1.0)
+        p = tile(128)
+        mms(W(p[0], 0, 64), [(M("I"), W("tcc", 0, 64)), (M("BI"), inv)])
+        if EARLY:
+            mms(W(p[0], 64, 64), [(M("N4"), W("ra", 64 * o, 64)) for o in range(4)] + [(M("I4"), W("ob", 0, 64))])
         else:
-            tt(W("de", 512, 256), W("de", 0, 256), W("ps5", 0, 256), ALU.max)
-        ts(W("fl", 192, 64), W("fl", 128, 64), 0.0, ALU.is_equal, -65536.0, ALU.mult)
-        if t == 0:
-            tt(W("de", 1280, 256), W("de", 1024, 256), W("ps5", 0, 256), ALU.add)
+            mms(W(p[0], 64, 64), [(M("NI"), W("ra", 64 * o, 64)) for o in range(4)] + [(M("I4"), W("ob", 0, 64)), (M("BI"), inv)])
+        tt(W("wk", 448, 64), W("wk", 0, 64), W(p[0], 0, 64), ALU.min)
+        ts(W("ls", 96, 64), W("wk", 448, 64), 2048.0, ALU.add)
+        if EARLY:
+            ts(W("rb", 0, 64), W(p[0], 64, 64), 768.0 + S + 15.0 - CEN, ALU.add)
         else:
-            tt(W("de", 768, 256), W("de", 512, 256), W("ps5", 256, 256), ALU.min)
-        tt(W("fl", 256, 64), W("fl", 192, 64), W("fl", 64, 64), ALU.add)
+            ts(W("ls", 32, 64), W(p[0], 64, 64), 192.0, ALU.add, 256.0, ALU.min)
+            for b in range(2):
+                tt(W("k16", 64 * b, 64), W("pay", 64 * b, 64), inv, ALU.mult)
+        for lo in (0, 512):
+            root, x, out = G("bt", RL0, NXB, "ls", 96 + lo // 16, 32), W("bt", XN0 + lo, 512), W(nxt, 16 + B0 + lo, 512)
+            if HALVE[t] == "s":
+                act(W("sel", lo, 512), root)
+                p = tile()
+                mms(p, [(M("I"), x), (M("I"), W("sel", lo, 512))])
+                act(out, p, bias=127.75, scale=0.5)
+            else:
+                tt(W("sel", lo, 512), root, x, ALU.add)
+                ts(out, W("sel", lo, 512), 0.5, ALU.mult, 127.75, ALU.add)
+        if EARLY:
+            for lo in (0, 512):
+                act(W("rs", lo, 512), G("tkt", 0, 4096, "ls", 32 + lo // 16, 32))
+            p = tile(128)
+            for b in range(2):
+                for i in range(0, 16, 4):
+                    mms(W(p[0], 64 * b, 64), wrap16("ZK%d" % b, "rs", 0)[i:i + 4], i == 0, i == 12)
+            rq = W("rq", 0, 128)
+            inner, none, wrap = [W("rm", 128 * i, 128) for i in range(3)]
+            ts(rq, p, -12288.0, ALU.add)
+            ts(inner, rq, 4.5, ALU.is_lt)
+            ts(none, rq, 0.0, ALU.is_equal)
+            back = [(M("I"), W("vl", 0, 128)), (M("NI"), rq)]
+            if t == 0:
+                p = tile(128)
+                mms(p, back)
+                ts(wrap, p, -4.0, ALU.is_lt)
+                back = back + [(M("IK"), wrap)]
+            p = tile(128)
+            mms(p, back + [(M("BI"), inner)])
+            act(W("de", 512, 128), p, bias=B0 + 20.0 - CEN)
+            p = tile(128)
+            mms(p, [(M("I"), rq), (M("NBI"), none)], True, False)
+            for b in range(2):
+                mms(W(p[0], 64 * b, 64), [(M("I"), W("rb", 0, 64)), (M("NBI"), inv)], False, b == 1)
+            tt(W("de", 640, 128), W("de", 512, 128), p, ALU.min)
+            p = tile(128)
+            mms(p, [(M("NBI"), W("ones", 0, 128)), (M("I"), W("k16", 0, 128))], True, False, [hit])
+            for b in range(2):
+                mms(W(p[0], 64 * b, 64), [(M("BI"), inv)], False, b == 1)
+            tt(W("rd", 0, 128), W("de", 640, 128), p, ALU.max)
+            for b in range(2):
+                ts(W("kl%d" % b, 64 * t, 64), W("rd", 64 * b, 64), CEN, ALU.add)
+        inner, none, foot, wrap = [W("mk", 256 * i, 256) for i in range(4)]
+        ts(inner, q, C(INC), ALU.is_lt)
+        ts(none, q, C(ZC), ALU.is_equal)
+        p = tile(256)
+        mms(p, [(M("RF"), q)])
+        ts(foot, p, C(JC), ALU.is_equal)
+        back = [(M("I"), cg), (M("RW"), mask), (M("NI"), q)]
         if t == 0:
-            tt(W("de", 512, 256), W("de", 1280, 256), W("de", 0, 256), ALU.max)
-        else:
-            tt(W("de", 1280, 256), W("de", 768, 256), W("ps7", 256, 256), ALU.min)
-        tt(W("fl", 320, 64), W("fl", 256, 64), W("ps3", 128, 64), ALU.max)
-        tt(W("ps6", 256, 256), W("ps4", 0, 256), W("de", 256, 256), ALU.subtract)
-        ts(W("ls", 192, 64), W("fl", 320, 64), sh, ALU.add)
-        o2c(2)
-        o2c(3)
-        for c in old[:EARLY]:
-            ga("ar", 512 * c, 512, S)
-        for hf in range(2):
-            act(W("ar", 16 + S + 512 * hf, 512), G("bt", RCW, NXB + 16384, "ls", 192 + 32 * hf, 32), bias=128.0)
-        if t == 0:
-            tt(W("de", 768, 256), W("de", 512, 256), W("ps5", 256, 256), ALU.min)
-            ts(W("thl", 0, 64), W("ps3", 0, 64), 0.0, ALU.is_gt, C(THF), ALU.mult)
-            tt(W("de", 1280, 256), W("de", 768, 256), W("ps7", 256, 256), ALU.min)
-        if t == 1:
-            ts(W("thl", 0, 64), W("ps3", 0, 64), 0.0, ALU.is_gt, C(THF), ALU.mult)
-        tt(W("dw", 0, 256), W("de", 1280, 256), W("ps6", 256, 256), ALU.max)
-        ts(W("d16", 0, 256), W("dw", 0, 256), 0.0, ALU.max, -CEN, ALU.add)
-        wrap4(W("ps4", 0, 64), "PK0", "d16")
-        wrap4(W("ps4", 64, 64), "PK1", "d16")
-        for c in old[EARLY:]:
-            ga("ar", 512 * c, 512, S)
-        ts(W("dv", 0, 512), G("dw", 0, 1280, "ls", 64, 32), 0.0, ALU.max, -CEN, ALU.add)
-        ts(W("kl0", 64 * t + 64, 64), W("ps4", 0, 64), CEN, ALU.add)
-        ts(W("kl1", 64 * t + 64, 64), W("ps4", 64, 64), CEN, ALU.add)
-        ts(W("dv", 512, 512), G("dw", 0, 1280, "ls", 96, 32), 0.0, ALU.max, -CEN, ALU.add)
+            p = tile(256)
+            mms(p, back)
+            ts(wrap, p, -4.0, ALU.is_lt)
+            back = back + [(M("IK"), wrap)]
+        p = tile(256)
+        mms(p, back[:2], True, False)
+        mms(p, back[2:] + [(M("BI"), inner)], False, True)
+        act(W("de", 0, 256), p, bias=B0 + 20.0 - CEN)
+        p = tile(256)
+        mms(p, [(M("N2B"), W("ones", 0, 256)), (M("I"), W("kb", 256 * t, 256)), (M("BB"), mask), (M("B12"), tree)], True, False, [hit])
+        mms(p, [(M("DL"), q), (M("NBI"), none)], False, False)
+        mms(p, [(M("NBI"), foot)], False, True)
+        tt(W("de", 256, 256), W("de", 0, 256), p, ALU.min)
+        p = tile(256)
+        mms(p, [(M("N3B"), W("ones", 0, 256)), (M("BB"), mask), (M("DH"), cg), (M("RH"), mask)], True, False, [hit])
+        mms(p, [(M("LO0"), old0)], False, False)
+        mms(p, [(M("LO1"), old1)], False, False)
+        mms(p, [(M("BI"), foot)], False, True)
+        tt(W("d16", 0, 256), W("de", 256, 256), p, ALU.max)
+        if not EARLY:
+            tt(W("d32", 0, 256), W("de", 256, 256), p, ALU.max)
+        p = tile(64)
+        mms(p, wrap4("PG", "mk", 512), True, False)
+        mms(p, wrap4("PFI", "d16"), False, True)
+        ts(W("ls", 160, 64), p, C(FC), ALU.add)
         if t < 2:
-            cp(W("k16", 0, 128), W("ps4", 0, 128))
-        wrap16(W("ps3", 0, 64), "ZK0", "dv", 0)
-        wrap16(W("ps6", 0, 64), "ZK1", "dv", 0)
-        E = S + V
-        ga("ar", S, 512, E)
-        ga("ar", S + 512, 512, E)
-        seq = [(c, S) for c in old] + [(c1 + 1, E), (c1 + 2, E), (c0, E), (c1, E)]
-        nr = RELU_CHUNKS[t]
-        gb("ar", 512 * seq[0][0], 512, seq[0][1])
-        ts(W("kl0", 64 * t, 64), W("ps3", 0, 64), 2 * CEN, ALU.add)
-        ts(W("kl1", 64 * t, 64), W("ps6", 0, 64), 2 * CEN, ALU.add)
-        ga("ar", B0, 512, E)
-        ga("ar", B0 + 512, 512, E)
-        for (c, w) in seq[1:nr]:
-            gb("ar", 512 * c, 512, w)
-        side = []
-        for (c, w) in seq[:nr]:
-            side.append((p1r, c))
-        for (c, w) in seq[:nr]:
-            side.insert(min(len(side), side.index((p1r, c)) + 2), (p1s, c))
-        pend = None
-        rest = seq[nr:]
-        for i, (c, w) in enumerate(rest):
-            f = p1b(c, w)
-            if pend is not None:
-                pend()
-            pend = f
-            k = -(-len(side) // max(1, len(rest) - 1 - i))
-            for (fn, cc) in side[:k]:
-                fn(cc)
-            side = side[k:]
-        pend()
+            ts(W("thl", 0, 64), p, -20000.0, ALU.is_gt, C(THF), ALU.mult)
+        for lo in (0, 512):
+            out, src = W(nxt, 16 + S + lo, 512), G("bt", ZR0, NXB + 16384, "ls", 160 + lo // 16, 32)
+            if FILL[t][lo // 512] == "s":
+                act(out, src, bias=128.0)
+            else:
+                ts(out, src, 128.0, ALU.add)
+        p = tile(128)
+        for b in range(2):
+            mms(W(p[0], 64 * b, 64), wrap4("PK%d" % b, "d16"))
+        for b in range(2):
+            ts(W("kl%d" % b, 64 * t + 64, 64), W(p[0], 64 * b, 64), CEN, ALU.add)
+        if t < 2:
+            ts(W("pay", 0, 128), p, -CEN, ALU.max)
+            if EARLY:
+                ts(W("k16", 0, 128), p, -CEN, ALU.max)
+        if not EARLY:
+            for lo in (0, 512):
+                ts(W("q16", lo, 512), G("d32", 0, 272, "ls", 32 + lo // 16, 32), -CEN, ALU.max)
+            for b in range(2):
+                p = tile(64)
+                mms(p, [(M("I"), W("k16", 64 * b, 64))] + wrap16("ZK%d" % b, "q16", 0))
+                ts(W("kl%d" % b, 64 * t, 64), p, CEN, ALU.add)
+        for lo in range(0, B0, OLD):
+            pass1(t + 1, lo, OLD)
+        for (lo, n) in TAIL:
+            pass1(t + 1, B0 + lo, n)
 
-    def last(c):
-        lo = 512 * c
-        b, x, m = bank(), W("ar", 16 + lo, 512), W("tb", lo, 512)
-        if c in LAST_V:
-            mms(b, [(M("I63"), x), (M("I63"), m)])
-            ts(W("yo", lo, 512), b, MAGIC - 127.0, ALU.add, -MAGIC, ALU.add)
-        else:
-            mms(b, [(M("I"), x), (M("I"), m)])
-            act(W("dd", lo, 512), b, bias=-1.25, scale=0.5)
-
-    def result(c):
-        lo = 512 * c
-        if c not in LAST_V:
-            ts(W("yo", lo, 512), W("dd", lo, 512), -128.0, ALU.add)
-        if c >= 6:
-            dma("y", T.y[:, lo:lo + 512], W("yo", lo, 512))
-        elif c % 2:
-            dma("y", T.y[:, lo - 512:lo + 512], W("yo", lo - 512, V))
-
-    ga("qq", 0, 256, 4096)
-    ga("qq", 256, 256, 4096)
-    ga("qq", 512, 512, 4096)
     for c in range(8):
-        if c == 0:
-            gb("qq", 0, 256, 4096)
-            gb("qq", 256, 256, 4096)
-        elif c == 7:
-            gb("qq", 3584, 384, 4096)
-            gb("qq", 3968, 128, 4096)
-        else:
-            gb("qq", 512 * c, 512, 4096)
-        if c + 2 < 8:
-            ga("qq", 512 * (c + 2), 512, 4096)
-        if c >= 1:
-            last(c - 1)
-        if c >= 2:
-            result(c - 2)
-    result(6)
-    for (lo, n) in ((3584, 384), (3968, 128)):
-        b = bank(n)
-        mms(b, [(M("I63"), W("ar", 16 + lo, n)), (M("I63"), W("tb", lo, n))])
-        ts(W("yo", lo, n), b, MAGIC - 127.0, ALU.add, -MAGIC, ALU.add)
-        dma("y" if n > 128 else "s", T.y[:, lo:lo + n], W("yo", lo, n))
+        for (lo, n) in (((512 * c, 512),) if c < 7 else ((3584, 384), (3968, 128))):
+            pass2(3, lo, n, W("yo", lo, n), "v" if c in LAST_V else "sv")
+            if c >= 6:
+                dma("y", T.y[:, lo:lo + n], W("yo", lo, n), 256 * n)
+            elif c % 2:
+                dma("y", T.y[:, lo - 512:lo + 512], W("yo", lo - 512, V), 1 << 18)
+
+    got, extra = banks(ops, tiles)
+    where.update(got)
+    start = place(ops, extra)[0]
+    for (a, b) in extra:
+        ops[b]["dep"][a] = True
+    cnt = {e: 0 for e in Q}
+    seen = {e: {} for e in Q}
+    mark, final = {}, {}
+
+    def wait(e, sem, val):
+        if seen[e].get(sem, 0) < val:
+            Q[e].wait_ge(T.sem[sem], val)
+            seen[e][sem] = val
+
+    for i in sorted(range(len(ops)), key=lambda i: (start[i], i)):
+        o = ops[i]
+        if o["e"] is not None:
+            need = {}
+            for a in o["dep"]:
+                if o["dep"][a] and mark[a]:
+                    need[mark[a][0]] = max(need.get(mark[a][0], 0), mark[a][1])
+            for sem in need:
+                wait(o["e"], sem, need[sem])
+            call = o["fn"]()
+            if o["sem"] is None:
+                cnt[o["e"]] += 1
+                o["sem"] = ("c" + o["e"], cnt[o["e"]])
+                call.then_inc(T.sem[o["sem"][0]], 1)
+            elif o["sem"]:
+                call.then_inc(T.sem[o["sem"][0]], 16)
+        mark[i] = o["sem"]
+        if o["sem"]:
+            final[o["sem"][0]] = o["sem"][1]
     for sem in final:
         wait("g" if sem == "cg" else "y", sem, final[sem])

@@ -12,32 +12,59 @@ CEN = 2064.0
 BIG = 16384.0
 FAR = 131072.0
 MAGIC = 12582912.0
-RELAY = (("tkt", [0], "t"), ("bt", [NXB, NXB + 4096], "n"), ("bt", [NXB + 8192, NXB + 12288], "m"))
+RELAY = (("tkt", [0], "t"), ("bt", [NXB, NXB + 4096], "n"), ("bt", [NXB + 8192], "m"), ("bt", [NXB + 12288], "l"))
 
 DIST = (("s", "vs", "vs", "vs"),) * 3
-EARLY = False
-HALVE = ("s", "s", "s")
+HASH = (((0, 64),),) * 3
+GAPS = ((0, 512), (512, 512))
+EARLY = (False, False, False)
+ROOT = ((0, 256), (256, 256), (512, 256), (768, 256))
+FOLD = True
+SIGNS = "sv"
+RAW = ("v", "v", "v")
+FORM = "pppp"
 RELU = ((), (0,), (0, 2), (0, 2, 4, 6))
-LAST_V = (3, 7)
-FILL = ("ss", "ss", "ss")
-NEW_V = (0, 1, 2, 3)
-PIECES = ((0, 256), (256, 384), (640, 256), (896, 128))
+HALVE = ("s", "s", "s")
+HALF = ("s", "s", "s")
+DV = ((0, 256), (256, 256), (512, 512))
+OLDS = ((), ("ss", "ss"), ("ss", "ss", "ss", "ss"))
+LAST = ("ss", "ss", "ms", "ss", "sv", "ms", "sv", "mv")
+DEPTH = 9
+FILL = (((0, 768, "s"), (768, 256, "v")),) * 3
+ALONE = 0
+VALS = "s"
+NEW = ("ws", "ms", "ms", "ms", "ms")
+PIECES = ((0, 128), (128, 256), (384, 384), (768, 128), (896, 128))
 OLD = 512
-TAIL = ((0, 512), (512, 512), (1024, 512), (1536, 512))
+TAIL = ((1024, 256), (1280, 256), (1536, 512), (0, 512), (512, 384), (896, 128))
 FIRST = ((0, 128), (128, 384), (512, 384), (896, 128))
 WEAVE = ("v", "g", "s", "v")
+DIRECT = "ml"
+PRE = 2
 
-CYC, GATHER, HOP, PECYC = 0.9, 1.56, 90.0, 0.45
-TURNS = 4
-GIVE = {"v": 1.0, "s": 1.0, "p": 0.3, "g": 0.3, "y": 0.0}
-GRACE = {"v": 300.0, "s": 300.0, "p": 50.0, "g": 50.0, "y": 0.0}
+CYC, GATHER = 0.83, 1.56
+FUSED = 1.56
+CALL = 5.0
+HOP = 205.0
+PECYC = 0.43
+PEFIX = 10.0
+SCORE = 4
+TURNS = 2
+TRIES = 8000
+PLANS = {}
+SHAKE = 3000.0
+SLACK = 30.0
+SOME = 0.3
+SWAP = 0.0
+RULES = ((1.0, 300.0),)
+EAGER = (0.3, 20.0)
 LOAD = 2000.0
-ARRIVE = {"r": (1500.0, 900.0), "t": (10000.0, 0.0), "n": (14000.0, 0.0), "m": (16000.0, 0.0)}
+ARRIVE = {"r": (1500.0, 900.0), "t": (9000.0, 0.0), "n": (10000.0, 0.0), "m": (10000.0, 0.0), "l": (10000.0, 0.0)}
 
-DIAG = {"I": 1.0, "I2": 65.0 / 64.0, "I63": 63.0 / 128.0, "NI": -1.0, "C2": 2.0, "IB": FAR, "BI": BIG, "NBI": -BIG,
-        "N2B": -2 * BIG, "IK": 1024.0, "N4": -4.0, "I4": 0.25 if EARLY else 0.0625}
-MATS = list(DIAG) + ["N3B", "DL", "DH", "BLK", "BB", "UN", "RF", "B12", "RW", "RH", "LO0", "LO1", "TA", "TB"]
-WIDE = ["Z", "ZW", "ZN", "ZM", "ZP", "ZK0", "ZK1", "PK0", "PK1", "PFI", "PG"]
+DIAG = {"I": 1.0, "I2": 65.0 / 64.0, "I63": 63.0 / 128.0, "NI": -1.0, "IB": FAR, "BI": BIG, "NBI": -BIG, "N4B": -4 * BIG,
+        "IK": 1024.0, "I16": 0.0625, "C2": 2.0, "NW": -1020.0, "IF": 256 * FAR}
+MATS = list(DIAG) + ["BLK", "BB", "UN", "RF", "B12", "LO0", "LO1"]
+WIDE = ["Z", "ZW", "ZN", "ZK0", "ZK1", "PK0", "PK1", "PFI", "PG"]
 MOFF = {k: 128 * i for i, k in enumerate(MATS)}
 MOFF.update({k: 144 * i for i, k in enumerate(WIDE)})
 
@@ -46,28 +73,23 @@ SCRATCH = {"bt": ("sbuf", [128, NXB + 16384], "bfloat16"), "cm": ("sbuf", [128, 
 for _t, _l in (("bfloat16", (("x_0", 1040), ("x_1", 2064), ("x_2", 3088), ("x_3", 4112), ("q_0", 1040), ("q_1", 2064),
                              ("q_2", 3088), ("q_3", 4112), ("ta", 4096), ("tb", 4096), ("tc", 4096), ("td", 4096), ("dd", 4096),
                              ("da", 4096), ("yo", 4096), ("sel", V), ("ones", 512), ("zt", 384), ("t8", 128), ("thl", 64),
-                             ("ask", 256), ("keep", 256), ("cs", 256), ("cg", 256), ("c16", 64), ("oc", 16), ("hi", V), ("rs", V),
-                             ("il", 64), ("ra", 256), ("sg", V), ("sn", V), ("mask", 256), ("ob", 64), ("inv", 64), ("mk", V),
-                             ("rm", 384))),
-               ("float32", (("col", 32), ("val", 256), ("sc", 192), ("pay", 128), ("wk", 512), ("de", 768),
-                            ("c0", 64), ("tkt", 4096))),
-               ("float16", (("q16", V), ("k16", 128), ("r16", 256), ("kb", V), ("d16", 256), ("pr", 768), ("k4", 512), ("vl", 128),
-                            ("tcc", 64), ("rq", 128), ("rb", 64), ("rd", 128))),
-               ("int32", (("tki", V), ("kin", 128), ("wti", 8), ("thi", 8), ("pi", 8), ("c1", 128), ("bi", 192))),
-               ("uint16", (("kz", 128), ("kl0", 256), ("kl1", 256), ("offl", 256), ("ls", 224)))):
+                             ("ask", 256), ("keep", 256), ("cs", 256), ("oc", 16), ("il", 64), ("ra", 256), ("sg", V), ("sn", V),
+                             ("mask", 256), ("ob", 64), ("inv", 64), ("mk", V), ("rm", 384), ("got", 64), ("xb", V))),
+               ("float32", (("col", 32), ("val", 256), ("sc", 256), ("pay", 192), ("wk", 512), ("de", 768), ("c0", 64), ("d32", 272))),
+               ("float16", (("dv", V), ("k16", 128), ("r16", 256), ("kb", V), ("d16", 256), ("pr", V), ("k4", 256), ("tcc", 64),
+                            ("vl", 128), ("rq", 128), ("rb", 64))),
+               ("int32", (("tkt", 4096), ("kin", 128), ("wti", 8), ("thi", 8), ("pi", 8), ("c1", 128), ("bi", 192))),
+               ("uint16", (("kz", 128), ("kl", 512), ("offl", 256), ("ls", 224)))):
     for _k, _n in _l:
         SCRATCH[_k] = ("sbuf", [128, _n], _t)
-if not EARLY:
-    SCRATCH["tkt"] = ("sbuf", [128, 4096], "int32")
-    SCRATCH["d32"] = ("sbuf", [128, 272], "float32")
 for _b in range(8):
     SCRATCH["ps%d" % _b] = ("psum", [128, 512], "float32")
 
-SEMAPHORES = (["cv", "cs", "cp", "cg", "ar_t", "ar_n", "ar_m", "sn_r", "sn_t", "sn_n", "sn_m"] + ["ar_r%d" % i for i in range(N)]
+SEMAPHORES = (["cv", "cs", "cp", "cg", "ar_t", "ar_n", "ar_m", "sn_r", "sn_t", "sn_n", "sn_m", "ar_l", "sn_l"] + ["ar_r%d" % i for i in range(N)]
               + ["dm%d" % i for i in range(32)])
 
 
-def run(ops, pred, release, rank, choose=False):
+def run(ops, pred, release, rank, rule, choose=False):
     n = len(ops)
     succ = [[] for _ in ops]
     for b in range(n):
@@ -83,13 +105,13 @@ def run(ops, pred, release, rank, choose=False):
         if ops[b]["alt"]:
             ops[b].update(e=e, cost=ops[b]["alt"][e][0], fn=ops[b]["alt"][e][1])
         if e is not None:
-            soon, hold = {}, []
+            soon, hold, (give, grace) = {}, [], rule if e in "vs" else EAGER
             for i in order:
                 if rank[i] <= rank[b]:
                     break
                 if start[i] is None:
                     soon[i] = max([soon.get(a, start[a]) + ops[a]["cost"] + pred[i][a] for a in pred[i]] + [t, free[ops[i]["e"]]])
-                    if ops[i]["e"] == e and t + ops[b]["cost"] - soon[i] > GIVE[e] * (soon[i] - t) + GRACE[e]:
+                    if ops[i]["e"] == e and t + ops[b]["cost"] - soon[i] > give * (soon[i] - t) + grace:
                         hold.append(soon[i])
             if hold and min(hold) > t:
                 ready[b] = min(hold) + 1.0
@@ -104,32 +126,106 @@ def run(ops, pred, release, rank, choose=False):
     return start
 
 
-def place(ops, extra):
+def place(ops):
     n = len(ops)
+    pred, back = links(ops, [])
+    free = [dict(o, e=None, alt=None) for o in ops]
+    tail = [o["lat"] for o in ops]
+    best = None
+    for rule in RULES:
+        late = run(free, back, tail, [0.0] * n, rule)
+        for _ in range(TURNS):
+            start = run(ops, pred, [0.0] * n, [late[i] + ops[i]["cost"] for i in range(n)], rule, True)
+            span = max(start[i] + ops[i]["cost"] + tail[i] for i in range(n))
+            if best is None or span < best[0]:
+                best = (span, start, [o["e"] for o in ops])
+            late = run(ops, back, tail, [start[i] + ops[i]["cost"] for i in range(n)], rule)
+    for o, e in zip(ops, best[2]):
+        if o["alt"]:
+            o.update(e=e, cost=o["alt"][e][0], fn=o["alt"][e][1])
+    return best[1]
+
+
+def links(ops, extra):
     pred = [{a: ops[a]["lat"] + HOP if o["dep"][a] else 1.0 for a in o["dep"]} for o in ops]
     for (a, b) in extra:
         pred[b][a] = ops[a]["lat"] + HOP
     back = [{} for _ in ops]
-    for b in range(n):
+    for b in range(len(ops)):
         for a in pred[b]:
             back[a][b] = pred[b][a]
-    free = [dict(o, e=None, alt=None) for o in ops]
-    tail = [o["lat"] for o in ops]
-    late, best = run(free, back, tail, [0.0] * n), None
-    for _ in range(TURNS):
-        start = run(ops, pred, [0.0] * n, [late[i] + ops[i]["cost"] for i in range(n)], True)
-        span = max(start[i] + ops[i]["cost"] + tail[i] for i in range(n))
-        if best is None or span < best[0]:
-            best = (span, start, [o["e"] for o in ops])
-        late = run(ops, back, tail, [start[i] + ops[i]["cost"] for i in range(n)])
+    return pred, back
+
+
+def pack(on, cost, pred, order, release):
+    start, lines = [0.0] * len(on), {e: ([], []) for e in on}
+    for b in order:
+        t = release[b]
+        for a, d in pred[b]:
+            if start[a] + cost[a] + d > t:
+                t = start[a] + cost[a] + d
+        if on[b] is not None:
+            begin, end = lines[on[b]]
+            k = top = len(end)
+            while k and end[k - 1] > t:
+                k -= 1
+            while k < top and t + cost[b] > begin[k]:
+                t = end[k] if end[k] > t else t
+                k += 1
+            begin.insert(k, t)
+            end.insert(k, t + cost[b])
+        start[b] = t
+    return start
+
+
+def tighten(ops, extra, start, tries):
+    n = len(ops)
+    tail, zero, seed = [o["lat"] for o in ops], [0.0] * n, [1]
+    pred, back = [[list(x.items()) for x in side] for side in links(ops, extra)]
+    either = [i for i in range(n) if ops[i]["alt"]]
+
+    def draw():
+        seed[0] = (seed[0] * 1103515245 + 12345) % 2147483648
+        return seed[0] / 2147483648.0
+
+    def settle(key, on):
+        cost = [o["alt"][e][0] if o["alt"] else o["cost"] for o, e in zip(ops, on)]
+
+        def ends(s):
+            return sorted(range(n), key=lambda i: -s[i] - cost[i])
+
+        moved = True
+        while moved:
+            moved = False
+            for b in range(n):
+                for a, _ in pred[b]:
+                    if key[b] <= key[a]:
+                        key[b], moved = key[a] + 0.5, True
+        s = pack(on, cost, pred, sorted(range(n), key=lambda i: key[i]), zero)
+        s = pack(on, cost, pred, ends(pack(on, cost, back, ends(s), tail)), zero)
+        return max(a + b + c for a, b, c in zip(s, cost, tail)), s, on
+
+    now = best = settle(list(start), [o["e"] for o in ops])
+    for _ in range(tries):
+        lo = draw() * now[0]
+        hi = lo + 2000.0 + 8000.0 * draw()
+        on = list(now[2])
+        for i in either:
+            if lo <= now[1][i] < hi and draw() < SWAP:
+                on[i] = "v" if on[i] == "s" else "s"
+        new = settle([x + SHAKE * (draw() + draw() - 1.0) if lo <= x < hi and draw() < SOME else x for x in now[1]], on)
+        if new[0] <= now[0] + SLACK:
+            now = new
+        if new[0] < best[0]:
+            best = new
     for o, e in zip(ops, best[2]):
         if o["alt"]:
             o.update(e=e, cost=o["alt"][e][0], fn=o["alt"][e][1])
-    return best[1], [list(x) for x in back]
+    return best[1]
 
 
-def banks(ops, tiles):
-    start, succ = place(ops, [])
+def banks(ops, tiles, start):
+    succ = [list(x) for x in links(ops, [])[1]]
     end = [start[i] + o["cost"] + o["lat"] for i, o in enumerate(ops)]
     held, where, extra = [[] for _ in range(8)], {}, []
 
@@ -187,15 +283,22 @@ def rank_program(g, core, T, topo):
     def far_of(c):
         return [d for d in ranks if topo.die(d) != topo.die(c)]
 
+    def direct(c, tag):
+        return far_of(c) + near_of(c) if tag in DIRECT else near_of(c) + [helper[c]]
+
+    def handed(c, tag):
+        return far_of(c)
+
     if rank is None:
         for c in ranks:
             if helper[c] == core:
                 o = T.rank_of(c)
-                for (name, starts, tag) in RELAY:
-                    g.wait_ge(T.sem["ar_" + tag], count(c, near_of(c) + [core], len(starts)))
-                    send(core, far_of(c), name, [s0 + V * o for s0 in starts], tag, "ar_" + tag)
-                for (name, starts, tag) in RELAY:
-                    g.wait_ge(T.sem["sn_" + tag], count(core, far_of(c), len(starts)))
+                relay = [r for r in RELAY if r[2] not in DIRECT]
+                for (name, starts, tag) in relay:
+                    g.wait_ge(T.sem["ar_" + tag], count(c, direct(c, tag), len(starts)))
+                    send(core, handed(c, tag), name, [s0 + V * o for s0 in starts], tag, "ar_" + tag)
+                for (name, starts, tag) in relay:
+                    g.wait_ge(T.sem["sn_" + tag], count(core, handed(c, tag), len(starts)))
         return
 
     Q = {"v": g.vector, "s": g.scalar, "p": g.tensor, "g": g, "y": g.sync}
@@ -262,7 +365,9 @@ def rank_program(g, core, T, topo):
         return me
 
     def vcost(out, a, per):
-        return 50.0 + GATHER * CYC * size(a) if a[4] is not None else max(64.0, per * size(a)) * CYC
+        if a[4] is not None:
+            return 55.0 + (FUSED if per == 2.0 else GATHER) * CYC * size(a)
+        return CALL + max(64.0, per * size(a)) * CYC
 
     def ts(out, a, s1, op0, s2=None, op1=None):
         more = (op0,) if op1 is None else (op0, op1)
@@ -286,17 +391,16 @@ def rank_program(g, core, T, topo):
         return add("s", [out], [a, bias, scale], vcost(out, a, 1.0),
                    lambda: g.scalar.activation(A(out), A(a), func, bias=A(bias), scale=A(scale)))
 
-    def lin(out, a, scale=1.0, bias=0.0):
-        alt = {"v": (vcost(out, a, 0.5 if short(out, a) else 1.0),
-                     lambda: g.vector.tensor_scalar(A(out), A(a), A(scale), A(bias), ALU.mult, ALU.add)),
-               "s": (vcost(out, a, 1.0), lambda: g.scalar.activation(A(out), A(a), ACT.Identity, bias=A(bias), scale=A(scale)))}
-        return add("v", [out], [a, scale, bias], alt["v"][0], alt["v"][1], alt=alt)
+    def lin(out, a, scale=1.0, bias=0.0, on="a", relu=False):
+        how = (A(bias), 0.0, ALU.add, ALU.max) if relu else (A(scale), A(bias), ALU.mult, ALU.add)
+        alt = {"v": (vcost(out, a, 0.5 if short(out, a) else 1.0), lambda: g.vector.tensor_scalar(A(out), A(a), *how)),
+               "s": (vcost(out, a, 1.0),
+                     lambda: g.scalar.activation(A(out), A(a), ACT.Relu if relu else ACT.Identity, bias=A(bias), scale=A(scale)))}
+        e = "s" if on == "s" else "v"
+        return add(e, [out], [a, scale, bias], alt[e][0], alt[e][1], alt=alt if on == "a" else None)
 
     def asel(out, a, pat, op, fill, base, cm=1):
         return add("g", [out], [a], 170.0 + 2 * CYC * size(a), lambda: g.affine_select(A(out), A(a), pat, op, fill, base, cm))
-
-    def put(a, pat, val, base):
-        asel(a, a, pat, ALU.not_equal, val, base)
 
     def iota(out, pat, base, cm=0):
         if SCRATCH[out[0]][2] == "int32":
@@ -309,7 +413,7 @@ def rank_program(g, core, T, topo):
             for i, (lt, rhs) in enumerate(pairs):
                 last = g.tensor.matmul(A(out), A(lt), A(rhs), first and i == 0, final and i == len(pairs) - 1)
             return last
-        return add("p", [out], [x for p in pairs for x in p], sum(10.0 + PECYC * max(64, size(r)) for (_, r) in pairs), fn, 60.0, after)
+        return add("p", [out], [x for p in pairs for x in p], sum(PEFIX + PECYC * max(64, size(r)) for (_, r) in pairs), fn, 60.0, after)
 
     ndm = [0]
 
@@ -318,7 +422,7 @@ def rank_program(g, core, T, topo):
         return add(e, [out] if isinstance(out, tuple) else [], [in_], 60.0 + (nbytes / 300.0 if e == "y" else 0.0),
                    lambda: Q[e].dma_start(A(out), A(in_)), LOAD, after, ("dm%d" % (ndm[0] - 1), 16), behind)
 
-    sent = {}
+    sent, calls = {}, []
 
     def share(name, starts, tag):
         own = [s0 + V * rank for s0 in starts]
@@ -331,12 +435,13 @@ def rank_program(g, core, T, topo):
                 add(None, [W(name, starts[0] + V * o, V)], [], 0.0, None, ARRIVE[tag][0] + k * ARRIVE[tag][1], [me],
                     ("ar_r%d" % o, count(ranks[o], [c for c in ranks if c != ranks[o]], 1)))
         else:
-            to = near_of(core) + [helper[core]]
-            me = add("g", [], src, 400.0, lambda: send(core, to, name, own, tag, "ar_" + tag), sem=())
-            got = (sum(count(c, near_of(c) + [helper[c]], len(starts)) for c in near_of(core))
-                   + sum(count(helper[c], far_of(c), len(starts)) for c in far_of(core)))
+            to = direct(core, tag)
+            me = add("g", [], src, 400.0, lambda: send(core, to, name, own, tag, "ar_" + tag), sem=(), behind=list(calls))
+            got = sum(count(c, direct(c, tag), len(starts)) if core in direct(c, tag)
+                      else count(helper[c], handed(c, tag), len(starts)) for c in ranks if c != core)
             add(None, [W(name, s0 + V * o, V) for s0 in starts for o in range(N) if o != rank], [], 0.0, None, ARRIVE[tag][0], [me],
                 ("ar_" + tag, got))
+        calls.append(me)
         sent[tag] = add(None, [], [], 0.0, None, ARRIVE["r"][0] + 2000.0, [me], ("sn_" + tag, count(core, to, len(starts))))
 
     def weave(o, e):
@@ -355,23 +460,24 @@ def rank_program(g, core, T, topo):
         return [(M(k, 12 - 4 * kk), R(src, lo + kk, lo + 256, 4)) for kk in range(4)]
 
     loads = []
-    for (name, n, src) in (("kin", 64, T.k0), ("x_0", V, T.x0), ("tki", V, T.tk), ("wti", 1, T.wt), ("thi", 1, T.th)):
-        out = W("tkt", V * rank, V) if name == "tki" and not EARLY else W(name, 0, n)
-        loads.append(dma("y", out, src[:], 256 * n, behind=loads[-1:]))
+    for (name, lo, n, src) in (("kin", 0, 64, T.k0), ("x_0", 0, V, T.x0), ("tkt", V * rank, V, T.tk), ("wti", 0, 1, T.wt),
+                               ("thi", 0, 1, T.th)):
+        loads.append(dma("y", W(name, lo, n), src[:], 256 * n, behind=loads[-1:]))
     dma("s", W("bt", RL0 + V * rank, V), T.rx[:], 1 << 18, behind=[dma("s", W("kin", 64, 64), T.k1[:], 1 << 15)])
     share("bt", [RL0], "r")
     for j in range(4):
-        dma("y", W("bt", NXB + 4096 * j + V * rank, V), T.nx[:, V * j:V * j + V], 1 << 18, [sent["r"]])
+        dma("y", W("bt", NXB + 4096 * j + V * rank, V), T.nx[:, V * j:V * j + V], 1 << 18, [sent["r"]] if j >= PRE else [],
+            loads[-1:])
     for k in range(N):
         weave((rank - k) % N, WEAVE[k])
     lin(W("bt", 4096, RCW - 4096), W("bt", 0, RCW - 4096))
 
-    ROW, JC, ZC, LOW, WF, THF, FC, HIGH, IC, TMP, INC, TBC, KBC = 0, 1, 2, 3, 4, 5, 6, 7, 8, 12, 16, 17, 20
+    ROW, JC, ZC, LOW, WF, THF, FC, HIGH, IC, TMP, HC, KBC = 0, 1, 2, 3, 4, 5, 6, 7, 8, 12, 16, 20
     rows = [[-16, 8], [0, 16]]
     ms(W("zt", 0, 128), 0.0)
     ms(W("ones", 0, 512), 1.0)
     ms(W("x_0", V, 16), 0.0)
-    ms(W("q_0", V, 16), 2.0)
+    ms(W("q_0", V, 16), 0.0 if FORM[0] == "p" else 2.0)
     iota(W("pi", 0, 1), [[0, 1]], 0, 1)
     asel(M("I"), W("zt", 0, 128), [[-1, 128]], ALU.not_equal, 1.0, 0)
     asel(W("t8", 0, 128), W("ones", 0, 128), rows, ALU.is_ge, 0.0, 0)
@@ -380,21 +486,17 @@ def rank_program(g, core, T, topo):
         lin(M(k), M("I"), DIAG[k])
     for s in (1, 2, 3):
         lin(W("x_%d" % s, 0, 16), W("zt", 0, 16), 0.0, 128.0)
-        lin(W("q_%d" % s, 0, 16), W("zt", 0, 16), 0.0, 130.0)
+        lin(W("q_%d" % s, 0, 16), W("zt", 0, 16), 0.0, 128.0 if FORM[s] == "p" else 130.0)
     lin(W("bt", ZR0, 16), W("zt", 0, 16))
-    for (k, n) in (("Z", 144), ("ZK0", 432), ("PK1", 432), ("TB", 128)):
+    for (k, n) in (("Z", 144), ("ZK0", 432), ("PK1", 432)):
         lin(M(k, 0, n), W("ones", 0, n), 0.0)
-    lin(M("TA"), M("I"))
 
     def move(k, col, row, val, src="I"):
         lin(M(k, col, 113, 16), M(src, row, 113, 16), val)
 
     move("Z", 15, 0, 1.0, "BLK")
     lin(M("ZN", 0, 144), M("Z", 0, 144), -FAR)
-    if any("v" in d for d in DIST):
-        lin(M("ZM", 0, 144), M("Z", 0, 144), -2 * FAR)
-        lin(M("ZP", 0, 144), M("Z", 0, 144), FAR)
-    lin(M("BB"), M("BLK"), 2 * BIG)
+    lin(M("BB"), M("BLK"), 3 * BIG)
     asel(W("t8", 0, 128), M("BLK"), [[-1, 128]], ALU.is_gt, 0.0, 0)
     lin(W("zt", 128, 128), W("t8", 0, 128), -1.0)
     asel(M("UN"), W("zt", 128, 128), [[-1, 128]], ALU.not_equal, -BIG, 0)
@@ -403,44 +505,30 @@ def rank_program(g, core, T, topo):
     asel(W("zt", 256, 128), M("BLK"), [[0, 8], [-1, 16]], ALU.is_ge, 0.0, 11, 0)
     for b in range(2):
         asel(M("LO%d" % b), W("zt", 256, 128), [[0, 64], [1, 2]], ALU.is_equal, 0.0, -b, 0)
-    if EARLY:
-        put(M("ZK0", 15, 273, 16), [[-2, 2], [-16, 9]], 64.0, -12)
-        put(M("ZK0", 15, 273, 16), [[-2, 2], [-16, 9]], 1.0, -13)
-    else:
-        put(M("ZK0", 15, 273, 16), [[-1, 2], [-16, 9]], 1.0, 0)
+    for b in range(2):
+        move("ZK%d" % b, 15, b, 1.0)
     for j in range(4):
         for b in range(2):
             move("PK%d" % b, 12 + j, 2 * j + 2 + b, 1.0)
         move("PFI", 12 + j, 12 + j, 1.0)
         move("PG", 12 + j, 12 + j, -4096.0 * (j + 1))
-    for b in range(2) if EARLY else ():
-        put(M("TA", 13 + 2 * b, 113, 16), [[-16, 8]], 1.0, -b)
-        move("TB", 12 + 2 * b, b, 1.0)
-        move("TB", 13 + 2 * b, b, -64.0)
     asel(W("keep", 0, 256), W("ones", 0, 256), [[0, 4], [1, 64]], ALU.is_gt, 0.0, 0, 0)
     iota(W("il", 0, 64), [[-1, 64]], 64)
     iota(W("oc", 0, 16), [[1024, 4], [0, 4]], 0)
     scan(W("k4", 0, 256), W("ones", 0, 256), W("ones", 0, 256), -1.0, ALU.mult, ALU.add)
-    ts(W("c16", 0, 64), W("k4", 0, 64), 16.0, ALU.mult)
     ts(W("pi", 1, 1), W("pi", 0, 1), 15, ALU.bitwise_and)
     ts(W("pi", 2, 1), W("pi", 1, 1), 1, ALU.logical_shift_right)
     ts(W("pi", 3, 1), W("pi", 0, 1), 3, ALU.bitwise_and)
-    ts(W("pi", 4, 1), W("pi", 0, 1), 1, ALU.bitwise_and)
     cp(C(ROW), W("pi", 1, 1))
     ts(C(LOW), C(ROW), 12.0, ALU.is_lt)
     ts(C(HIGH), C(ROW), 12.0, ALU.is_ge)
-    lin(C(ZC), C(HIGH), -4096.0)
-    lin(C(INC), C(HIGH), 4096.0, 4.5)
+    lin(C(ZC), C(HIGH), -1.0)
     ts(C(TMP), W("pi", 2, 1), C(LOW), ALU.mult)
     ts(C(TMP + 1), C(ROW), -11.0, ALU.add, 0.0, ALU.max)
     tt(C(JC), C(TMP), C(TMP + 1), ALU.add)
     ts(C(FC), W("pi", 3, 1), 4096.0, ALU.mult, NXB - ZR0 + 2048.0, ALU.add)
     for ic in range(4):
         lin(C(IC + ic), C(ROW), 1.0, 16.0 * ic + 0.5)
-    ts(C(TBC), W("pi", 4, 1), C(HIGH), ALU.mult, 12288.0, ALU.mult)
-    lin(C(TMP + 2), C(HIGH), 1024.0, -3 * BIG)
-    for (k, base, c) in (("N3B", "I", TMP + 2), ("DL", "I", LOW), ("DH", "I", HIGH), ("RW", "BLK", ROW), ("RH", "B12", ROW)):
-        lin(M(k), M(base), C(c))
     lin(C(TMP + 3), C(LOW), 4.0)
     for o in range(4):
         lin(C(KBC + 4 + o), C(HIGH), 1024.0 * o - 2048.0)
@@ -448,39 +536,39 @@ def rank_program(g, core, T, topo):
     for t in range(3):
         lin(C(KBC + t), C(LOW), V * (t + 1) + 15.0 - CEN)
         ts(W("kb", 256 * t, 256), W("kb", 768, 256), C(KBC + t), ALU.add)
-    for b in range(2):
-        ts(W("vl", 64 * b, 64), W("c16", 0, 64), C(ROW), ALU.add)
-    ts(W("wk", 0, 64), W("c16", 0, 64), C(ROW), ALU.add, XN0 - RL0 - 2048.0, ALU.add)
-    for lo in (0, 512) if EARLY else ():
-        cp(W("q16", lo, 512), W("tki", lo, 512))
-        ts(W("hi", lo, 512), W("q16", lo, 512), 1.0 / 64.0, ALU.mult, 192.0, ALU.add)
-        p = tile()
-        mms(p, [(M("TA"), W("q16", lo, 512)), (M("TB"), W("hi", lo, 512))])
-        act(W("tkt", V * rank + lo, 512), p, bias=C(TBC))
+    lin(C(TMP + 2), C(ROW), 1.0, 1024.0)
+    ts(W("pay", 128, 64), W("k4", 0, 64), 16.0, ALU.mult, C(TMP + 2), ALU.add)
+    lin(W("wk", 0, 64), W("pay", 128, 64), 1.0, XN0 - RL0 - 3072.0)
+    for b in range(2) if any(EARLY) else ():
+        ts(W("vl", 64 * b, 64), W("pay", 128, 64), -1020.0, ALU.add)
     for r in RELAY:
         share(*r)
     cp(C(WF), W("wti", 0, 1))
     cp(C(THF), W("thi", 0, 1))
     lin(M("ZW", 0, 144), M("Z", 0, 144), C(WF))
+    cp(W("got", 0, 1), W("wti", 0, 1))
+    p = tile(1)
+    mms(p, [(M("BLK"), W("got", 0, 1))])
+    lin(C(HC), p, -128.0)
     lin(W("thl", 0, 64), W("ones", 0, 64), C(THF))
     ts(W("kz", 0, 128), W("kin", 0, 128), float(V), ALU.min)
     ts(W("wk", 64, 128), W("kin", 0, 128), -8.0, ALU.mult, 32768.0 - CEN, ALU.add)
     ts(W("wk", 192, 128), W("kin", 0, 128), 16.0 - CEN, ALU.add)
     tt(W("pay", 0, 128), W("wk", 64, 128), W("wk", 192, 128), ALU.min)
-    if EARLY:
-        cp(W("k16", 0, 128), W("pay", 0, 128))
-    else:
-        lin(W("d32", 256, 16), W("zt", 0, 16))
+    lin(W("d32", 256, 16), W("zt", 0, 16))
 
     def own(buf, s, lo, n):
         return W("%s_%d" % (buf, s), lo + (16 if s else 0), n)
 
     def kid(buf, s, b, lo, n):
         end = 16 + V * min(lo // V + 2, s + 1)
-        return G("%s_%d" % (buf, s), 0, end, *(("kl%d" % b, lo // 16) if s else ("kz", 64 * b + lo // 16)), n // 16)
+        return G("%s_%d" % (buf, s), 0, end, "kl" if s else "kz", 128 * (lo // V) + 64 * b + lo % V // 16, n // 16)
 
-    def pass1(s, lo, n=512):
-        first = act(W("ta", lo, n), kid("x", s, 0, lo, n))
+    def pass1(s, lo, n, on="s"):
+        first = (cp if on == "v" else act)(W("ta", lo, n), kid("x", s, 0, lo, n))
+        if FORM[s] == "p":
+            tt(own("q", s, lo, n), kid("x", s, 1, lo, n), W("ta", lo, n), ALU.max)
+            return
         tt(W("tb", lo, n), kid("x", s, 1, lo, n), W("ta", lo, n), ALU.max)
         x, p = own("x", s, lo, n), tile(n)
         if lo // 256 in RELU[s]:
@@ -493,61 +581,100 @@ def rank_program(g, core, T, topo):
             mms(p, [(M("I2"), x)] if s else [(M("I"), x), (M("C2"), W("ones", 0, n))], after=[first])
             tt(own("q", s, lo, n), W("tb", lo, n), p, ALU.max)
 
-    def pass2(s, lo, n, out, how):
-        act(W("tc", lo, n), kid("q", s, 0, lo, n))
-        tt(W("td", lo, n), kid("q", s, 1, lo, n), W("tc", lo, n), ALU.max)
-        p, k = tile(n), "I63" if how == "v" else "I"
-        mms(p, [(M(k), own("x", s, lo, n)), (M(k), W("td", lo, n))])
-        if how == "v":
-            ts(out, p, MAGIC - (127.0 if s else 1.0), ALU.add, -MAGIC, ALU.add)
-        elif how == "s":
-            act(out, p, bias=-1.25, scale=0.5)
+    def pass2(s, lo, n, out, how, behind=()):
+        x, q, a, b = own("x", s, lo, n), own("q", s, lo, n), W("tc", lo, n), W("td", lo, n)
+        if how[0] == "w":
+            ts(W("tb", lo, n), q, 2.0, ALU.add)
+            first = tt(a, kid("q", s, 0, lo, n), W("tb", lo, n), ALU.max)
         else:
-            act(W("tc", lo, n), p, bias=-1.25 if s else 126.75, scale=0.5)
-            ts(out, W("tc", lo, n), -128.0, ALU.add)
+            first = act(a, kid("q", s, 0, lo, n))
+        if how[0] == "m":
+            p = tile(n)
+            mms(p, [(M("I2"), q)] if s else [(M("I"), q), (M("C2"), W("ones", 0, n))], after=[first] if n > 256 else [])
+            tt(W("tb", lo, n), a, p, ALU.max)
+            a = W("tb", lo, n)
+        second = tt(b, kid("q", s, 1, lo, n), a, ALU.max)
+        for i in behind:
+            for u in (first, second):
+                if ops[i]["e"] == ops[u]["e"] and not ops[i]["alt"]:
+                    ops[u]["dep"].setdefault(i, False)
+        k = "I63" if how[1] == "v" and s == 3 else "I"
+        if FORM[s] == "q" or how[0] in "mw":
+            parts, off = [x, b], 1.0
+        else:
+            p = tile(n)
+            mms(p, [(M("NI"), q), (M("I"), b)])
+            lin(a, p, 1.0, -2.0, how[0], True)
+            parts, off = [x, q, a], 0.0
+        p = tile(n)
+        mms(p, [(M(k), u) for u in parts])
+        if s < 3:
+            lin(out, p, 0.5, (-0.25 if s else 127.75) - off, how[1])
+        elif how[1] == "v":
+            ts(out, p, MAGIC - off - 126.0, ALU.add, -MAGIC, ALU.add)
+        else:
+            u = a if FORM[s] == "q" or how[0] in "mw" else b
+            act(u, p, bias=(-0.25 if s else 127.75) - off, scale=0.5)
+            ts(out, u, -128.0, ALU.add)
+        return range(second + 1, len(ops))
 
-    for (lo, n) in FIRST:
-        pass1(0, lo, n)
+    for i, (lo, n) in enumerate(FIRST):
+        pass1(0, lo, n, "v" if i < ALONE else "s")
 
     for t in range(3):
         S = V * (t + 1)
         B0 = S - V
         nxt = "x_%d" % (t + 1)
         for i, (lo, n) in enumerate(PIECES):
-            pass2(t, B0 + lo, n, W("bt", XN0 + lo, n), "v" if i in NEW_V else "sv")
+            pass2(t, B0 + lo, n, W("xb", lo, n), NEW[i])
+        for lo in (0, 512):
+            lin(W("bt", XN0 + lo, 512), W("xb", lo, 512), 1.0, -128.0, RAW[t])
         for lo in range(0, B0, OLD):
-            pass2(t, lo, OLD, own("x", t + 1, lo, OLD), "s")
-        p = tile(64)
-        mms(p, wrap16("ZW", "bt", XN0))
-        ts(W("c1", 0, 64), p, 31.0 * t, ALU.add)
-        ts(W("c1", 64, 64), W("c1", 0, 64), 4095, ALU.bitwise_and)
+            pass2(t, lo, OLD, own("x", t + 1, lo, OLD), OLDS[t][lo // OLD])
+        for (lo, n) in HASH[t]:
+            p = tile(n)
+            mms(p, wrap16("ZW", "xb", 16 * lo, 16 * n))
+            ts(W("c1", lo, n), p, C(HC), ALU.add, 31.0 * t, ALU.add)
+            ts(W("c1", 64 + lo, n), W("c1", lo, n), 4095, ALU.bitwise_and)
+            for m in range(4):
+                ts(W("offl", 64 * m + lo, n), W("c1", 64 + lo, n), 97.0 * m, ALU.add)
+        if VALS == "s":
+            cp(W("c0", 0, 64), W("c1", 64, 64))
         for m in range(4):
-            ts(W("offl", 64 * m, 64), W("c1", 64, 64), 97.0 * m, ALU.add)
-        cp(W("c0", 0, 64), W("c1", 64, 64))
-        for m in range(4):
-            act(W("val", 64 * m, 64), W("c0", 0, 64), bias=float(2 * (8192 * (4 - m) + 97 * m) + 1), scale=2.0)
+            lin(W("val", 64 * m, 64), W("c0", 0, 64) if VALS == "s" else W("c1", 64, 64), 2.0, 2.0 * (8192 * (4 - m) + 97 * m) + 1, VALS)
+        near = tile(192)
         for m in range(4):
             how = DIST[t][m]
-            for lo in (0, 512):
-                root, x = G("bt", 0, RCW, "offl", 64 * m + lo // 16, 32), W("bt", XN0 + lo, 512)
-                d, a = W("dd", V * m + lo, 512), W("da", V * m + lo, 512)
+            for (lo, n) in (GAPS if m == 3 else ((0, 512), (512, 512))):
+                root, x = G("bt", 0, RCW, "offl", 64 * m + lo // 16, n // 16), W("xb", lo, n)
+                d, a = W("dd", V * m + lo, n), W("da", V * m + lo, n)
                 if how == "s":
                     act(d, root)
-                    p = tile()
+                    p = tile(n)
                     mms(p, [(M("NI"), x), (M("I"), d)])
-                    act(a, p, ACT.Abs)
+                    act(a, p, ACT.Abs, bias=128.0)
                 else:
                     tt(d, root, x, ALU.subtract)
-                    if how == "vs":
-                        act(a, d, ACT.Abs)
-                    else:
-                        ts(a, d, 0.0, ALU.max)
-            p = tile(64)
-            pairs = wrap16("ZP", "dd", V * m) + wrap16("ZM", "da", V * m) if how == "v" else wrap16("ZN", "da", V * m)
-            mms(p, [(M("IB"), W("thl", 0, 64))] + pairs)
-            tt(W(p[0], 64, 64) if m else W("sc", 0, 64), W("val", 64 * m, 64), p, ALU.min)
-            if m:
-                tt(W("sc", 64 * m, 64) if m < 3 else W("bi", 0, 64), W("sc", 64 * m - 64, 64), W(p[0], 64, 64), ALU.max)
+                    act(a, d, ACT.Abs, bias=128.0)
+            p = W(near[0], 64 * m, 64) if m < 3 else tile(64)
+            mms(p, [(M("IB"), W("thl", 0, 64))] + wrap16("ZN", "da", V * m), True, m < 3 or not FOLD)
+            if m < 3 and SCORE == 4:
+                near = tile(64) if m < 2 else near
+                tt(W(p[0], 192, 64) if m else W("sc", 0, 64), W("val", 64 * m, 64), p, ALU.min)
+                if m:
+                    tt(W("sc", 64 * m + 64, 64), W("sc", 128 * m - 128, 64), W(p[0], 192, 64), ALU.max)
+        if SCORE == 3:
+            tt(W("sc", 0, 192), W("val", 0, 192), near, ALU.min)
+            tt(W(near[0], 192, 64), W("sc", 0, 64), W("sc", 64, 64), ALU.max)
+            tt(W("sc", 192, 64), W("sc", 128, 64), W(near[0], 192, 64), ALU.max)
+        if FOLD:
+            ts(W("got", 0, 64), W("sc", 192, 64), 0.0, ALU.is_gt)
+            tt(W("sc", 64, 64), W("sc", 192, 64), W("val", 192, 64), ALU.max)
+            mms(p, [(M("IF"), W("got", 0, 64))], False, True)
+            tt(W("bi", 0, 64), W("sc", 64, 64), p, ALU.min)
+        else:
+            tt(W(p[0], 64, 64), W("val", 192, 64), p, ALU.min)
+            tt(W("bi", 0, 64), W("sc", 192, 64), W(p[0], 64, 64), ALU.max)
         ts(W("bi", 64, 64), W("bi", 0, 64), 7, ALU.bitwise_and)
         for o in range(4):
             ts(W("ask", 64 * o, 64), W("bi", 64, 64), float(2 * o + 1), ALU.is_equal)
@@ -555,28 +682,41 @@ def rank_program(g, core, T, topo):
         ts(W("bi", 128, 64), W("bi", 0, 64), 3, ALU.logical_shift_right, 1023, ALU.bitwise_and)
         ts(W("ob", 0, 64), W("bi", 64, 64), 512.0, ALU.mult, -2560.0, ALU.add)
         tt(W("tcc", 0, 64), W("bi", 128, 64), W("ob", 0, 64), ALU.add)
-        if EARLY:
-            ts(W("ls", 32, 64), W("tcc", 0, 64), 2048.0, ALU.add)
         p = tile(256)
-        mms(p, [(M("BLK"), W("cs", 0, 256))])
-        for ic in range(4):
-            act(W("sg", 256 * ic, 256), p, ACT.Sign, bias=C(IC + ic), scale=-1.0)
-            scan(W("sn", 256 * ic, 256), W("keep", 0, 256), W("sg", 256 * ic, 256), 0.0, ALU.mult, ALU.add)
+        count0 = mms(p, [(M("BLK"), W("cs", 0, 256))])
+        if SIGNS == "s":
+            for ic in range(4):
+                act(W("sg", 256 * ic, 256), p, ACT.Sign, bias=C(IC + ic), scale=-1.0)
+                scan(W("sn", 256 * ic, 256), W("keep", 0, 256), W("sg", 256 * ic, 256), 0.0, ALU.mult, ALU.add)
+        else:
+            p2 = tile(128)
+            mms(p2, [(M("BLK"), W("cs", 128, 128))])
+            for ic in range(4):
+                act(W("sg", 128 * ic, 128), W(p[0], 0, 128), ACT.Sign, bias=C(IC + ic), scale=-1.0)
+                ts(W("sg", 512 + 128 * ic, 128), p2, C(IC + ic), ALU.is_lt)
+            for lo in (512, 768, 0, 256):
+                scan(W("sn", lo, 256), W("keep", 0, 256), W("sg", lo, 256), 0.0, ALU.mult, ALU.add)
         p = tile(256)
         mms(p, [(M("UN"), W("ask", 0, 256)), (M("BLK"), W("cs", 0, 256))])
         act(W("ra", 0, 256), p, ACT.Relu, bias=65.0 - BIG, scale=-1.0)
         for o in range(4):
-            ts(W("ls", 4 * o, 4), R("sn", 64 * o + 62, V, 256), 0.5, ALU.mult, 31.5, ALU.add)
+            if SIGNS == "s":
+                ts(W("ls", 4 * o, 4), R("sn", 64 * o + 62, V, 256), 0.5, ALU.mult, 31.5, ALU.add)
+            elif o < 2:
+                ts(W("ls", 4 * o, 4), R("sn", 64 * o + 62, 512, 128), 0.5, ALU.mult, 31.5, ALU.add)
+            else:
+                cp(W("ls", 4 * o, 4), R("sn", 384 + 64 * o + 62, V, 128))
         for o in range(4):
-            hit = tt(W("mask", 64 * o, 64), G("ra", 64 * o, 64 * o + 64, "ls", 4 * o, 4), W("il", 0, 64), ALU.is_equal)
-        mask, cg = W("mask", 0, 256), W("cg", 0, 256)
-        tree, old0, old1 = [W("pr", 256 * i, 256) for i in range(3)]
+            tt(W("mask", 64 * o, 64), G("ra", 64 * o, 64 * o + 64, "ls", 4 * o, 4), W("il", 0, 64), ALU.is_equal)
+        mask = W("mask", 0, 256)
+        tree, vv, old0, old1 = [W("pr", 256 * i, 256) for i in range(4)]
         tt(tree, G("bi", 128, 192, "ls", 0, 16), mask, ALU.mult)
-        act(cg, G("c16", 0, 64, "ls", 0, 16))
+        tt(vv, G("pay", 128, 192, "ls", 0, 16), mask, ALU.mult)
         tt(old0, G("pay", 0, 64, "ls", 0, 16), mask, ALU.mult)
         tt(old1, G("pay", 64, 128, "ls", 0, 16), mask, ALU.mult)
         p = tile(16)
-        mms(p, [(M("I"), W("oc", 0, 16))] + wrap16("Z", "pr", 0, 256))
+        mms(p, [(M("I"), W("oc", 0, 16))], True, False, [count0])
+        mms(p, wrap16("Z", "pr", 0, 256), False, True)
         cp(W("ls", 16, 16), p)
         q = W("r16", 0, 256)
         cp(q, G("tkt", 0, 4096, "ls", 16, 16))
@@ -586,134 +726,136 @@ def rank_program(g, core, T, topo):
         act(inv, p, ACT.Relu, bias=1.0, scale=-1.0)
         p = tile(128)
         mms(W(p[0], 0, 64), [(M("I"), W("tcc", 0, 64)), (M("BI"), inv)])
-        if EARLY:
-            mms(W(p[0], 64, 64), [(M("N4"), W("ra", 64 * o, 64)) for o in range(4)] + [(M("I4"), W("ob", 0, 64))])
-        else:
-            mms(W(p[0], 64, 64), [(M("NI"), W("ra", 64 * o, 64)) for o in range(4)] + [(M("I4"), W("ob", 0, 64)), (M("BI"), inv)])
+        mms(W(p[0], 64, 64), [(M("NI"), W("ra", 64 * o, 64)) for o in range(4)] + [(M("I16"), W("ob", 0, 64))]
+            + ([] if EARLY[t] else [(M("BI"), inv)]))
         tt(W("wk", 448, 64), W("wk", 0, 64), W(p[0], 0, 64), ALU.min)
         ts(W("ls", 96, 64), W("wk", 448, 64), 2048.0, ALU.add)
-        if EARLY:
-            ts(W("rb", 0, 64), W(p[0], 64, 64), 768.0 + S + 15.0 - CEN, ALU.add)
-        else:
-            ts(W("ls", 32, 64), W(p[0], 64, 64), 192.0, ALU.add, 256.0, ALU.min)
-            for b in range(2):
-                tt(W("k16", 64 * b, 64), W("pay", 64 * b, 64), inv, ALU.mult)
-        for lo in (0, 512):
-            root, x, out = G("bt", RL0, NXB, "ls", 96 + lo // 16, 32), W("bt", XN0 + lo, 512), W(nxt, 16 + B0 + lo, 512)
-            if HALVE[t] == "s":
-                act(W("sel", lo, 512), root)
-                p = tile()
-                mms(p, [(M("I"), x), (M("I"), W("sel", lo, 512))])
-                act(out, p, bias=127.75, scale=0.5)
-            else:
-                tt(W("sel", lo, 512), root, x, ALU.add)
-                ts(out, W("sel", lo, 512), 0.5, ALU.mult, 127.75, ALU.add)
-        if EARLY:
-            for lo in (0, 512):
-                act(W("rs", lo, 512), G("tkt", 0, 4096, "ls", 32 + lo // 16, 32))
+        if EARLY[t]:
+            ts(W("rb", 0, 64), W(p[0], 64, 64), 4.0, ALU.mult, 768.0 + S + 15.0 - CEN, ALU.add)
+            ts(W("ls", 32, 64), W("tcc", 0, 64), 2048.0, ALU.add)
+            cp(W("k16", 0, 128), W("pay", 0, 128))
+            for (lo, n) in ROOT:
+                cp(W("dv", lo, n), G("tkt", 0, 4096, "ls", 32 + lo // 16, n // 16))
             p = tile(128)
             for b in range(2):
-                for i in range(0, 16, 4):
-                    mms(W(p[0], 64 * b, 64), wrap16("ZK%d" % b, "rs", 0)[i:i + 4], i == 0, i == 12)
+                for i in range(0, 16, 8):
+                    mms(W(p[0], 64 * b, 64), wrap16("ZK%d" % b, "dv", 0)[i:i + 8], i == 0, i == 8)
             rq = W("rq", 0, 128)
             inner, none, wrap = [W("rm", 128 * i, 128) for i in range(3)]
-            ts(rq, p, -12288.0, ALU.add)
+            cp(rq, p)
             ts(inner, rq, 4.5, ALU.is_lt)
             ts(none, rq, 0.0, ALU.is_equal)
-            back = [(M("I"), W("vl", 0, 128)), (M("NI"), rq)]
+            back = [(M("I"), W("vl", 0, 128)), (M("NI"), rq), (M("BI"), inner)]
             if t == 0:
-                p = tile(128)
-                mms(p, back)
-                ts(wrap, p, -4.0, ALU.is_lt)
+                tt(wrap, rq, W("vl", 0, 128), ALU.is_gt)
                 back = back + [(M("IK"), wrap)]
             p = tile(128)
-            mms(p, back + [(M("BI"), inner)])
-            act(W("de", 512, 128), p, bias=B0 + 20.0 - CEN)
+            mms(p, back)
+            act(W("de", 512, 128), p, bias=B0 + 16.0 - CEN)
             p = tile(128)
             mms(p, [(M("I"), rq), (M("NBI"), none)], True, False)
             for b in range(2):
                 mms(W(p[0], 64 * b, 64), [(M("I"), W("rb", 0, 64)), (M("NBI"), inv)], False, b == 1)
             tt(W("de", 640, 128), W("de", 512, 128), p, ALU.min)
             p = tile(128)
-            mms(p, [(M("NBI"), W("ones", 0, 128)), (M("I"), W("k16", 0, 128))], True, False, [hit])
+            mms(p, [(M("NBI"), W("ones", 0, 128)), (M("I"), W("k16", 0, 128))], True, False, [count0])
             for b in range(2):
                 mms(W(p[0], 64 * b, 64), [(M("BI"), inv)], False, b == 1)
-            tt(W("rd", 0, 128), W("de", 640, 128), p, ALU.max)
+            tt(W("de", 512, 128), W("de", 640, 128), p, ALU.max)
+            ts(W("kl", 128 * t, 128), W("de", 512, 128), CEN, ALU.add)
+        else:
+            ts(W("ls", 32, 64), W(p[0], 64, 64), 192.0, ALU.add, 256.0, ALU.min)
             for b in range(2):
-                ts(W("kl%d" % b, 64 * t, 64), W("rd", 64 * b, 64), CEN, ALU.add)
+                tt(W("k16", 64 * b, 64), W("pay", 64 * b, 64), inv, ALU.mult)
+        for lo in (0, 512):
+            root, x, out = G("bt", RL0, NXB, "ls", 96 + lo // 16, 32), W("xb", lo, 512), W(nxt, 16 + B0 + lo, 512)
+            if HALVE[t] == "s":
+                act(W("sel", lo, 512), root)
+                p = tile()
+                mms(p, [(M("I"), x), (M("I"), W("sel", lo, 512))])
+                lin(out, p, 0.5, 63.75, HALF[t])
+            else:
+                tt(W("sel", lo, 512), root, x, ALU.add)
+                ts(out, W("sel", lo, 512), 0.5, ALU.mult, 63.75, ALU.add)
         inner, none, foot, wrap = [W("mk", 256 * i, 256) for i in range(4)]
-        ts(inner, q, C(INC), ALU.is_lt)
+        ts(inner, q, 4.5, ALU.is_lt)
         ts(none, q, C(ZC), ALU.is_equal)
         p = tile(256)
         mms(p, [(M("RF"), q)])
         ts(foot, p, C(JC), ALU.is_equal)
-        back = [(M("I"), cg), (M("RW"), mask), (M("NI"), q)]
+        back = [(M("NI"), q), (M("BI"), inner)]
         if t == 0:
             p = tile(256)
-            mms(p, back)
-            ts(wrap, p, -4.0, ALU.is_lt)
+            mms(p, [(M("NW"), W("ones", 0, 256)), (M("BLK"), vv)])
+            tt(wrap, q, p, ALU.is_gt)
             back = back + [(M("IK"), wrap)]
         p = tile(256)
-        mms(p, back[:2], True, False)
-        mms(p, back[2:] + [(M("BI"), inner)], False, True)
-        act(W("de", 0, 256), p, bias=B0 + 20.0 - CEN)
+        mms(p, [(M("BB"), mask)], True, False)
+        mms(p, [(M("BLK"), vv)], False, False)
+        mms(p, back, False, True)
+        act(W("de", 0, 256), p, bias=B0 + 20.0 - 1024.0 - CEN - 3 * BIG)
         p = tile(256)
-        mms(p, [(M("N2B"), W("ones", 0, 256)), (M("I"), W("kb", 256 * t, 256)), (M("BB"), mask), (M("B12"), tree)], True, False, [hit])
-        mms(p, [(M("DL"), q), (M("NBI"), none)], False, False)
+        mms(p, [(M("I"), W("kb", 256 * t, 256))], True, False, [count0])
+        mms(p, [(M("B12"), tree)], False, False)
+        mms(p, [(M("I"), q), (M("NBI"), none)], False, False)
         mms(p, [(M("NBI"), foot)], False, True)
         tt(W("de", 256, 256), W("de", 0, 256), p, ALU.min)
         p = tile(256)
-        mms(p, [(M("N3B"), W("ones", 0, 256)), (M("BB"), mask), (M("DH"), cg), (M("RH"), mask)], True, False, [hit])
-        mms(p, [(M("LO0"), old0)], False, False)
-        mms(p, [(M("LO1"), old1)], False, False)
+        mms(p, [(M("N4B"), W("ones", 0, 256))], True, False, [count0])
+        for pair in ((M("BB"), mask), (M("B12"), vv), (M("LO0"), old0), (M("LO1"), old1)):
+            mms(p, [pair], False, False)
         mms(p, [(M("BI"), foot)], False, True)
-        tt(W("d16", 0, 256), W("de", 256, 256), p, ALU.max)
-        if not EARLY:
-            tt(W("d32", 0, 256), W("de", 256, 256), p, ALU.max)
+        first = tt(W("d16", 0, 256), W("de", 256, 256), p, ALU.max)
+        if not EARLY[t]:
+            ops[tt(W("d32", 0, 256), W("de", 256, 256), p, ALU.max)]["dep"][first] = False
         p = tile(64)
         mms(p, wrap4("PG", "mk", 512), True, False)
         mms(p, wrap4("PFI", "d16"), False, True)
         ts(W("ls", 160, 64), p, C(FC), ALU.add)
         if t < 2:
             ts(W("thl", 0, 64), p, -20000.0, ALU.is_gt, C(THF), ALU.mult)
-        for lo in (0, 512):
-            out, src = W(nxt, 16 + S + lo, 512), G("bt", ZR0, NXB + 16384, "ls", 160 + lo // 16, 32)
-            if FILL[t][lo // 512] == "s":
+        for (lo, n, e) in FILL[t]:
+            out, src = W(nxt, 16 + S + lo, n), G("bt", ZR0, NXB + 16384, "ls", 160 + lo // 16, n // 16)
+            if e == "s":
                 act(out, src, bias=128.0)
             else:
                 ts(out, src, 128.0, ALU.add)
         p = tile(128)
         for b in range(2):
             mms(W(p[0], 64 * b, 64), wrap4("PK%d" % b, "d16"))
-        for b in range(2):
-            ts(W("kl%d" % b, 64 * t + 64, 64), W(p[0], 64 * b, 64), CEN, ALU.add)
+        ts(W("kl", 128 * t + 128, 128), p, CEN, ALU.add)
         if t < 2:
             ts(W("pay", 0, 128), p, -CEN, ALU.max)
-            if EARLY:
-                ts(W("k16", 0, 128), p, -CEN, ALU.max)
-        if not EARLY:
-            for lo in (0, 512):
-                ts(W("q16", lo, 512), G("d32", 0, 272, "ls", 32 + lo // 16, 32), -CEN, ALU.max)
-            for b in range(2):
-                p = tile(64)
-                mms(p, [(M("I"), W("k16", 64 * b, 64))] + wrap16("ZK%d" % b, "q16", 0))
-                ts(W("kl%d" % b, 64 * t, 64), p, CEN, ALU.add)
+        for (lo, n) in () if EARLY[t] else DV:
+            ts(W("dv", lo, n), G("d32", 0, 272, "ls", 32 + lo // 16, n // 16), -CEN, ALU.max)
+        for b in () if EARLY[t] else range(2):
+            p = tile(64)
+            mms(p, [(M("I"), W("k16", 64 * b, 64))] + wrap16("ZK%d" % b, "dv", 0))
+            ts(W("kl", 128 * t + 64 * b, 64), p, CEN, ALU.add)
         for lo in range(0, B0, OLD):
             pass1(t + 1, lo, OLD)
-        for (lo, n) in TAIL:
-            pass1(t + 1, B0 + lo, n)
+        for i, (lo, n) in enumerate(TAIL):
+            pass1(t + 1, B0 + lo, n, "v" if i < ALONE else "s")
 
+    done = []
     for c in range(8):
         for (lo, n) in (((512 * c, 512),) if c < 7 else ((3584, 384), (3968, 128))):
-            pass2(3, lo, n, W("yo", lo, n), "v" if c in LAST_V else "sv")
+            done.append(pass2(3, lo, n, W("yo", lo, n), LAST[c], done[-DEPTH] if len(done) >= DEPTH else ()))
             if c >= 6:
                 dma("y", T.y[:, lo:lo + n], W("yo", lo, n), 256 * n)
             elif c % 2:
                 dma("y", T.y[:, lo - 512:lo + 512], W("yo", lo - 512, V), 1 << 18)
 
-    got, extra = banks(ops, tiles)
+    shape = tuple((o["e"], o["cost"], tuple(o["dep"].items())) for o in ops)
+    if shape not in PLANS:
+        start = tighten(ops, [], place(ops), TRIES)
+        got, extra = banks(ops, tiles, start)
+        PLANS[shape] = (tighten(ops, extra, start, TRIES // 4), got, extra, [o["e"] for o in ops])
+    start, got, extra, on = PLANS[shape]
+    for o, e in zip(ops, on):
+        if o["alt"]:
+            o.update(e=e, cost=o["alt"][e][0], fn=o["alt"][e][1])
     where.update(got)
-    start = place(ops, extra)[0]
     for (a, b) in extra:
         ops[b]["dep"][a] = True
     cnt = {e: 0 for e in Q}

from concourse.bass import DstId, RemoteDMATransfer
from concourse.mybir import AluOpType as ALU, ActivationFunctionType as ACT

N = 4
V = 1024
RCW = 4096 + 304
RL0 = RCW
ZR0 = RL0 + 4096
XN0 = ZR0 + 16
NXB = XN0 + V
CEN = 2064.0
BIG = 16384.0
FAR = 131072.0
MAGIC = 12582912.0
RELAY = (("tkt", [0], "t"), ("bt", [NXB, NXB + 4096], "n"), ("bt", [NXB + 8192], "m"), ("bt", [NXB + 12288], "l"))

DIST = (("s", "vs", "vs", "vs"),) * 3
HASH = (((0, 64),),) * 3
GAPS = ((0, 512), (512, 512))
EARLY = (False, False, False)
ROOT = ((0, 256), (256, 256), (512, 256), (768, 256))
FOLD = True
SIGNS = "sv"
RAW = ("v", "v", "v")
FORM = "pppp"
RELU = ((), (0,), (0, 2), (0, 2, 4, 6))
HALVE = ("s", "s", "s")
HALF = ("s", "s", "s")
DV = ((0, 256), (256, 256), (512, 512))
OLDS = ((), ("ss", "ss"), ("ss", "ss", "ss", "ss"))
LAST = ("ss", "ss", "ms", "ss", "sv", "ms", "sv", "mv")
DEPTH = 9
FILL = (((0, 768, "s"), (768, 256, "v")),) * 3
ALONE = 0
VALS = "s"
NEW = ("ws", "ms", "ms", "ms", "ms")
PIECES = ((0, 128), (128, 256), (384, 384), (768, 128), (896, 128))
OLD = 512
TAIL = ((1024, 256), (1280, 256), (1536, 512), (0, 512), (512, 384), (896, 128))
FIRST = ((0, 128), (128, 384), (512, 384), (896, 128))
WEAVE = ("v", "g", "s", "v")
DIRECT = "ml"
PRE = 2

CYC, GATHER = 0.83, 1.56
FUSED = 1.56
CALL = 5.0
HOP = 205.0
PECYC = 0.43
PEFIX = 10.0
SCORE = 4
TURNS = 2
TRIES = 8000
PLANS = {}
SHAKE = 3000.0
SLACK = 30.0
SOME = 0.3
SWAP = 0.0
RULES = ((1.0, 300.0),)
EAGER = (0.3, 20.0)
LOAD = 2000.0
ARRIVE = {"r": (1500.0, 900.0), "t": (9000.0, 0.0), "n": (10000.0, 0.0), "m": (10000.0, 0.0), "l": (10000.0, 0.0)}

DIAG = {"I": 1.0, "I2": 65.0 / 64.0, "I63": 63.0 / 128.0, "NI": -1.0, "IB": FAR, "BI": BIG, "NBI": -BIG, "N4B": -4 * BIG,
        "IK": 1024.0, "I16": 0.0625, "C2": 2.0, "NW": -1020.0, "IF": 256 * FAR}
MATS = list(DIAG) + ["BLK", "BB", "UN", "RF", "B12", "LO0", "LO1"]
WIDE = ["Z", "ZW", "ZN", "ZK0", "ZK1", "PK0", "PK1", "PFI", "PG"]
MOFF = {k: 128 * i for i, k in enumerate(MATS)}
MOFF.update({k: 144 * i for i, k in enumerate(WIDE)})

SCRATCH = {"bt": ("sbuf", [128, NXB + 16384], "bfloat16"), "cm": ("sbuf", [128, 128 * len(MATS)], "bfloat16"),
           "cz": ("sbuf", [128, 144 * len(WIDE)], "bfloat16")}
for _t, _l in (("bfloat16", (("x_0", 1040), ("x_1", 2064), ("x_2", 3088), ("x_3", 4112), ("q_0", 1040), ("q_1", 2064),
                             ("q_2", 3088), ("q_3", 4112), ("ta", 4096), ("tb", 4096), ("tc", 4096), ("td", 4096), ("dd", 4096),
                             ("da", 4096), ("yo", 4096), ("sel", V), ("ones", 512), ("zt", 384), ("t8", 128), ("thl", 64),
                             ("ask", 256), ("keep", 256), ("cs", 256), ("oc", 16), ("il", 64), ("ra", 256), ("sg", V), ("sn", V),
                             ("mask", 256), ("ob", 64), ("inv", 64), ("mk", V), ("rm", 384), ("got", 64), ("xb", V))),
               ("float32", (("col", 32), ("val", 256), ("sc", 256), ("pay", 192), ("wk", 512), ("de", 768), ("c0", 64), ("d32", 272))),
               ("float16", (("dv", V), ("k16", 128), ("r16", 256), ("kb", V), ("d16", 256), ("pr", V), ("k4", 256), ("tcc", 64),
                            ("vl", 128), ("rq", 128), ("rb", 64))),
               ("int32", (("tkt", 4096), ("kin", 128), ("wti", 8), ("thi", 8), ("pi", 8), ("c1", 128), ("bi", 192))),
               ("uint16", (("kz", 128), ("kl", 512), ("offl", 256), ("ls", 224)))):
    for _k, _n in _l:
        SCRATCH[_k] = ("sbuf", [128, _n], _t)
for _b in range(8):
    SCRATCH["ps%d" % _b] = ("psum", [128, 512], "float32")

SEMAPHORES = (["cv", "cs", "cp", "cg", "ar_t", "ar_n", "ar_m", "sn_r", "sn_t", "sn_n", "sn_m", "ar_l", "sn_l"] + ["ar_r%d" % i for i in range(N)]
              + ["dm%d" % i for i in range(32)])


def run(ops, pred, release, rank, rule, choose=False):
    n = len(ops)
    succ = [[] for _ in ops]
    for b in range(n):
        for a in pred[b]:
            succ[a].append(b)
    order = sorted(range(n), key=lambda i: (-rank[i], i))
    start, free = [None] * n, {e: 0.0 for e in (None, "v", "s", "p", "g", "y")}
    wait = [len(p) for p in pred]
    ready = {i: release[i] for i in range(n) if not wait[i]}
    while ready:
        t, _, b, e = min((max(ready[i], free[e]), -rank[i], i, e) for i in ready
                         for e in (ops[i]["alt"] if choose and ops[i]["alt"] else [ops[i]["e"]]))
        if ops[b]["alt"]:
            ops[b].update(e=e, cost=ops[b]["alt"][e][0], fn=ops[b]["alt"][e][1])
        if e is not None:
            soon, hold, (give, grace) = {}, [], rule if e in "vs" else EAGER
            for i in order:
                if rank[i] <= rank[b]:
                    break
                if start[i] is None:
                    soon[i] = max([soon.get(a, start[a]) + ops[a]["cost"] + pred[i][a] for a in pred[i]] + [t, free[ops[i]["e"]]])
                    if ops[i]["e"] == e and t + ops[b]["cost"] - soon[i] > give * (soon[i] - t) + grace:
                        hold.append(soon[i])
            if hold and min(hold) > t:
                ready[b] = min(hold) + 1.0
                continue
            free[e] = t + ops[b]["cost"]
        start[b] = t
        del ready[b]
        for c in succ[b]:
            wait[c] -= 1
            if not wait[c]:
                ready[c] = max([start[a] + ops[a]["cost"] + pred[c][a] for a in pred[c]] + [release[c]])
    return start


def place(ops):
    n = len(ops)
    pred, back = links(ops, [])
    free = [dict(o, e=None, alt=None) for o in ops]
    tail = [o["lat"] for o in ops]
    best = None
    for rule in RULES:
        late = run(free, back, tail, [0.0] * n, rule)
        for _ in range(TURNS):
            start = run(ops, pred, [0.0] * n, [late[i] + ops[i]["cost"] for i in range(n)], rule, True)
            span = max(start[i] + ops[i]["cost"] + tail[i] for i in range(n))
            if best is None or span < best[0]:
                best = (span, start, [o["e"] for o in ops])
            late = run(ops, back, tail, [start[i] + ops[i]["cost"] for i in range(n)], rule)
    for o, e in zip(ops, best[2]):
        if o["alt"]:
            o.update(e=e, cost=o["alt"][e][0], fn=o["alt"][e][1])
    return best[1]


def links(ops, extra):
    pred = [{a: ops[a]["lat"] + HOP if o["dep"][a] else 1.0 for a in o["dep"]} for o in ops]
    for (a, b) in extra:
        pred[b][a] = ops[a]["lat"] + HOP
    back = [{} for _ in ops]
    for b in range(len(ops)):
        for a in pred[b]:
            back[a][b] = pred[b][a]
    return pred, back


def pack(on, cost, pred, order, release):
    start, lines = [0.0] * len(on), {e: ([], []) for e in on}
    for b in order:
        t = release[b]
        for a, d in pred[b]:
            if start[a] + cost[a] + d > t:
                t = start[a] + cost[a] + d
        if on[b] is not None:
            begin, end = lines[on[b]]
            k = top = len(end)
            while k and end[k - 1] > t:
                k -= 1
            while k < top and t + cost[b] > begin[k]:
                t = end[k] if end[k] > t else t
                k += 1
            begin.insert(k, t)
            end.insert(k, t + cost[b])
        start[b] = t
    return start


def tighten(ops, extra, start, tries):
    n = len(ops)
    tail, zero, seed = [o["lat"] for o in ops], [0.0] * n, [1]
    pred, back = [[list(x.items()) for x in side] for side in links(ops, extra)]
    either = [i for i in range(n) if ops[i]["alt"]]

    def draw():
        seed[0] = (seed[0] * 1103515245 + 12345) % 2147483648
        return seed[0] / 2147483648.0

    def settle(key, on):
        cost = [o["alt"][e][0] if o["alt"] else o["cost"] for o, e in zip(ops, on)]

        def ends(s):
            return sorted(range(n), key=lambda i: -s[i] - cost[i])

        moved = True
        while moved:
            moved = False
            for b in range(n):
                for a, _ in pred[b]:
                    if key[b] <= key[a]:
                        key[b], moved = key[a] + 0.5, True
        s = pack(on, cost, pred, sorted(range(n), key=lambda i: key[i]), zero)
        s = pack(on, cost, pred, ends(pack(on, cost, back, ends(s), tail)), zero)
        return max(a + b + c for a, b, c in zip(s, cost, tail)), s, on

    now = best = settle(list(start), [o["e"] for o in ops])
    for _ in range(tries):
        lo = draw() * now[0]
        hi = lo + 2000.0 + 8000.0 * draw()
        on = list(now[2])
        for i in either:
            if lo <= now[1][i] < hi and draw() < SWAP:
                on[i] = "v" if on[i] == "s" else "s"
        new = settle([x + SHAKE * (draw() + draw() - 1.0) if lo <= x < hi and draw() < SOME else x for x in now[1]], on)
        if new[0] <= now[0] + SLACK:
            now = new
        if new[0] < best[0]:
            best = new
    for o, e in zip(ops, best[2]):
        if o["alt"]:
            o.update(e=e, cost=o["alt"][e][0], fn=o["alt"][e][1])
    return best[1]


def banks(ops, tiles, start):
    succ = [list(x) for x in links(ops, [])[1]]
    end = [start[i] + o["cost"] + o["lat"] for i, o in enumerate(ops)]
    held, where, extra = [[] for _ in range(8)], {}, []

    def reaches(a, goal):
        seen, todo = {a}, [a]
        while todo:
            for b in succ[todo.pop()]:
                if b in goal:
                    return True
                if b not in seen:
                    seen.add(b)
                    todo.append(b)
        return False

    for name in sorted(tiles, key=lambda k: start[tiles[k][0]]):
        first = tiles[name][0]
        for b in sorted(range(8), key=lambda b: max([end[i] for i in held[b]] + [0.0])):
            if all(end[i] <= start[first] for i in held[b]) or not reaches(first, set(held[b])):
                break
        for i in held[b]:
            extra.append((i, first))
            succ[i].append(first)
        held[b], where[name] = tiles[name], "ps%d" % b
    return where, extra


def rank_program(g, core, T, topo):
    rank = T.rank_of(core)
    ranks = list(T.cores)
    spare = [c for c in topo.cores_of(ranks[0]) if c not in ranks]
    helper = {}
    for c in ranks:
        helper[c] = [h for h in spare if topo.die(h) != topo.die(c) and h not in helper.values()][0]

    def common(src, dsts):
        return [e for e in topo.engines(src, dsts[0]) if all(e in topo.engines(src, d) for d in dsts)]

    def send(src, dsts, name, starts, tag, sem):
        eng = common(src, dsts)
        per = len(eng) // len(starts)
        ids = [DstId(rid=topo.addr(c)[0], pnc=topo.addr(c)[1]) for c in dsts]
        trs = []
        for i, s0 in enumerate(starts):
            a = T[name][:, s0:s0 + V]
            trs.append(RemoteDMATransfer(dst_ids=ids, dma_engine_mask=sum(1 << e for e in eng[i * per:(i + 1) * per]),
                                         remote_sem=T.sem[sem], src=a, dsts=[a] * len(ids)))
        g.remote_dma_fused(trs, local_sem=T.sem["sn_" + tag])

    def count(src, dsts, k):
        return len(common(src, dsts)) // k * k

    def near_of(c):
        return [d for d in ranks if d != c and topo.die(d) == topo.die(c)]

    def far_of(c):
        return [d for d in ranks if topo.die(d) != topo.die(c)]

    def direct(c, tag):
        return far_of(c) + near_of(c) if tag in DIRECT else near_of(c) + [helper[c]]

    def handed(c, tag):
        return far_of(c)

    if rank is None:
        for c in ranks:
            if helper[c] == core:
                o = T.rank_of(c)
                relay = [r for r in RELAY if r[2] not in DIRECT]
                for (name, starts, tag) in relay:
                    g.wait_ge(T.sem["ar_" + tag], count(c, direct(c, tag), len(starts)))
                    send(core, handed(c, tag), name, [s0 + V * o for s0 in starts], tag, "ar_" + tag)
                for (name, starts, tag) in relay:
                    g.wait_ge(T.sem["sn_" + tag], count(core, handed(c, tag), len(starts)))
        return

    Q = {"v": g.vector, "s": g.scalar, "p": g.tensor, "g": g, "y": g.sync}
    ops, hist, tiles, where = [], {}, {}, {}

    def R(name, lo, hi, st=1):
        return (name, lo, hi, st, None)

    def W(name, lo, n):
        return R(name, lo, lo + n)

    def G(name, lo, hi, oname, olo, n):
        return (name, lo, hi, 1, W(oname, olo, n))

    def M(k, lo=0, n=128, st=1):
        return R("cm" if k in MATS else "cz", MOFF[k] + lo, MOFF[k] + lo + n, st)

    def C(i):
        return W("col", i, 1)

    def tile(n=512):
        name = "#%d" % len(tiles)
        tiles[name] = []
        return W(name, 0, n)

    def A(a):
        if not isinstance(a, tuple):
            return a
        ap = T[where.get(a[0], a[0])][:, a[1]:a[2]:a[3]] if a[3] > 1 else T[where.get(a[0], a[0])][:, a[1]:a[2]]
        return ap if a[4] is None else ap.indirect(A(a[4]))

    def size(a):
        return len(range(a[1], a[2], a[3])) if a[4] is None else 16 * size(a[4])

    def short(*xs):
        return all(a[0] in SCRATCH and SCRATCH[a[0]][2] in ("bfloat16", "float16", "uint16") for a in xs)

    def meets(a, b):
        if a[2] <= b[1] or b[2] <= a[1]:
            return False
        return a[3] != b[3] or (a[1] - b[1]) % a[3] == 0

    def add(e, outs, ins, cost, fn, lat=0.0, after=(), sem=None, behind=(), alt=None):
        me, dep = len(ops), {a: a in after for a in list(after) + list(behind)}
        ins = [a for a in ins if isinstance(a, tuple)]
        ins = ins + [a[4] for a in ins if a[4] is not None]
        for w, regs in ((False, ins), (True, outs)):
            for a in regs:
                for (b, w2, i) in hist.get(a[0], []):
                    if a[0] in tiles:
                        if w or w2 or e != ops[i]["e"]:
                            dep[i] = dep.get(i, False) or e != "p" or ops[i]["e"] != "p"
                    elif (w or w2) and meets(a, b):
                        dep[i] = True
        for w, regs in ((False, ins), (True, outs)):
            for a in regs:
                h = hist.setdefault(a[0], [])
                if w and a[3] == 1 and a[0] not in tiles:
                    h[:] = [x for x in h if not (a[1] <= x[0][1] and x[0][2] <= a[2])]
                h.append((a, w, me))
                if a[0] in tiles and me not in tiles[a[0]]:
                    tiles[a[0]].append(me)
        ops.append({"e": e, "dep": dep, "cost": cost, "lat": lat, "fn": fn, "sem": sem, "alt": alt})
        return me

    def vcost(out, a, per):
        if a[4] is not None:
            return 55.0 + (FUSED if per == 2.0 else GATHER) * CYC * size(a)
        return CALL + max(64.0, per * size(a)) * CYC

    def ts(out, a, s1, op0, s2=None, op1=None):
        more = (op0,) if op1 is None else (op0, op1)
        return add("v", [out], [a, s1, s2], vcost(out, a, 0.5 if short(out, a) else 1.0),
                   lambda: g.vector.tensor_scalar(A(out), A(a), A(s1), A(s2), *more))

    def tt(out, a, b, op):
        return add("v", [out], [a, b], vcost(out, a, 1.0 if a[0] in tiles or b[0] in tiles else 2.0),
                   lambda: g.vector.tensor_tensor(A(out), A(a), A(b), op))

    def cp(out, a):
        return add("v", [out], [a], vcost(out, a, 0.5 if short(out, a) else 1.0), lambda: g.vector.tensor_copy(A(out), A(a)))

    def ms(out, c):
        return add("v", [out], [], vcost(out, out, 0.5 if short(out) else 1.0), lambda: g.vector.memset(A(out), c))

    def scan(out, a, b, init, op0, op1):
        return add("v", [out], [a, b], vcost(out, a, 0.5), lambda: g.vector.tensor_tensor_scan(A(out), A(a), A(b), init, op0, op1))

    def act(out, a, func=ACT.Identity, bias=0.0, scale=1.0):
        return add("s", [out], [a, bias, scale], vcost(out, a, 1.0),
                   lambda: g.scalar.activation(A(out), A(a), func, bias=A(bias), scale=A(scale)))

    def lin(out, a, scale=1.0, bias=0.0, on="a", relu=False):
        how = (A(bias), 0.0, ALU.add, ALU.max) if relu else (A(scale), A(bias), ALU.mult, ALU.add)
        alt = {"v": (vcost(out, a, 0.5 if short(out, a) else 1.0), lambda: g.vector.tensor_scalar(A(out), A(a), *how)),
               "s": (vcost(out, a, 1.0),
                     lambda: g.scalar.activation(A(out), A(a), ACT.Relu if relu else ACT.Identity, bias=A(bias), scale=A(scale)))}
        e = "s" if on == "s" else "v"
        return add(e, [out], [a, scale, bias], alt[e][0], alt[e][1], alt=alt if on == "a" else None)

    def asel(out, a, pat, op, fill, base, cm=1):
        return add("g", [out], [a], 170.0 + 2 * CYC * size(a), lambda: g.affine_select(A(out), A(a), pat, op, fill, base, cm))

    def iota(out, pat, base, cm=0):
        if SCRATCH[out[0]][2] == "int32":
            return add("g", [out], [], 130.0 + 2 * CYC * size(out), lambda: g.iota(A(out), pat, base, cm))
        return add("g", [out], [], 130.0 + 2 * CYC * size(out),
                   lambda: g.iota(A(out), pat, base, cm, allow_small_or_imprecise_dtypes=True))

    def mms(out, pairs, first=True, final=True, after=()):
        def fn():
            for i, (lt, rhs) in enumerate(pairs):
                last = g.tensor.matmul(A(out), A(lt), A(rhs), first and i == 0, final and i == len(pairs) - 1)
            return last
        return add("p", [out], [x for p in pairs for x in p], sum(PEFIX + PECYC * max(64, size(r)) for (_, r) in pairs), fn, 60.0, after)

    ndm = [0]

    def dma(e, out, in_, nbytes, after=(), behind=()):
        ndm[0] += 1
        return add(e, [out] if isinstance(out, tuple) else [], [in_], 60.0 + (nbytes / 300.0 if e == "y" else 0.0),
                   lambda: Q[e].dma_start(A(out), A(in_)), LOAD, after, ("dm%d" % (ndm[0] - 1), 16), behind)

    sent, calls = {}, []

    def share(name, starts, tag):
        own = [s0 + V * rank for s0 in starts]
        src = [W(name, s0, V) for s0 in own]
        if tag == "r":
            to = [ranks[(rank + k) % N] for k in range(1, N)]
            me = add("g", [], src, 3000.0, lambda: send(core, to, name, own, tag, "ar_r%d" % rank), sem=())
            for k in range(1, N):
                o = (rank - k) % N
                add(None, [W(name, starts[0] + V * o, V)], [], 0.0, None, ARRIVE[tag][0] + k * ARRIVE[tag][1], [me],
                    ("ar_r%d" % o, count(ranks[o], [c for c in ranks if c != ranks[o]], 1)))
        else:
            to = direct(core, tag)
            me = add("g", [], src, 400.0, lambda: send(core, to, name, own, tag, "ar_" + tag), sem=(), behind=list(calls))
            got = sum(count(c, direct(c, tag), len(starts)) if core in direct(c, tag)
                      else count(helper[c], handed(c, tag), len(starts)) for c in ranks if c != core)
            add(None, [W(name, s0 + V * o, V) for s0 in starts for o in range(N) if o != rank], [], 0.0, None, ARRIVE[tag][0], [me],
                ("ar_" + tag, got))
        calls.append(me)
        sent[tag] = add(None, [], [], 0.0, None, ARRIVE["r"][0] + 2000.0, [me], ("sn_" + tag, count(core, to, len(starts))))

    def weave(o, e):
        out, src = R("bt", o, 4096, 4), W("bt", RL0 + V * o, V)
        if e == "g":
            asel(out, src, [[0, V]], ALU.is_equal, 0.0, 0, 0)
        elif e == "s":
            act(out, src)
        else:
            cp(out, src)

    def wrap16(k, src, lo, n=V):
        return [(M(k, 15 - r), R(src, lo + r, lo + n, 16)) for r in range(16)]

    def wrap4(k, src, lo=0):
        return [(M(k, 12 - 4 * kk), R(src, lo + kk, lo + 256, 4)) for kk in range(4)]

    loads = []
    for (name, lo, n, src) in (("kin", 0, 64, T.k0), ("x_0", 0, V, T.x0), ("tkt", V * rank, V, T.tk), ("wti", 0, 1, T.wt),
                               ("thi", 0, 1, T.th)):
        loads.append(dma("y", W(name, lo, n), src[:], 256 * n, behind=loads[-1:]))
    dma("s", W("bt", RL0 + V * rank, V), T.rx[:], 1 << 18, behind=[dma("s", W("kin", 64, 64), T.k1[:], 1 << 15)])
    share("bt", [RL0], "r")
    for j in range(4):
        dma("y", W("bt", NXB + 4096 * j + V * rank, V), T.nx[:, V * j:V * j + V], 1 << 18, [sent["r"]] if j >= PRE else [],
            loads[-1:])
    for k in range(N):
        weave((rank - k) % N, WEAVE[k])
    lin(W("bt", 4096, RCW - 4096), W("bt", 0, RCW - 4096))

    ROW, JC, ZC, LOW, WF, THF, FC, HIGH, IC, TMP, HC, KBC = 0, 1, 2, 3, 4, 5, 6, 7, 8, 12, 16, 20
    rows = [[-16, 8], [0, 16]]
    ms(W("zt", 0, 128), 0.0)
    ms(W("ones", 0, 512), 1.0)
    ms(W("x_0", V, 16), 0.0)
    ms(W("q_0", V, 16), 0.0 if FORM[0] == "p" else 2.0)
    iota(W("pi", 0, 1), [[0, 1]], 0, 1)
    asel(M("I"), W("zt", 0, 128), [[-1, 128]], ALU.not_equal, 1.0, 0)
    asel(W("t8", 0, 128), W("ones", 0, 128), rows, ALU.is_ge, 0.0, 0)
    asel(M("BLK"), W("t8", 0, 128), [[16, 8], [0, 16]], ALU.is_ge, 0.0, 15, -1)
    for k in list(DIAG)[1:]:
        lin(M(k), M("I"), DIAG[k])
    for s in (1, 2, 3):
        lin(W("x_%d" % s, 0, 16), W("zt", 0, 16), 0.0, 128.0)
        lin(W("q_%d" % s, 0, 16), W("zt", 0, 16), 0.0, 128.0 if FORM[s] == "p" else 130.0)
    lin(W("bt", ZR0, 16), W("zt", 0, 16))
    for (k, n) in (("Z", 144), ("ZK0", 432), ("PK1", 432)):
        lin(M(k, 0, n), W("ones", 0, n), 0.0)

    def move(k, col, row, val, src="I"):
        lin(M(k, col, 113, 16), M(src, row, 113, 16), val)

    move("Z", 15, 0, 1.0, "BLK")
    lin(M("ZN", 0, 144), M("Z", 0, 144), -FAR)
    lin(M("BB"), M("BLK"), 3 * BIG)
    asel(W("t8", 0, 128), M("BLK"), [[-1, 128]], ALU.is_gt, 0.0, 0)
    lin(W("zt", 128, 128), W("t8", 0, 128), -1.0)
    asel(M("UN"), W("zt", 128, 128), [[-1, 128]], ALU.not_equal, -BIG, 0)
    asel(M("RF"), W("zt", 0, 128), rows, ALU.not_equal, 1.0, -10)
    asel(M("B12"), M("BLK"), [[0, 8], [1, 16]], ALU.is_ge, 0.0, -12, 0)
    asel(W("zt", 256, 128), M("BLK"), [[0, 8], [-1, 16]], ALU.is_ge, 0.0, 11, 0)
    for b in range(2):
        asel(M("LO%d" % b), W("zt", 256, 128), [[0, 64], [1, 2]], ALU.is_equal, 0.0, -b, 0)
    for b in range(2):
        move("ZK%d" % b, 15, b, 1.0)
    for j in range(4):
        for b in range(2):
            move("PK%d" % b, 12 + j, 2 * j + 2 + b, 1.0)
        move("PFI", 12 + j, 12 + j, 1.0)
        move("PG", 12 + j, 12 + j, -4096.0 * (j + 1))
    asel(W("keep", 0, 256), W("ones", 0, 256), [[0, 4], [1, 64]], ALU.is_gt, 0.0, 0, 0)
    iota(W("il", 0, 64), [[-1, 64]], 64)
    iota(W("oc", 0, 16), [[1024, 4], [0, 4]], 0)
    scan(W("k4", 0, 256), W("ones", 0, 256), W("ones", 0, 256), -1.0, ALU.mult, ALU.add)
    ts(W("pi", 1, 1), W("pi", 0, 1), 15, ALU.bitwise_and)
    ts(W("pi", 2, 1), W("pi", 1, 1), 1, ALU.logical_shift_right)
    ts(W("pi", 3, 1), W("pi", 0, 1), 3, ALU.bitwise_and)
    cp(C(ROW), W("pi", 1, 1))
    ts(C(LOW), C(ROW), 12.0, ALU.is_lt)
    ts(C(HIGH), C(ROW), 12.0, ALU.is_ge)
    lin(C(ZC), C(HIGH), -1.0)
    ts(C(TMP), W("pi", 2, 1), C(LOW), ALU.mult)
    ts(C(TMP + 1), C(ROW), -11.0, ALU.add, 0.0, ALU.max)
    tt(C(JC), C(TMP), C(TMP + 1), ALU.add)
    ts(C(FC), W("pi", 3, 1), 4096.0, ALU.mult, NXB - ZR0 + 2048.0, ALU.add)
    for ic in range(4):
        lin(C(IC + ic), C(ROW), 1.0, 16.0 * ic + 0.5)
    lin(C(TMP + 3), C(LOW), 4.0)
    for o in range(4):
        lin(C(KBC + 4 + o), C(HIGH), 1024.0 * o - 2048.0)
        ts(W("kb", 768 + 64 * o, 64), W("k4", 64 * o, 64), C(TMP + 3), ALU.mult, C(KBC + 4 + o), ALU.add)
    for t in range(3):
        lin(C(KBC + t), C(LOW), V * (t + 1) + 15.0 - CEN)
        ts(W("kb", 256 * t, 256), W("kb", 768, 256), C(KBC + t), ALU.add)
    lin(C(TMP + 2), C(ROW), 1.0, 1024.0)
    ts(W("pay", 128, 64), W("k4", 0, 64), 16.0, ALU.mult, C(TMP + 2), ALU.add)
    lin(W("wk", 0, 64), W("pay", 128, 64), 1.0, XN0 - RL0 - 3072.0)
    for b in range(2) if any(EARLY) else ():
        ts(W("vl", 64 * b, 64), W("pay", 128, 64), -1020.0, ALU.add)
    for r in RELAY:
        share(*r)
    cp(C(WF), W("wti", 0, 1))
    cp(C(THF), W("thi", 0, 1))
    lin(M("ZW", 0, 144), M("Z", 0, 144), C(WF))
    cp(W("got", 0, 1), W("wti", 0, 1))
    p = tile(1)
    mms(p, [(M("BLK"), W("got", 0, 1))])
    lin(C(HC), p, -128.0)
    lin(W("thl", 0, 64), W("ones", 0, 64), C(THF))
    ts(W("kz", 0, 128), W("kin", 0, 128), float(V), ALU.min)
    ts(W("wk", 64, 128), W("kin", 0, 128), -8.0, ALU.mult, 32768.0 - CEN, ALU.add)
    ts(W("wk", 192, 128), W("kin", 0, 128), 16.0 - CEN, ALU.add)
    tt(W("pay", 0, 128), W("wk", 64, 128), W("wk", 192, 128), ALU.min)
    lin(W("d32", 256, 16), W("zt", 0, 16))

    def own(buf, s, lo, n):
        return W("%s_%d" % (buf, s), lo + (16 if s else 0), n)

    def kid(buf, s, b, lo, n):
        end = 16 + V * min(lo // V + 2, s + 1)
        return G("%s_%d" % (buf, s), 0, end, "kl" if s else "kz", 128 * (lo // V) + 64 * b + lo % V // 16, n // 16)

    def pass1(s, lo, n, on="s"):
        first = (cp if on == "v" else act)(W("ta", lo, n), kid("x", s, 0, lo, n))
        if FORM[s] == "p":
            tt(own("q", s, lo, n), kid("x", s, 1, lo, n), W("ta", lo, n), ALU.max)
            return
        tt(W("tb", lo, n), kid("x", s, 1, lo, n), W("ta", lo, n), ALU.max)
        x, p = own("x", s, lo, n), tile(n)
        if lo // 256 in RELU[s]:
            mms(p, [(M("NI"), x), (M("I"), W("tb", lo, n))])
            act(W("ta", lo, n), p, ACT.Relu, bias=-2.0)
            p = tile(n)
            mms(p, [(M("I"), x), (M("I"), W("ta", lo, n))])
            act(own("q", s, lo, n), p, bias=2.0)
        else:
            mms(p, [(M("I2"), x)] if s else [(M("I"), x), (M("C2"), W("ones", 0, n))], after=[first])
            tt(own("q", s, lo, n), W("tb", lo, n), p, ALU.max)

    def pass2(s, lo, n, out, how, behind=()):
        x, q, a, b = own("x", s, lo, n), own("q", s, lo, n), W("tc", lo, n), W("td", lo, n)
        if how[0] == "w":
            ts(W("tb", lo, n), q, 2.0, ALU.add)
            first = tt(a, kid("q", s, 0, lo, n), W("tb", lo, n), ALU.max)
        else:
            first = act(a, kid("q", s, 0, lo, n))
        if how[0] == "m":
            p = tile(n)
            mms(p, [(M("I2"), q)] if s else [(M("I"), q), (M("C2"), W("ones", 0, n))], after=[first] if n > 256 else [])
            tt(W("tb", lo, n), a, p, ALU.max)
            a = W("tb", lo, n)
        second = tt(b, kid("q", s, 1, lo, n), a, ALU.max)
        for i in behind:
            for u in (first, second):
                if ops[i]["e"] == ops[u]["e"] and not ops[i]["alt"]:
                    ops[u]["dep"].setdefault(i, False)
        k = "I63" if how[1] == "v" and s == 3 else "I"
        if FORM[s] == "q" or how[0] in "mw":
            parts, off = [x, b], 1.0
        else:
            p = tile(n)
            mms(p, [(M("NI"), q), (M("I"), b)])
            lin(a, p, 1.0, -2.0, how[0], True)
            parts, off = [x, q, a], 0.0
        p = tile(n)
        mms(p, [(M(k), u) for u in parts])
        if s < 3:
            lin(out, p, 0.5, (-0.25 if s else 127.75) - off, how[1])
        elif how[1] == "v":
            ts(out, p, MAGIC - off - 126.0, ALU.add, -MAGIC, ALU.add)
        else:
            u = a if FORM[s] == "q" or how[0] in "mw" else b
            act(u, p, bias=(-0.25 if s else 127.75) - off, scale=0.5)
            ts(out, u, -128.0, ALU.add)
        return range(second + 1, len(ops))

    for i, (lo, n) in enumerate(FIRST):
        pass1(0, lo, n, "v" if i < ALONE else "s")

    for t in range(3):
        S = V * (t + 1)
        B0 = S - V
        nxt = "x_%d" % (t + 1)
        for i, (lo, n) in enumerate(PIECES):
            pass2(t, B0 + lo, n, W("xb", lo, n), NEW[i])
        for lo in (0, 512):
            lin(W("bt", XN0 + lo, 512), W("xb", lo, 512), 1.0, -128.0, RAW[t])
        for lo in range(0, B0, OLD):
            pass2(t, lo, OLD, own("x", t + 1, lo, OLD), OLDS[t][lo // OLD])
        for (lo, n) in HASH[t]:
            p = tile(n)
            mms(p, wrap16("ZW", "xb", 16 * lo, 16 * n))
            ts(W("c1", lo, n), p, C(HC), ALU.add, 31.0 * t, ALU.add)
            ts(W("c1", 64 + lo, n), W("c1", lo, n), 4095, ALU.bitwise_and)
            for m in range(4):
                ts(W("offl", 64 * m + lo, n), W("c1", 64 + lo, n), 97.0 * m, ALU.add)
        if VALS == "s":
            cp(W("c0", 0, 64), W("c1", 64, 64))
        for m in range(4):
            lin(W("val", 64 * m, 64), W("c0", 0, 64) if VALS == "s" else W("c1", 64, 64), 2.0, 2.0 * (8192 * (4 - m) + 97 * m) + 1, VALS)
        near = tile(192)
        for m in range(4):
            how = DIST[t][m]
            for (lo, n) in (GAPS if m == 3 else ((0, 512), (512, 512))):
                root, x = G("bt", 0, RCW, "offl", 64 * m + lo // 16, n // 16), W("xb", lo, n)
                d, a = W("dd", V * m + lo, n), W("da", V * m + lo, n)
                if how == "s":
                    act(d, root)
                    p = tile(n)
                    mms(p, [(M("NI"), x), (M("I"), d)])
                    act(a, p, ACT.Abs, bias=128.0)
                else:
                    tt(d, root, x, ALU.subtract)
                    act(a, d, ACT.Abs, bias=128.0)
            p = W(near[0], 64 * m, 64) if m < 3 else tile(64)
            mms(p, [(M("IB"), W("thl", 0, 64))] + wrap16("ZN", "da", V * m), True, m < 3 or not FOLD)
            if m < 3 and SCORE == 4:
                near = tile(64) if m < 2 else near
                tt(W(p[0], 192, 64) if m else W("sc", 0, 64), W("val", 64 * m, 64), p, ALU.min)
                if m:
                    tt(W("sc", 64 * m + 64, 64), W("sc", 128 * m - 128, 64), W(p[0], 192, 64), ALU.max)
        if SCORE == 3:
            tt(W("sc", 0, 192), W("val", 0, 192), near, ALU.min)
            tt(W(near[0], 192, 64), W("sc", 0, 64), W("sc", 64, 64), ALU.max)
            tt(W("sc", 192, 64), W("sc", 128, 64), W(near[0], 192, 64), ALU.max)
        if FOLD:
            ts(W("got", 0, 64), W("sc", 192, 64), 0.0, ALU.is_gt)
            tt(W("sc", 64, 64), W("sc", 192, 64), W("val", 192, 64), ALU.max)
            mms(p, [(M("IF"), W("got", 0, 64))], False, True)
            tt(W("bi", 0, 64), W("sc", 64, 64), p, ALU.min)
        else:
            tt(W(p[0], 64, 64), W("val", 192, 64), p, ALU.min)
            tt(W("bi", 0, 64), W("sc", 192, 64), W(p[0], 64, 64), ALU.max)
        ts(W("bi", 64, 64), W("bi", 0, 64), 7, ALU.bitwise_and)
        for o in range(4):
            ts(W("ask", 64 * o, 64), W("bi", 64, 64), float(2 * o + 1), ALU.is_equal)
        scan(W("cs", 0, 256), W("keep", 0, 256), W("ask", 0, 256), 0.0, ALU.mult, ALU.add)
        ts(W("bi", 128, 64), W("bi", 0, 64), 3, ALU.logical_shift_right, 1023, ALU.bitwise_and)
        ts(W("ob", 0, 64), W("bi", 64, 64), 512.0, ALU.mult, -2560.0, ALU.add)
        tt(W("tcc", 0, 64), W("bi", 128, 64), W("ob", 0, 64), ALU.add)
        p = tile(256)
        count0 = mms(p, [(M("BLK"), W("cs", 0, 256))])
        if SIGNS == "s":
            for ic in range(4):
                act(W("sg", 256 * ic, 256), p, ACT.Sign, bias=C(IC + ic), scale=-1.0)
                scan(W("sn", 256 * ic, 256), W("keep", 0, 256), W("sg", 256 * ic, 256), 0.0, ALU.mult, ALU.add)
        else:
            p2 = tile(128)
            mms(p2, [(M("BLK"), W("cs", 128, 128))])
            for ic in range(4):
                act(W("sg", 128 * ic, 128), W(p[0], 0, 128), ACT.Sign, bias=C(IC + ic), scale=-1.0)
                ts(W("sg", 512 + 128 * ic, 128), p2, C(IC + ic), ALU.is_lt)
            for lo in (512, 768, 0, 256):
                scan(W("sn", lo, 256), W("keep", 0, 256), W("sg", lo, 256), 0.0, ALU.mult, ALU.add)
        p = tile(256)
        mms(p, [(M("UN"), W("ask", 0, 256)), (M("BLK"), W("cs", 0, 256))])
        act(W("ra", 0, 256), p, ACT.Relu, bias=65.0 - BIG, scale=-1.0)
        for o in range(4):
            if SIGNS == "s":
                ts(W("ls", 4 * o, 4), R("sn", 64 * o + 62, V, 256), 0.5, ALU.mult, 31.5, ALU.add)
            elif o < 2:
                ts(W("ls", 4 * o, 4), R("sn", 64 * o + 62, 512, 128), 0.5, ALU.mult, 31.5, ALU.add)
            else:
                cp(W("ls", 4 * o, 4), R("sn", 384 + 64 * o + 62, V, 128))
        for o in range(4):
            tt(W("mask", 64 * o, 64), G("ra", 64 * o, 64 * o + 64, "ls", 4 * o, 4), W("il", 0, 64), ALU.is_equal)
        mask = W("mask", 0, 256)
        tree, vv, old0, old1 = [W("pr", 256 * i, 256) for i in range(4)]
        tt(tree, G("bi", 128, 192, "ls", 0, 16), mask, ALU.mult)
        tt(vv, G("pay", 128, 192, "ls", 0, 16), mask, ALU.mult)
        tt(old0, G("pay", 0, 64, "ls", 0, 16), mask, ALU.mult)
        tt(old1, G("pay", 64, 128, "ls", 0, 16), mask, ALU.mult)
        p = tile(16)
        mms(p, [(M("I"), W("oc", 0, 16))], True, False, [count0])
        mms(p, wrap16("Z", "pr", 0, 256), False, True)
        cp(W("ls", 16, 16), p)
        q = W("r16", 0, 256)
        cp(q, G("tkt", 0, 4096, "ls", 16, 16))
        inv = W("inv", 0, 64)
        p = tile(64)
        mms(p, [(M("I"), W("ra", 64 * o, 64)) for o in range(4)])
        act(inv, p, ACT.Relu, bias=1.0, scale=-1.0)
        p = tile(128)
        mms(W(p[0], 0, 64), [(M("I"), W("tcc", 0, 64)), (M("BI"), inv)])
        mms(W(p[0], 64, 64), [(M("NI"), W("ra", 64 * o, 64)) for o in range(4)] + [(M("I16"), W("ob", 0, 64))]
            + ([] if EARLY[t] else [(M("BI"), inv)]))
        tt(W("wk", 448, 64), W("wk", 0, 64), W(p[0], 0, 64), ALU.min)
        ts(W("ls", 96, 64), W("wk", 448, 64), 2048.0, ALU.add)
        if EARLY[t]:
            ts(W("rb", 0, 64), W(p[0], 64, 64), 4.0, ALU.mult, 768.0 + S + 15.0 - CEN, ALU.add)
            ts(W("ls", 32, 64), W("tcc", 0, 64), 2048.0, ALU.add)
            cp(W("k16", 0, 128), W("pay", 0, 128))
            for (lo, n) in ROOT:
                cp(W("dv", lo, n), G("tkt", 0, 4096, "ls", 32 + lo // 16, n // 16))
            p = tile(128)
            for b in range(2):
                for i in range(0, 16, 8):
                    mms(W(p[0], 64 * b, 64), wrap16("ZK%d" % b, "dv", 0)[i:i + 8], i == 0, i == 8)
            rq = W("rq", 0, 128)
            inner, none, wrap = [W("rm", 128 * i, 128) for i in range(3)]
            cp(rq, p)
            ts(inner, rq, 4.5, ALU.is_lt)
            ts(none, rq, 0.0, ALU.is_equal)
            back = [(M("I"), W("vl", 0, 128)), (M("NI"), rq), (M("BI"), inner)]
            if t == 0:
                tt(wrap, rq, W("vl", 0, 128), ALU.is_gt)
                back = back + [(M("IK"), wrap)]
            p = tile(128)
            mms(p, back)
            act(W("de", 512, 128), p, bias=B0 + 16.0 - CEN)
            p = tile(128)
            mms(p, [(M("I"), rq), (M("NBI"), none)], True, False)
            for b in range(2):
                mms(W(p[0], 64 * b, 64), [(M("I"), W("rb", 0, 64)), (M("NBI"), inv)], False, b == 1)
            tt(W("de", 640, 128), W("de", 512, 128), p, ALU.min)
            p = tile(128)
            mms(p, [(M("NBI"), W("ones", 0, 128)), (M("I"), W("k16", 0, 128))], True, False, [count0])
            for b in range(2):
                mms(W(p[0], 64 * b, 64), [(M("BI"), inv)], False, b == 1)
            tt(W("de", 512, 128), W("de", 640, 128), p, ALU.max)
            ts(W("kl", 128 * t, 128), W("de", 512, 128), CEN, ALU.add)
        else:
            ts(W("ls", 32, 64), W(p[0], 64, 64), 192.0, ALU.add, 256.0, ALU.min)
            for b in range(2):
                tt(W("k16", 64 * b, 64), W("pay", 64 * b, 64), inv, ALU.mult)
        for lo in (0, 512):
            root, x, out = G("bt", RL0, NXB, "ls", 96 + lo // 16, 32), W("xb", lo, 512), W(nxt, 16 + B0 + lo, 512)
            if HALVE[t] == "s":
                act(W("sel", lo, 512), root)
                p = tile()
                mms(p, [(M("I"), x), (M("I"), W("sel", lo, 512))])
                lin(out, p, 0.5, 63.75, HALF[t])
            else:
                tt(W("sel", lo, 512), root, x, ALU.add)
                ts(out, W("sel", lo, 512), 0.5, ALU.mult, 63.75, ALU.add)
        inner, none, foot, wrap = [W("mk", 256 * i, 256) for i in range(4)]
        ts(inner, q, 4.5, ALU.is_lt)
        ts(none, q, C(ZC), ALU.is_equal)
        p = tile(256)
        mms(p, [(M("RF"), q)])
        ts(foot, p, C(JC), ALU.is_equal)
        back = [(M("NI"), q), (M("BI"), inner)]
        if t == 0:
            p = tile(256)
            mms(p, [(M("NW"), W("ones", 0, 256)), (M("BLK"), vv)])
            tt(wrap, q, p, ALU.is_gt)
            back = back + [(M("IK"), wrap)]
        p = tile(256)
        mms(p, [(M("BB"), mask)], True, False)
        mms(p, [(M("BLK"), vv)], False, False)
        mms(p, back, False, True)
        act(W("de", 0, 256), p, bias=B0 + 20.0 - 1024.0 - CEN - 3 * BIG)
        p = tile(256)
        mms(p, [(M("I"), W("kb", 256 * t, 256))], True, False, [count0])
        mms(p, [(M("B12"), tree)], False, False)
        mms(p, [(M("I"), q), (M("NBI"), none)], False, False)
        mms(p, [(M("NBI"), foot)], False, True)
        tt(W("de", 256, 256), W("de", 0, 256), p, ALU.min)
        p = tile(256)
        mms(p, [(M("N4B"), W("ones", 0, 256))], True, False, [count0])
        for pair in ((M("BB"), mask), (M("B12"), vv), (M("LO0"), old0), (M("LO1"), old1)):
            mms(p, [pair], False, False)
        mms(p, [(M("BI"), foot)], False, True)
        first = tt(W("d16", 0, 256), W("de", 256, 256), p, ALU.max)
        if not EARLY[t]:
            ops[tt(W("d32", 0, 256), W("de", 256, 256), p, ALU.max)]["dep"][first] = False
        p = tile(64)
        mms(p, wrap4("PG", "mk", 512), True, False)
        mms(p, wrap4("PFI", "d16"), False, True)
        ts(W("ls", 160, 64), p, C(FC), ALU.add)
        if t < 2:
            ts(W("thl", 0, 64), p, -20000.0, ALU.is_gt, C(THF), ALU.mult)
        for (lo, n, e) in FILL[t]:
            out, src = W(nxt, 16 + S + lo, n), G("bt", ZR0, NXB + 16384, "ls", 160 + lo // 16, n // 16)
            if e == "s":
                act(out, src, bias=128.0)
            else:
                ts(out, src, 128.0, ALU.add)
        p = tile(128)
        for b in range(2):
            mms(W(p[0], 64 * b, 64), wrap4("PK%d" % b, "d16"))
        ts(W("kl", 128 * t + 128, 128), p, CEN, ALU.add)
        if t < 2:
            ts(W("pay", 0, 128), p, -CEN, ALU.max)
        for (lo, n) in () if EARLY[t] else DV:
            ts(W("dv", lo, n), G("d32", 0, 272, "ls", 32 + lo // 16, n // 16), -CEN, ALU.max)
        for b in () if EARLY[t] else range(2):
            p = tile(64)
            mms(p, [(M("I"), W("k16", 64 * b, 64))] + wrap16("ZK%d" % b, "dv", 0))
            ts(W("kl", 128 * t + 64 * b, 64), p, CEN, ALU.add)
        for lo in range(0, B0, OLD):
            pass1(t + 1, lo, OLD)
        for i, (lo, n) in enumerate(TAIL):
            pass1(t + 1, B0 + lo, n, "v" if i < ALONE else "s")

    done = []
    for c in range(8):
        for (lo, n) in (((512 * c, 512),) if c < 7 else ((3584, 384), (3968, 128))):
            done.append(pass2(3, lo, n, W("yo", lo, n), LAST[c], done[-DEPTH] if len(done) >= DEPTH else ()))
            if c >= 6:
                dma("y", T.y[:, lo:lo + n], W("yo", lo, n), 256 * n)
            elif c % 2:
                dma("y", T.y[:, lo - 512:lo + 512], W("yo", lo - 512, V), 1 << 18)

    shape = tuple((o["e"], o["cost"], tuple(o["dep"].items())) for o in ops)
    if shape not in PLANS:
        start = tighten(ops, [], place(ops), TRIES)
        got, extra = banks(ops, tiles, start)
        PLANS[shape] = (tighten(ops, extra, start, TRIES // 4), got, extra, [o["e"] for o in ops])
    start, got, extra, on = PLANS[shape]
    for o, e in zip(ops, on):
        if o["alt"]:
            o.update(e=e, cost=o["alt"][e][0], fn=o["alt"][e][1])
    where.update(got)
    for (a, b) in extra:
        ops[b]["dep"][a] = True
    cnt = {e: 0 for e in Q}
    seen = {e: {} for e in Q}
    mark, final = {}, {}

    def wait(e, sem, val):
        if seen[e].get(sem, 0) < val:
            Q[e].wait_ge(T.sem[sem], val)
            seen[e][sem] = val

    for i in sorted(range(len(ops)), key=lambda i: (start[i], i)):
        o = ops[i]
        if o["e"] is not None:
            need = {}
            for a in o["dep"]:
                if o["dep"][a] and mark[a]:
                    need[mark[a][0]] = max(need.get(mark[a][0], 0), mark[a][1])
            for sem in need:
                wait(o["e"], sem, need[sem])
            call = o["fn"]()
            if o["sem"] is None:
                cnt[o["e"]] += 1
                o["sem"] = ("c" + o["e"], cnt[o["e"]])
                call.then_inc(T.sem[o["sem"][0]], 1)
            elif o["sem"]:
                call.then_inc(T.sem[o["sem"][0]], 16)
        mark[i] = o["sem"]
        if o["sem"]:
            final[o["sem"][0]] = o["sem"][1]
    for sem in final:
        wait("g" if sem == "cg" else "y", sem, final[sem])
